import numpy as np, ml_dtypes
CORES = [6,15,38,47]
N = 4
BF = ml_dtypes.bfloat16
def gentries(a):
    return np.ascontiguousarray(a.reshape(8, 16, -1).transpose(0, 2, 1)).reshape(8, -1)
def gtable(e):
    e = np.asarray(e); return np.ascontiguousarray(e.reshape(8, -1, 16).transpose(0, 2, 1)).reshape(128, -1).astype(np.int32)
def f(rng, *shape):
    return (rng.standard_normal(shape, dtype=np.float32) * np.exp2(rng.integers(-2, 3, shape[:-1] + (1,)))).astype(BF)
def wide(rng, *shape):
    v = f(rng, *shape).astype(np.float32); k = shape[:-2] + (1, shape[-1])
    return (v * np.exp2(rng.integers(-6, 7, k)) * (rng.random(k) > 0.0625)).astype(BF)
V, W, G, P, Q, RO = 2560, 4096, 256, 256, 64, 4
M = V + (N - 1) * G + 1
def nodes(an, of):
    A = np.full((N, 8, M), M - 1, np.int64); A[..., :V] = an
    O = np.zeros((N, 8, M), np.int64); O[..., :M - 1] = of
    return A, O
def dates(A, O):
    s, p = O, A
    for i in range(3):
        s = s + np.take_along_axis(s, p, 2); p = np.take_along_axis(p, p, 2)
    return s & (W - 1)
def parts(rng):
    u = rng.random((N, 8, V))
    an = np.where(u < 0.25, M - 1, np.where(u < 0.4, rng.integers(V, M - 1, (N, 8, V)), rng.integers(0, V, (N, 8, V))))
    return an, rng.integers(0, W, (N, 8, M - 1)), rng.integers(0, 256, (N, 8, 16, W)), rng.integers(0, V, (N, 8, (N - 1) * G))
def statures(rng):
    sc = np.exp2(rng.integers(-2, 3, (1, 8, 16, 1)).astype(np.float64)); sh = rng.choice(np.array([-0.8, -0.5, -0.2, 0.1]), (N, 8, 1, 1))
    x = rng.standard_normal((N, 8, 16, V)) + 0.7 * rng.standard_normal((N, 8, 1, V)) + sh
    s = rng.standard_normal((N, 8, 16, W)) + 0.7 * rng.standard_normal((N, 8, 1, W))
    return np.floor(8 * x) * 0.125 * sc, np.floor(8 * s) * 0.125 * sc
def pack(x, an, of, s, wk, snd):
    b = lambda v: np.ascontiguousarray(v).reshape(N, 128, -1).astype(np.float32).astype(BF)
    return {"x": b(x), "an0": np.stack([gtable(e) for e in an]), "of0": np.stack([gtable(e) for e in of]), "s0": b(s), "wk": b(wk), "snd": np.stack([gtable(e) for e in snd])}
def setup_inputs(rng):
    an, of, wk, snd = parts(rng); x, s = statures(rng)
    return pack(x, an, of, s, wk, snd)
def setup_inputs_room(rng):
    an, of, wk, snd = parts(rng); day = np.arange(W)
    an[..., 0] = M - 1; an[..., V - 1] = M - 1; of[..., 0] = 0; of[..., V - 1] = W - 2
    D = dates(*nodes(an, of))[..., :V]
    s = rng.integers(36, 61, (N, 8, 16, W)) * 0.25
    s[..., day % 4 == 3] = rng.integers(4, 29, (N, 8, 16, W // 4)) * 0.25
    o = s[1::2]; o[..., day % 4 == 1] = rng.integers(-32, -3, (o.shape[0], 8, 16, W // 4)) * 0.25
    k = rng.permutation(16)
    wk[:, :, k[0]] = 4 * rng.integers(0, 64, (N, 8, W)) + (day + 1) % 4
    wk[1::2, :, k[1]] = 4 * rng.integers(0, 64, (o.shape[0], 8, W)) + (day + 3) % 4
    x = 16 + rng.integers(0, 33, (N, 8, 16, V)) * 0.25
    for q in range(N):
        for g in range(8):
            n = int(rng.choice(np.array([0, 1, 2, P - 1, P, P + 1, P + Q]))); nf = int(rng.choice(np.array([0, 1, Q - 1, Q, Q + 1, P])))
            if q == 0: n = (P, P + 1, P - 1, 1, 0, P, P, P)[g]; nf = (Q, Q + 1, Q - 1, 1, 0, 0, P, Q + 1)[g]
            e = np.flatnonzero(D[q, g] % 2 == 0); e = e[(e > 0) & (e < V - 1)]
            w = np.concatenate([np.array([0, V - 1]), rng.permutation(e)])[:n]
            x[q, g][:, w] = rng.integers(29, 36, (16, len(w))) * 0.25
            i = w[len(w) - min(nf, len(w)):]
            x[q, g][:, i] = rng.integers(0, 4, (16, len(i))) * 0.25
    return pack(x, an, of, s, wk, snd)
def setup_inputs_ties(rng):
    an, of, wk, snd = parts(rng)
    of = rng.choice(np.array([0, 1, W - 1, W // 2, 14]), (N, 8, M - 1)); wk[:, ::2] = rng.choice(np.array([0, 1, 2, 255]), (N, 4, 16, W))
    x = np.floor(4 * rng.random((N, 8, 16, V)) * (0.3 + 0.7 * rng.random((N, 8, 1, V))))
    s = np.floor(4 * rng.random((N, 8, 16, W)) * (0.3 + 0.7 * rng.random((N, 8, 1, W)))) + 2 * (rng.random((N, 8, 1, W)) < 0.4)
    x[..., 0] = -1; x[..., V - 1] = -1
    x = np.where((x == 0) & (rng.random(x.shape) < 0.5), -0.0, x); s = np.where((s == 0) & (rng.random(s.shape) < 0.5), -0.0, s)
    return pack(x, an, of, s, wk, snd)
def setup_inputs_chains(rng):
    an, of, wk, snd = parts(rng); x, s = statures(rng); v = np.arange(V); d = int(rng.integers(0, W))
    for q in range(N):
        for g in range(8):
            k = (g + q) % 8
            if k == 0: an[q, g] = (v + 1) % V
            if k == 1: an[q, g] = v
            if k == 2: an[q, g] = rng.integers(V, M - 1, V)
            if k == 3: an[q, g] = M - 1
            if k == 4: an[q, g] = rng.choice(np.array([0, 5, V - 1]), V)
            if k == 5: an[q, g] = np.where(v == 0, M - 1, v - 1)
            if k > 5:
                an[q, g] = M - 1; of[q, g, :V] = d
                w = 1 + rng.permutation(255)[:16]; wk[q, g, :, d] = w; c = (d + 7 * w) & (W - 1)
                i = np.sort(rng.permutation(16)[:2])
                s[q, g] = 16 + 0.25 * rng.integers(0, 32, (16, W))
                s[q, g][:, c[i[0]]] = 0.25 * rng.integers(0, 16, 16)
                m = np.arange(P) if k == 6 else np.arange(int(rng.integers(0, 16)), V, 16)
                y = 28 + 0.25 * rng.integers(0, 16, (16, V))
                y[:, m] = 8 + 0.25 * rng.integers(0, 16, (16, len(m)))
                if k == 6: y[:, rng.permutation(P)[:56]] = -8 + 0.25 * rng.integers(0, 16, (16, 56))
                if k == 7: s[q, g][:, c[i[1]]] = -16 + 0.25 * rng.integers(0, 16, 16)
                x[q, g] = y
    snd[:, ::2] = rng.choice(np.array([0, 3, V // 2, V - 1]), (N, 4, (N - 1) * G))
    return pack(x, an, of, s, wk, snd)
def setup_inputs_calm(rng):
    an, of, wk, snd = parts(rng); x, s = statures(rng); q = int(rng.integers(0, N)); g = int(rng.integers(0, 8))
    x[:, g] += 64
    x[(q + 2) % N] += 64; x[q] = np.minimum(x[q], 20) - 64
    o = s[(q + 1) % N]; o[..., 1::2] -= 128
    w = rng.permutation(256)[:16]; wk[:, g, :, 0] = w; day = (7 * w) & (W - 1)
    for r in range(N):
        if r != q: s[r, g][:, day] = -2.0 ** 20
    x[q, :, :, 0] = -2.0 ** 20
    return pack(x, an, of, s, wk, snd)
def setup_inputs_spread(rng):
    an, of, wk, snd = parts(rng)
    of = np.minimum(np.exp2(13 * rng.random((N, 8, M - 1))).astype(np.int64) - 1, W - 1)
    x = np.abs(wide(rng, N, 8, 16, V).astype(np.float32)); s = np.abs(wide(rng, N, 8, 16, W).astype(np.float32))
    k = rng.permutation(8); sc = np.ones((1, 8, 1, 1), np.float32); sc[:, k[0]] = 2.0 ** -40; sc[:, k[1]] = 512
    x = np.minimum(x * sc, np.float32(2.0 ** 20)); s = np.minimum(s * sc, np.float32(2.0 ** 20))
    x[:, k[1], :, V - 1] = 2.0 ** 20; s[:, k[1], :, W - 1] = 2.0 ** 20
    return pack(x, an, of, s, wk, snd)
def check_inputs(d):
    bad = []
    for k, lo, hi in (("x", -2 ** 20, 2 ** 20), ("s0", -2 ** 20, 2 ** 20), ("wk", 0, 255), ("an0", 0, M - 1), ("of0", 0, W - 1), ("snd", 0, V - 1)):
        v = np.asarray(d[k]).astype(np.float64)
        if not (np.min(v) >= lo and np.max(v) <= hi): bad.append("range of " + k)
        elif k == "wk" and np.any(v != np.floor(v)): bad.append("whole numbers of wk")
        elif k in ("x", "s0") and np.any((v != 0) & (np.abs(v) < 2.0 ** -100)): bad.append("tiny numbers of " + k)
    return bad
def best(S, K, x, D):
    c = (D + 7 * K[:, D]) & (W - 1)
    e = np.sum((x[:, None, :] > S[:, c]).astype(np.int64), axis=0)
    k = np.argmax(e, axis=0); i = np.arange(len(D))
    return c[k, i], e[k, i]
def put(S, c, x):
    u, i = np.unique(c, return_index=True)
    S[:, u] = x[:, i]
def reference(x, an0, of0, s0, wk, snd):
    X = x.astype(np.float32).reshape(N, 8, 16, V); S = s0.astype(np.float32).reshape(N, 8, 16, W).copy(); K = wk.astype(np.float32).astype(np.int64).reshape(N, 8, 16, W)
    A, O = nodes(np.stack([gentries(e) for e in an0]).astype(np.int64), np.stack([gentries(e) for e in of0]).astype(np.int64))
    sl = np.stack([gentries(e) for e in snd]).astype(np.int64).reshape(N, 8, N - 1, G)
    odd = np.zeros(N, np.int64)
    for t in range(RO):
        D = dates(A, O)[..., :V]
        a = np.sum((X >= np.take_along_axis(S, D[:, :, None, :], 3)).astype(np.int64), axis=2)
        moves = np.zeros(N, np.int64); go = {}
        for q in range(N):
            for g in range(8):
                v = np.flatnonzero(a[q, g] < 5)[:P]
                c, e = best(S[q, g], K[q, g], X[q, g][:, v], D[q, g, v])
                ok = e >= 9 + odd[q]; w = v[ok]
                A[q, g, w] = M - 1; O[q, g, w] = c[ok]
                put(S[q, g], c[ok], X[q, g][:, w])
                moves[q] += len(w)
                r = v[~ok][:Q]; go[q, g] = (X[q, g][:, r], D[q, g, r])
        for q in range(N):
            for g in range(8):
                y, b = go[(q - 1 - t % (N - 1)) % N, g]
                c, e = best(S[q, g], K[q, g], y, b)
                ok = e >= 9 + odd[q]
                put(S[q, g], c[ok], y[:, ok])
        odd = moves & 1
        for q in range(N):
            for d in range(1, N):
                p = (q - d) % N
                O[q, :, V + (d - 1) * G:V + d * G] = np.take_along_axis(D[p], sl[p, :, d - 1], 1)
    return {"ys": S.reshape(N, 128, W).astype(BF), "yan": A[..., :V].astype(np.float32), "yof": O[..., :V].astype(np.float32)}

@@ -1,0 +1,752 @@
+from concourse.bass import DstId, RemoteDMATransfer
+from concourse.mybir import AluOpType as O, AxisListType, ActivationFunctionType as F
+
+RO = 4
+NE = 6672
+SCRATCH, PACK = {}, {}
+FILL = {"float32": 0, "bfloat16": 0, "int32": 0, "uint16": 0}
+OWN = "AN WK X S OF SNDI WP OFb ANb AN0b E E1 E2 B OUT ONE B16 R2 CR".split()
+
+
+def _b(names, cols, d="float32", w="sbuf"):
+    for n in names.split():
+        if w == "psum" or isinstance(cols, list) or n in OWN or n[:2] in ("GS", "GR"):
+            SCRATCH[n] = (w, [128] + (cols if isinstance(cols, list) else [cols]), d)
+        else:
+            PACK[n] = ("pk_" + d, FILL[d], cols)
+            FILL[d] += (cols + 15) // 16 * 16
+            SCRATCH["pk_" + d] = ("sbuf", [128, FILL[d]], d)
+
+
+_b("K0 K1 K2 K3 K4 K5 K6 K7", 512, "float32", "psum")
+_b("CNT FD FF FP FV HC PFX", 2048, "bfloat16")
+_b("ONE B16 ID LT MB I16 IM1 IM1K B32 B40 B4 BW ZER I7 IM2K CR YW YT M16b", 128, "bfloat16")
+_b("M16 B16f ONEf A00 A01 A10 A11", 128)
+_b("E", NE + 256, "bfloat16")
+_b("E1 E2", NE, "bfloat16")
+_b("E3 CMP B", 2560, "bfloat16")
+_b("WP", 3344, "bfloat16")
+_b("X", 2576, "bfloat16")
+_b("S", 4368, "bfloat16")
+_b("WK XE CM", 4096, "bfloat16")
+_b("CT", 4112)
+_b("EQ", 2176, "bfloat16")
+_b("GT", 1024, "bfloat16")
+_b("N1b C1 C2 EQS DGH DGL XS EV Q WIN", 256, "bfloat16")
+_b("N1f MASK MD THP M256 CS COMB TR U RX", 256)
+_b("IC ON160 P2F P4F ISG R720 W1 DLT FPm RK1", 160)
+_b("CO DGf", 64)
+_b("DM10 TH TMPc T10 W2 RED VF NT NTL NLE G64 E1t PE_ T1 VA LS LS2 PS RR BAD RM GP INV HS TG Lg", 16)
+_b("INC RKM", 176)
+_b("TT Lf", 48)
+_b("GX", 24)
+_b("CSg CBg TRg Ug RXg", 64)
+_b("RI YI BI MI CI HI", 16, "int32")
+_b("AN LOI HII N1I PLI T4I P2I P4I DI DI2 DI3", 160, "int32")
+_b("OF", 208, "int32")
+_b("OFd", 624, "int32")
+_b("ANd AN0d", 480, "int32")
+_b("SNDI DQ", 48, "int32")
+_b("OFb", 624, "bfloat16")
+_b("ANb AN0b", 480, "bfloat16")
+_b("N1H P2H P2B P4H P4B BT", 160, "bfloat16")
+_b("R2 SG0 SG1", 512, "bfloat16")
+_b("DH DLO", 176, "bfloat16")
+_b("B16v C16v RFB", 16, "bfloat16")
+_b("NG", 320, "bfloat16")
+_b("HALF GH GLo WINg", 64, "bfloat16")
+_b("GD", 768, "bfloat16")
+_b("XGE CMg", 1024, "bfloat16")
+_b("EQg", 160, "bfloat16")
+_b("IDL PL P1L P2L P4L DL", 160, "uint16")
+_b("BL CL DNL VL REP POSE POSS POSG NL DGN POSQ", 16, "uint16")
+_b("SL CgL CRUg", 64, "uint16")
+_b("CAN CRU", 256, "uint16")
+_b("GI3", [3, 16], "int32")
+_b("DI4", [3, 3, 16], "int32")
+_b("OUT", 2560)
+for _t in range(RO):
+    _b("GM%d LAND%d" % (_t, _t), [3, 3, 16], "bfloat16")
+    _b("GS%d GR%d" % (_t, _t), 72, "bfloat16")
+
+SEMAPHORES = ["cv", "cs", "cp", "cg"] + ["d%d" % k for k in range(90)] + \
+    ["%s%d" % (k, t) for k in ("ga", "gl", "ua", "ul") for t in range(RO)]
+
+
+def rank_program(g, core, T, topo):
+    rank = T.rank_of(core)
+    if rank is None:
+        return
+    N = len(T.cores)
+    V, S, P, G = g.vector, g.scalar, g.tensor, g
+    QU = {"v": V, "s": S, "p": P, "g": G, "y": g.sync}
+    cnt = {"cv": 0, "cs": 0, "cp": 0, "cg": 0}
+    known = {q: {} for q in QU}
+    acc, bank, nd = {}, {}, [0]
+
+    def r(name, lo=0, hi=None, step=1, part=None):
+        ph, o, w = PACK.get(name, (name, 0, None))
+        if hi is None:
+            hi = w or T[name].shape[1]
+        ap = T[ph][:, o + lo:o + hi:step] if step > 1 else T[ph][:, o + lo:o + hi]
+        return (ap, name, lo, hi, step, lo % step, part)
+
+    def rp(name, row, lo, hi):
+        return (T[name][row::16, lo:hi], name, lo, hi, 1, 0, row)
+
+    def whole(name, ap=None, part=None):
+        return (T[name][:] if ap is None else ap, name, 0, 1 << 30, 1, 0, part)
+
+    def ind(win, off):
+        return (win[0].indirect(off[0]), [win, off])
+
+    def col(c):
+        return r("CO", c, c + 1)
+
+    def flat(x):
+        if x is None or isinstance(x, (int, float)):
+            return []
+        return list(x[1]) if isinstance(x[1], list) else [x]
+
+    def lap(a, b):
+        if a[1] <= b[0] or b[1] <= a[0] or (a[2] > 1 and a[2] == b[2] and a[3] != b[3]):
+            return False
+        return a[4] is None or b[4] is None or a[4] == b[4]
+
+    def need(q, evs):
+        for e in sorted(evs, key=lambda e: -sum(e[2].values())):
+            if known[q].get(e[0], 0) >= e[1]:
+                continue
+            QU[q].wait_ge(T.sem[e[0]], e[1])
+            for k, v in list(e[2].items()) + [(e[0], e[1])]:
+                if known[q].get(k, 0) < v:
+                    known[q][k] = v
+
+    def op(q, call, reads, writes, dma=None):
+        deps = {}
+
+        def dep(e):
+            if e[0] not in deps or deps[e[0]][1] < e[1]:
+                deps[e[0]] = e
+        tag = q if dma is None else "dma"
+        both = [(x, 0) for x in reads] + [(x, 1) for x in writes]
+        for R, isw in both:
+            if R[1][0] == "K":
+                for qq, e in bank.get(R[1], {}).items():
+                    if qq != q:
+                        dep(e)
+                continue
+            for a in acc.get(R[1], []):
+                if (isw or a[1]) and lap(a[0], R[2:7]):
+                    dep(a[3])
+        if q == "g" and dma is None and cnt["cg"]:
+            dep(("cg", cnt["cg"], {}))
+        need(q, list(deps.values()))
+        inst = call()
+        if dma is None:
+            c, n = "c" + q, cnt["c" + q] + 1
+            inst.then_inc(T.sem[c], 1)
+        elif dma == "local":
+            c, n = "d%d" % nd[0], 16
+            nd[0] += 1
+            inst.then_inc(T.sem[c], 16)
+        else:
+            c, n = dma
+        cnt[c] = n
+        ev = (c, n, dict(known[q]))
+        for R, isw in both:
+            if R[1][0] == "K":
+                bank.setdefault(R[1], {})[q] = ev
+                continue
+            reg = R[2:7]
+            L = acc.get(R[1], [])
+            if isw and reg[2] == 1 and reg[4] is None:
+                L = [a for a in L if not (reg[0] <= a[0][0] and a[0][1] <= reg[1])]
+            elif not isw:
+                L = [a for a in L if a[1] or a[2] != tag or tag == "dma" or a[0] != reg]
+            L.append((reg, isw, tag, ev))
+            acc[R[1]] = L
+
+    def arrive(R, sem, n):
+        cnt[sem] = n
+        acc.setdefault(R[1], []).append((R[2:7], 1, "dma", (sem, n, {})))
+
+    def ap(x):
+        return x if x is None or isinstance(x, (int, float)) else x[0]
+
+    def tt(o, a, b, f):
+        op("v", lambda: V.tensor_tensor(o[0], a[0], b[0], f), flat(a) + flat(b), flat(o))
+
+    def ts(o, a, s1, s2, f, f2=None):
+        more = () if f2 is None else (f2,)
+        op("v", lambda: V.tensor_scalar(o[0], a[0], ap(s1), ap(s2), f, *more), flat(a) + flat(s1) + flat(s2), flat(o))
+
+    def cp(o, a):
+        op("v", lambda: V.tensor_copy(o[0], a[0]), flat(a), flat(o))
+
+    def ms(o, v, apx=None):
+        op("v", lambda: V.memset(o[0] if apx is None else apx, v), [], flat(o))
+
+    def tr(o, a):
+        op("v", lambda: V.transpose(o[0], a[0]), flat(a), flat(o))
+
+    def scan(o, d0, d1, init, f0, f1):
+        op("v", lambda: V.tensor_tensor_scan(o[0], d0[0], d1[0], init, f0, f1), flat(d0) + flat(d1), flat(o))
+
+    def red(o, a):
+        op("v", lambda: V.tensor_reduce(o[0], a[0], AxisListType.X, O.add), flat(a), flat(o))
+
+    def act(o, a, f=F.Copy, bias=None, scale=None):
+        kw = {}
+        if bias is not None:
+            kw["bias"] = ap(bias)
+        if scale is not None:
+            kw["scale"] = ap(scale)
+        op("s", lambda: S.activation(o[0], a[0], f, **kw), flat(a) + flat(bias) + flat(scale), flat(o))
+
+    def mm(o, pairs, start=True, stop=True):
+        def call():
+            i = None
+            for k, (l, x) in enumerate(pairs):
+                i = P.matmul(o[0], l[0], x[0], start and k == 0, stop and k == len(pairs) - 1)
+            return i
+        op("p", call, [z for l, x in pairs for z in (l, x)], [o])
+
+    def fam(f, src, c0, c1):
+        return [(r(f, 128 * i, 128 * i + 128), r(src, 16 * c0 + i, 16 * c1, 16)) for i in range(16)]
+
+    def conv(f, src, c0, c1, o, extra=()):
+        mm(o, list(extra) + fam(f, src, c0, c1))
+
+    def dma(q, o, a):
+        op(q, lambda: QU[q].dma_start(o[0], a[0]), [a], [o], "local")
+
+    def iota(o, pat, base=0, cm=0, apx=None):
+        kw = {} if o[1] == "PI32" else {"allow_small_or_imprecise_dtypes": True}
+        op("g", lambda: G.iota(o[0] if apx is None else apx, pat, base, cm, **kw), [], [o])
+
+    def gsel(o, a, pat, base, cm):
+        op("g", lambda: G.affine_select(o[0], a[0], pat, O.is_ge, 0.0, base, cm), [a], [o])
+
+    def sel(dst, items):
+        for k, (row, val) in enumerate(items):
+            ts(col(dst) if k == 0 else col(40 + k), col(0), float(row), float(val), O.is_equal, O.mult)
+        for k in range(1, len(items)):
+            tt(col(dst), col(dst), col(40 + k), O.add)
+
+    dma("y", r("OF"), whole("of0"))
+    dma("s", r("AN"), whole("an0"))
+    dma("y", r("WK"), whole("wk"))
+    dma("s", r("SNDI"), whole("snd"))
+    dma("y", r("X", 0, 2560), whole("x"))
+    dma("s", r("S", 0, 4096), whole("s0"))
+    def pidx(n):
+        o = PACK["RI"][1]
+        return (T["pk_int32"][:, o:o + n], "PI32", 0, n, 1, 0, None)
+    iota(pidx(2), [[0, 2]], 0, 1)
+    ms(r("ONE"), 1.0)
+    iota(r("M16"), [[0, 8], [1, 16]])
+    gsel(r("B16"), r("ONE"), [[-16, 8], [0, 16]], 0, 1)
+    gsel(r("B16"), r("B16"), [[16, 8], [0, 16]], 15, -1)
+    iota(r("WP", 0, 2560), [[0, 2560]])
+    iota(r("IC"), [[1, 160]])
+    iota(r("R2", part="lo"), [[1, 32], [0, 16]], apx=T.R2[0:64, :])
+    iota(r("R2", part="hi"), [[0, 32], [1, 16]], apx=T.R2[64:128, :])
+    iota(r("M256"), [[0, 16], [1, 16]])
+    iota(r("N1f"), [[1, 256]], 1)
+    iota(r("NT"), [[32, 8], [0, 2]], 4096)
+    iota(r("NTL"), [[16, 16]], 4096)
+    iota(r("T10"), [[1, 16]])
+    iota(r("E", 3344, NE), [[0, NE - 3344]])
+    ts(r("YI", 0, 1), pidx(1), 31, None, O.bitwise_and)
+    ts(r("YI", 1, 2), pidx(1), 15, None, O.bitwise_and)
+    cp(col(0), r("YI", 1, 2))
+    cp(col(1), r("YI", 0, 1))
+    ms(r("WP", 2560, 3344), 0.0)
+    sel(7, [(6, 13)])
+    ts(r("WP", 2560, 3344), r("WP", 2560, 3344), col(7), None, O.add)
+    ms(r("CNT"), 0.0)
+    ts(r("LOI"), r("AN"), 15, None, O.bitwise_and)
+    ts(r("HII"), r("AN"), 4, None, O.arith_shift_right)
+    for k in range(2):
+        ts(r("OFd", 208 * k, 208 * k + 208), r("OF"), 4 * k, 15, O.arith_shift_right, O.bitwise_and)
+    ts(r("OFd", 416, 624), r("OF"), 8, None, O.arith_shift_right)
+    ts(r("W1"), r("LOI"), 48, 2400, O.mult, O.add)
+    ts(r("R720"), r("HII"), 208, 720, O.is_ge, O.mult)
+    cp(r("OFb"), r("OFd"))
+    tt(r("W1"), r("W1"), r("HII"), O.add)
+    ts(r("ISG"), r("HII"), 160, None, O.is_ge)
+    ts(r("AN0d", 0, 160), r("AN"), 15, None, O.bitwise_and)
+    tt(r("W1"), r("W1"), r("R720"), O.add)
+    ts(r("AN0d", 160, 320), r("AN"), 4, 15, O.arith_shift_right, O.bitwise_and)
+    tt(r("DLT"), r("W1"), r("AN"), O.subtract)
+    ts(r("AN0d", 320, 480), r("AN"), 8, None, O.arith_shift_right)
+    tt(r("DLT"), r("DLT"), r("ISG"), O.mult)
+    cp(r("AN0b"), r("AN0d"))
+    tt(r("N1I"), r("DLT"), r("AN"), O.add)
+    ts(r("FPm"), r("LOI"), 160, None, O.mult)
+    ts(r("ANd", 0, 160), r("N1I"), 15, None, O.bitwise_and)
+    ts(r("ANd", 160, 320), r("N1I"), 4, 15, O.arith_shift_right, O.bitwise_and)
+    ts(r("ANd", 320, 480), r("N1I"), 8, None, O.arith_shift_right)
+    tt(r("FPm"), r("FPm"), r("HII"), O.add)
+    cp(r("ANb"), r("ANd"))
+    for k in range(3):
+        dma("ysy"[k], rp("WP", k, 0, 2560), r("OFb", 208 * k, 208 * k + 160))
+        dma("sys"[k], rp("WP", k, 2560, 3328), r("OFb", 208 * k + 160, 208 * k + 208))
+        dma("ysy"[k], rp("WP", 8 + k, 0, 2560), r("AN0b", 160 * k, 160 * k + 160))
+        dma("sys"[k], rp("WP", 4 + k, 0, 2560), r("ANb", 160 * k, 160 * k + 160))
+    tt(r("DLT"), r("W1"), r("FPm"), O.subtract)
+    ts(col(13), col(0), 160.0, None, O.mult)
+    tt(r("DLT"), r("DLT"), r("ISG"), O.mult)
+    ts(r("IDL"), r("IC"), col(13), None, O.add)
+    tt(r("PLI"), r("DLT"), r("FPm"), O.add)
+    ts(col(8), col(0), 3.5, None, O.is_lt)
+    ts(col(9), col(0), 6.5, None, O.is_gt)
+    cp(r("PL"), r("PLI"))
+    tt(col(8), col(8), col(9), O.add)
+    for q in range(8):
+        cp(r("CNT", 16 * q, 2048, 129), r("B16", 16 * q, 16 * q + 16))
+    sel(5, [(4, 1), (5, 16), (6, 256)])
+    act(r("E1", 2560, 3344), r("WP", 2560, 3344))
+
+    def consts(j):
+        if j == 0:
+            ts(r("FP"), r("CNT"), col(5), None, O.mult)
+            ts(r("M16b"), r("M16"), col(0), None, O.is_equal)
+            tt(r("ID"), r("M16b"), r("B16"), O.mult)
+            ts(r("I7"), r("ID"), 7.0, None, O.mult)
+            ts(r("IM2K"), r("ID"), -2048.0, None, O.mult)
+            ms(r("CR", part="lo"), 0.25, T.CR[0:64, :])
+            ms(r("CR", part="hi"), 1.0 / 64, T.CR[64:128, :])
+            for b in range(8):
+                ms(col(48 + b), 512.0 * b - 4095.5)
+                ms(col(56 + b), 512.0 * b - 2048.0)
+        if j == 1:
+            sel(4, [(0, 1), (1, 16), (2, 256)])
+            ts(r("FD"), r("CNT"), col(4), None, O.mult)
+            ts(r("IM1"), r("ID"), -1.0, None, O.mult)
+            ts(r("HC"), r("CNT"), 0.5, None, O.mult)
+            ms(r("HALF"), 0.5)
+            ms(col(30), 2.0 ** -112)
+            ms(col(31), -2.0 ** -112)
+            ts(r("MB"), r("M16"), col(0), None, O.is_gt)
+            tt(r("LT"), r("MB"), r("B16"), O.mult)
+            ts(r("MB"), r("M16"), 1.0, None, O.add)
+            tt(r("MB"), r("MB"), r("B16"), O.mult)
+            ms(r("ON160"), 1.0)
+            ms(r("INC", 0, 1), 1.0)
+            ms(r("RKM", 160, 176), 0.0)
+            ms(r("W2", 10, 16), 1e6)
+            ms(r("DH", 160, 176), 0.0)
+            ms(r("DLO", 160, 176), 0.0)
+            ms(r("X", 2560, 2576), 0.0)
+            ms(r("CT", 4096, 4112), -4194304.0)
+            cp(r("SL", 0, 48), r("SNDI"))
+            for i in range(16):
+                ts(r("PFX", 128 * i, 128 * i + 128), r("MB"), float(i + 1), None, O.is_ge)
+        if j == 2:
+            ts(r("N1b"), r("N1f"), 1.0, None, O.mult)
+            ts(r("FV"), r("CNT"), col(0), None, O.mult)
+            ts(col(10), col(0), 9.5, None, O.is_lt)
+            ts(r("DM10"), r("T10"), col(0), None, O.is_equal)
+            ts(r("B32"), r("B16"), 32.0, None, O.mult)
+            ts(r("B40"), r("B16"), 40.0, None, O.mult)
+            ts(col(9), col(0), -0.0625, 0.9375, O.mult, O.add)
+            ts(r("MASK"), r("M256"), 0.5, None, O.is_gt)
+            ts(r("NT"), r("NT"), col(1), None, O.add)
+            ts(r("NTL"), r("NTL"), col(0), None, O.add)
+            ts(r("NLE"), r("NTL"), float(NE - 4096), None, O.add)
+            ts(r("G64"), r("NTL"), -4032.0, None, O.add)
+            ms(r("TH", 0, 1), 41.0)
+            ms(r("TH", 1, 2), 9.0)
+            ts(r("MD"), r("M256"), col(0), None, O.is_equal)
+            cp(r("REP"), r("T10"))
+            cp(r("B16f"), r("B16"))
+        if j == 3:
+            ts(col(2), col(1), 15.5, None, O.is_gt)
+            ts(col(3), col(1), 15.5, None, O.is_lt)
+            ms(r("A01", 0, 16), 0.0)
+            ms(r("A10", 112, 128), 0.0)
+            ts(r("A00"), r("ID"), col(3), None, O.mult)
+            ts(r("A01", 16, 128), r("ID", 0, 112), col(3), None, O.mult)
+            ts(r("A10", 0, 112), r("ID", 16, 128), col(2), None, O.mult)
+            ts(r("A11"), r("ID"), col(2), None, O.mult)
+            tt(r("RX"), r("M256"), r("M256"), O.mult)
+            ts(r("TR"), r("RX"), 9.0, 128.0, O.is_equal, O.mult)
+            ts(r("RX"), r("RX"), 100.0, 13.0, O.is_equal, O.mult)
+            tt(r("Q"), r("TR"), r("RX"), O.add)
+            ts(r("IM1K"), r("ID"), -1024.0, None, O.mult)
+            ts(r("I16"), r("ID"), 16.0, None, O.mult)
+            sel(6, [(3, 26)])
+            ts(r("FF"), r("CNT"), col(6), None, O.mult)
+        if j == 4:
+            act(r("E", 2560, 3344), r("WP", 2560, 3344))
+            dma("y", r("E1", 3344, NE), r("E", 3344, NE))
+            dma("y", r("E2", 3344, NE), r("E", 3344, NE))
+            for k in range(4):
+                ts(r("BI", 0, 1), r("YI", 1, 2), k, 1, O.arith_shift_right, O.bitwise_and)
+                ts(col(20 + k), r("BI", 0, 1), 2.0 ** -(1 << k) - 1.0, 1.0, O.mult, O.add)
+            tt(col(20), col(20), col(21), O.mult)
+            tt(col(22), col(22), col(23), O.mult)
+            tt(col(20), col(20), col(22), O.mult)
+            ts(r("BW"), r("B16"), col(20), None, O.mult)
+            ts(r("B4"), r("B16"), 4.0, None, O.mult)
+            ms(r("ZER"), 0.0)
+            for i in range(16):
+                ms(r("THP", i, 256, 16), 2.0 ** (1 - i))
+            ms(r("ONEf"), 1.0)
+            ts(r("T4I"), r("N1I"), 4, None, O.arith_shift_right)
+            cp(r("N1H"), r("T4I"))
+            for h, l, f, i in (("P2H", "P2B", "P2F", "P2I"), ("P4H", "P4B", "P4F", "P4I")):
+                cp(r(i), r(f))
+                ts(r("DI3"), r(i), 4, None, O.arith_shift_right)
+                cp(r(h), r("DI3"))
+                ts(r("DI3"), r(i), 15, None, O.bitwise_and)
+                cp(r(l), r("DI3"))
+
+    def ctab(b):
+        K, sg = ("K4", "K5")[b % 2], "SG%d" % (b % 2)
+        tv = [(r("I7"), r("WK", 512 * b, 512 * b + 512)), (r("CR"), r("R2"))]
+        mm(r(K), tv)
+        act(r(sg), r(K), F.Sign, bias=col(48 + b))
+        mm(r(K), tv + [(r("IM2K"), r(sg))])
+        act(r("CT", 512 * b, 512 * b + 512), r(K), F.Identity, bias=col(56 + b))
+
+    VC = [(32, 96), (96, 160)]
+
+    def addend(name, c0, c1):
+        dma("y", r("B", 16 * c0, 16 * c1), r(name, 16 * c0, 16 * c1))
+
+    def level(win, lst, out, f, extra, fill=None):
+        W = r(win, 0, NE)
+
+        def cv(c0, c1):
+            conv(f, out, c0, c1, r("K0", c0, c1), [(r(l), r(x, c0, c1)) for l, x in extra])
+
+        def vec(c0, c1):
+            tt(r(out, 16 * c0, 16 * c1), ind(W, r(lst, c0, c1)), r("B", 16 * c0, 16 * c1), O.add)
+            if out != "E3":
+                addend(out, c0, c1)
+        act(r("GT", 0, 512), ind(W, r(lst, 0, 32)))
+        vec(*VC[0])
+        mm(r("K1"), [(r("ID"), r("GT", 0, 512)), (r("ID"), r(win, 0, 512))])
+        act(r(out, 0, 512), r("K1"))
+        cv(*VC[0])
+        if fill:
+            fill()
+        vec(*VC[1])
+        cv(0, 32)
+        cv(*VC[1])
+
+    def ttol(src, n, K, k0):
+        for m2, (a0, a1) in enumerate((("A00", "A01"), ("A10", "A11"))):
+            mm(r(K, k0 + m2, k0 + n, 2), [(r(a0), r(src, 0, n, 2)), (r(a1), r(src, 1, n, 2))])
+
+    def dd1(L, n, RXn):
+        tt(r(RXn, 0, n), ind(r(L, 0, n // 16), r("REP", 0, n // 16)), r("MD", 0, n), O.mult)
+        mm(r("K5", 0, n), [(r("B16f"), r(RXn, 0, n))])
+
+    def dd2(L, n, CRn, EQn):
+        cp(r(CRn, 0, n), r("K5", 0, n))
+        z = [(r("ZER"), r("N1b", 0, n))]
+        mm(r("K5", 256, 256 + n), z, stop=False)
+        o = 0
+        for m in range(n // 16):
+            w = n - 16 * m
+            ts(r(EQn, o, o + w), r(CRn, 16 * m, n), r(L, m, m + 1), None, O.is_equal)
+            mm(r("K5", 256 + 16 * m, 272 + 16 * m), [(r("BW"), r(EQn, o, o + 16))], start=False, stop=False)
+            if w > 16:
+                mm(r("K5", 272 + 16 * m, 256 + n), [(r("B4"), r(EQn, o + 16, o + w))], start=False, stop=False)
+            o += w
+        mm(r("K5", 256, 256 + n), z, start=False)
+
+    def dd3(n, WINn):
+        tt(r(WINn, 0, n), r("K5", 256, 256 + n), r("THP", 0, n), O.is_lt)
+        conv("CNT", WINn, 0, n // 16, r("K3", 48, 48 + n // 16))
+
+    def dd4(L, n, posn, xs):
+        k = n // 16
+        ts(r("LS", 0, k), r("K3", 48, 48 + k), 8.0, None, O.is_lt)
+        tt(r("LS2", 0, k), r("LS", 0, k), r("NTL", 0, k), O.mult)
+        tt(r("PS", 0, k), r("LS2", 0, k), r(L, 0, k), O.max)
+        cp(r(posn, 0, k), r("PS", 0, k))
+        cp(ind(r("S"), r(posn, 0, k)), xs)
+
+    def guest1(t):
+        gr = "GR%d" % t
+        arrive(r(gr), "ua%d" % t, 8)
+        tt(r("DGf", 0, 4), r(gr, 64, 68), r(gr, 68, 72), O.add)
+        cp(r("DGN", 0, 4), r("DGf", 0, 4))
+        cp(r("CgL"), ind(r("CT"), r("DGN", 0, 4)))
+        for k in range(16):
+            if k % 3 == 2:
+                act(r("XGE", k, 1024, 16), r(gr, 0, 64))
+            else:
+                cp(r("XGE", k, 1024, 16), r(gr, 0, 64))
+        act(r("CSg"), ind(r("CT"), r("DGN", 0, 4)), F.Identity, bias=col(9), scale=2.0 ** -16)
+
+    def guest2(t):
+        tt(r("CMg"), ind(r("S", 0, 4096), r("CgL")), r("XGE"), O.is_lt)
+        conv("CNT", "CMg", 0, 64, r("K4", 256, 320))
+
+    def guest3(t):
+        tt(r("CBg"), r("K4", 256, 320), r("CSg"), O.add)
+        tr(r("TRg"), r("CBg"))
+        scan(r("Ug"), r("MASK", 0, 64), r("TRg"), 0.0, O.mult, O.max)
+        M = r("Ug", 15, 64, 16)
+        ts(r("MI", 0, 4), M, 65536.0, None, O.mult)
+        ts(r("T1", 0, 4), M, r("TH", 2 * t + 1, 2 * t + 2), None, O.is_lt)
+        ts(r("CI", 0, 4), r("MI", 0, 4), 4095, None, O.bitwise_and)
+        tt(r("VA", 0, 4), r("T1", 0, 4), r("NT", 0, 4), O.mult)
+        tt(r("TG", 0, 4), r("VA", 0, 4), r("CI", 0, 4), O.max)
+        ttol("TG", 4, "K6", 112)
+
+    def guest4(t):
+        cp(r("Lg", 0, 4), r("K6", 112, 116))
+        dd1("Lg", 64, "RXg")
+
+    CH = ((0, 64), (64, 128), (128, 160))
+    for t in range(RO):
+        more = t < RO - 1
+        if t == 0:
+            for c0, c1 in CH:
+                act(r("E", 16 * c0, 16 * c1), ind(r("WP"), r("IDL", c0, c1)), F.Identity, scale=col(8))
+                tt(r("E1", 16 * c0, 16 * c1), ind(r("WP"), r("PL", c0, c1)), r("E", 16 * c0, 16 * c1), O.add)
+                addend("E1", c0, c1)
+            act(r("E2", 2560, 3344), r("WP", 2560, 3344))
+            consts(0)
+            for c0, c1 in CH:
+                conv("FP", "E1", c0, c1, r("K0", c0, c1))
+            ctab(0)
+            ctab(1)
+            cp(r("P2L"), r("K0", 0, 160))
+            cp(r("P2F"), r("K0", 0, 160))
+            for win, lst, out, f in (("E1", "P2L", "E2", "FP"), ("E2", "P4L", "E3", "FD")):
+                for c0, c1 in CH:
+                    tt(r(out, 16 * c0, 16 * c1), ind(r(win, 0, 3344), r(lst, c0, c1)), r("B", 16 * c0, 16 * c1), O.add)
+                    if out == "E2":
+                        addend("E2", c0, c1)
+                    elif c0 == 0:
+                        ctab(4)
+                        ctab(5)
+                    conv(f, out, c0, c1, r("K0", c0, c1))
+                if out == "E2":
+                    ctab(2)
+                    ctab(3)
+                    consts(1)
+                    tt(r("P4F"), r("K0", 0, 160), r("P2F"), O.subtract)
+                    cp(r("P4L"), r("P4F"))
+            consts(2)
+        else:
+            level("E", "P1L", "E1", "FF", [("I16", "P2H"), ("ID", "P2B")])
+            dd4("Lf", 256, "POSS", r("XS"))
+            guest1(t - 1)
+            cp(r("P2L"), r("K0", 0, 160))
+            level("E1", "P2L", "E2", "FF", [("I16", "P4H"), ("ID", "P4B")])
+            guest2(t - 1)
+            cp(r("P4L"), r("K0", 0, 160))
+            level("E2", "P4L", "E3", "FD", [], lambda: guest3(t - 1))
+            guest4(t - 1)
+        cp(r("DI"), r("K0", 0, 160))
+        ts(r("DI"), r("DI"), 4095, None, O.bitwise_and)
+        if t:
+            dd2("Lg", 64, "CRUg", "EQg")
+        cp(r("DL"), r("DI"))
+        ts(r("DI2"), r("DI"), 4080, None, O.bitwise_and)
+        ts(r("DI3"), r("DI"), 15, None, O.bitwise_and)
+        if t:
+            dd3(64, "WINg")
+        cp(r("DH", 0, 160), r("DI2"))
+        cp(r("DLO", 0, 160), r("DI3"))
+        if t:
+            dd4("Lg", 64, "POSQ", r("GR%d" % (t - 1), 0, 64))
+        else:
+            ctab(6)
+        W = r("S", 0, 4096)
+        act(r("GT", 0, 512), ind(W, r("DL", 0, 32)))
+        for j, (c0, c1) in enumerate(VC):
+            tt(r("CMP", 16 * c0, 16 * c1), ind(W, r("DL", c0, c1)), r("X", 16 * c0, 16 * c1), O.is_le)
+            if j == 0:
+                mm(r("K2"), [(r("ID"), r("X", 0, 512)), (r("IM1"), r("GT", 0, 512))])
+                act(r("CMP", 0, 512), r("K2"), F.Sign, bias=col(30))
+            else:
+                conv("HC", "CMP", 0, 32, r("K1", 0, 32), [(r("B16"), r("HALF", 0, 32))])
+            conv("CNT", "CMP", c0, c1, r("K1", c0, c1))
+        if more:
+            act(r("GD"), ind(r("E3"), r("SL", 0, 48)))
+        if t == 0:
+            ctab(7)
+            consts(3)
+        ts(r("BT"), r("K1", 0, 160), 4.5, None, O.is_lt)
+        mm(r("K0", 160, 320), [(r("B16"), r("BT"))])
+        mm(r("K2", 0, 160), [(r("LT"), r("BT"))])
+        mm(r("K2", 320, 330), [(r("PFX", 128 * i, 128 * i + 128), r("BT", i, 160, 16)) for i in range(16)])
+        scan(r("INC", 1, 161), r("ON160"), r("K0", 160, 320), 1.0, O.mult, O.add)
+        tt(r("TMPc", 0, 10), r("INC", 16, 161, 16), r("DM10", 0, 10), O.mult)
+        red(r("RED", 0, 1), r("TMPc", 0, 10))
+        ts(r("C1"), r("N1b"), r("RED", 0, 1), col(10), O.is_ge, O.mult)
+        conv("CNT", "C1", 0, 16, r("K3", 0, 16))
+        if more:
+            conv("FD", "GD", 0, 48, r("K7", 64, 112))
+        tt(r("W2", 0, 10), r("K2", 320, 330), r("INC", 0, 160, 16), O.add)
+        tt(r("RK1"), r("K2", 0, 160), r("INC", 0, 160), O.add)
+        tt(r("RKM", 0, 160), r("RK1"), r("BT"), O.mult)
+        cp(r("BL"), r("K3", 0, 16))
+        ts(r("B16v"), r("K3", 0, 16), 16.0, None, O.mult)
+        tt(r("C2"), ind(r("W2"), r("BL")), r("N1f"), O.is_le)
+        conv("CNT", "C2", 0, 16, r("K3", 16, 32), [(r("ID"), r("B16v"))])
+        if more:
+            for d in range(3):
+                cp(whole("GI3", T.GI3[:, d, :]), r("K7", 64 + 16 * d, 80 + 16 * d))
+            for k in range(3):
+                ts(whole("DI4", T.DI4[:, :, k, :], k), whole("GI3"), 4 * k, 15, O.arith_shift_right, O.bitwise_and)
+        cp(r("CL"), r("K3", 16, 32))
+        ts(r("C16v"), r("K3", 16, 32), 16.0, None, O.mult)
+        tt(r("EQS"), ind(r("RKM"), r("CL")), r("N1f"), O.is_equal)
+        conv("FV", "EQS", 0, 16, r("K3", 32, 48), [(r("ID"), r("C16v"))])
+        tt(r("DGH"), ind(r("DH"), r("CL")), r("EQS"), O.mult)
+        tt(r("DGL"), ind(r("DLO"), r("CL")), r("EQS"), O.mult)
+        conv("CNT", "DGL", 0, 16, r("K6", 0, 16), fam("CNT", "DGH", 0, 16))
+        cp(r("VL"), r("K3", 32, 48))
+        cp(r("XS"), ind(r("X"), r("VL")))
+        for k in (0, 4, 8, 12):
+            act(r("XE", k, 4096, 16), r("XS"))
+        for k in (1, 5, 9):
+            gsel(r("XE", k, 4096, 16), r("XS"), [[0, 256]], 1, 0)
+        if more:
+            gm, ld = "GM%d" % t, "LAND%d" % t
+            cp(whole(gm), whole("DI4"))
+            tl = []
+            for d in range(1, N):
+                dst = T.cores[(rank + d) % N]
+                rid, pid, _ = topo.addr(dst)
+                e = topo.engines(core, dst)
+                tl.append(RemoteDMATransfer(src=T[gm][:, d - 1], dst=T[ld][:, d - 1], dst_ids=[DstId(rid=rid, pnc=pid)],
+                                            dma_engine_mask=(1 << e[2 * d - 2]) | (1 << e[2 * d - 1]), remote_sem=T.sem["ga%d" % t]))
+            op("g", lambda: G.remote_dma_fused(tl, local_sem=T.sem["gl%d" % t]), [whole(gm)], [], ("gl%d" % t, 6))
+            arrive(whole(ld), "ga%d" % t, 6)
+        for k in (2, 3, 6, 7, 10):
+            cp(r("XE", k, 4096, 16), r("XS"))
+        cp(r("DNL"), r("K6", 0, 16))
+        cp(r("CAN"), ind(r("CT"), r("DNL")))
+        act(r("VF"), r("K3", 32, 48))
+        for k in (11, 13, 14, 15):
+            cp(r("XE", k, 4096, 16), r("XS"))
+
+        def ecnt(n0, n1, bon, f):
+            conv(f, "CM", n0, n1, r("K4", n0, n1), [(r(bon), r("EQS", n0, n1))])
+        for j in range(2):
+            act(r("GT", 512 * j, 512 * j + 512), ind(W, r("CAN", 32 * j, 32 * j + 32)))
+        for j in range(3):
+            n0 = 64 + 64 * j
+            tt(r("CM", 16 * n0, 16 * n0 + 1024), ind(W, r("CAN", n0, n0 + 64)), r("XE", 16 * n0, 16 * n0 + 1024), O.is_lt)
+            if j < 2:
+                K = ("K1", "K2")[j]
+                mm(r(K), [(r("ID"), r("XE", 512 * j, 512 * j + 512)), (r("IM1"), r("GT", 512 * j, 512 * j + 512))])
+                act(r("CM", 512 * j, 512 * j + 512), r(K), F.Sign, bias=col(31))
+            else:
+                ecnt(0, 64, "B40", "HC")
+            ecnt(n0, n0 + 64, "B32", "CNT")
+        act(r("CS"), ind(r("CT"), r("DNL")), F.Identity, bias=col(9), scale=2.0 ** -16)
+        if t == 0:
+            consts(4)
+        if more:
+            for k in range(3):
+                dma("y", rp("E", k, 2560, 3328), whole(ld, T[ld][:, :, k, :]))
+        tt(r("COMB"), r("K4", 0, 256), r("CS"), O.add)
+        tr(r("TR"), r("COMB"))
+        scan(r("U"), r("MASK"), r("TR"), 0.0, O.mult, O.max)
+        M = r("U", 15, 256, 16)
+        ts(r("TT", 16, 32), M, r("TH", 2 * t, 2 * t + 1), None, O.is_lt)
+        ts(r("MI"), M, 65536.0, None, O.mult)
+        ts(r("VA"), M, 32.0, None, O.is_ge)
+        ts(r("CI"), r("MI"), 4095, None, O.bitwise_and)
+        tt(r("T1"), r("TT", 16, 32), r("NT"), O.mult)
+        tt(r("TT", 32, 48), r("TT", 16, 32), r("VA"), O.mult)
+        tt(r("TT", 0, 16), r("T1"), r("CI"), O.max)
+        ttol("TT", 48, "K6", 64)
+        ts(r("DQ", 0, 16), r("CI"), 15, None, O.bitwise_and)
+        ts(r("DQ", 16, 32), r("CI"), 4, 15, O.arith_shift_right, O.bitwise_and)
+        ts(r("DQ", 32, 48), r("CI"), 8, None, O.arith_shift_right)
+        for k in range(3):
+            cp(r("Q", k, 256, 16), r("DQ", 16 * k, 16 * k + 16))
+        tr(r("EV"), r("Q"))
+        cp(r("Lf"), r("K6", 64, 112))
+        cp(r("RFB"), r("Lf", 32, 48))
+        tt(r("E1t"), r("Lf", 16, 32), r("NLE"), O.mult)
+        mm(r("K7", 16, 32), [(r("B16"), r("RFB"))])
+        mm(r("K7", 0, 16), [(r("LT"), r("RFB")), (r("IM1K"), r("RFB"))])
+        tt(r("PE_"), r("E1t"), r("VF"), O.max)
+        dd1("Lf", 256, "RX")
+        cp(r("POSE"), r("PE_"))
+
+        def escat():
+            cp(ind(r("E"), r("POSE")), r("EV"))
+        if more:
+            escat()
+            for c0, c1 in VC:
+                addend("E", c0, c1)
+            conv("FF", "E", 0, 160, r("K0", 0, 160), [(r("I16"), r("N1H")), (r("ID"), r("ANb", 0, 160))])
+        ms(r("GX", 0, 1), 1024.0)
+        scan(r("GX", 1, 17), r("ON160", 0, 16), r("K7", 16, 32), 1024.0, O.mult, O.add)
+        ms(r("NG", 0, 64), 0.0)
+        tt(r("RR"), r("K7", 0, 16), r("GX", 0, 16), O.add)
+        ts(r("BAD"), r("RR"), 63.5, None, O.is_gt)
+        ts(r("RM"), r("RR"), 63.0, None, O.min)
+        tt(r("BAD"), r("BAD"), r("G64"), O.mult)
+        tt(r("GP"), r("BAD"), r("RM"), O.max)
+        cp(r("POSG"), r("GP"))
+        cp(ind(r("NG"), r("POSG")), r("N1b"))
+        conv("CNT", "NG", 0, 4, r("K7", 32, 36))
+        if more:
+            mm(r("K6", 0, 16), [(r("ONEf"), r("TT", 16, 32))])
+        ts(r("NL", 0, 4), r("K7", 32, 36), 0.0625, -1.0, O.mult, O.add)
+        ts(r("INV", 0, 4), r("K7", 32, 36), 0.5, 8192.0, O.is_lt, O.mult)
+        gs = "GS%d" % t
+        act(r("GH"), ind(r("DGH"), r("NL", 0, 4)))
+        act(r("GLo"), ind(r("DGL"), r("NL", 0, 4)))
+        act(r(gs, 0, 64), ind(r("XS"), r("NL", 0, 4)))
+        conv("CNT", "GH", 0, 4, r("K7", 36, 40))
+        conv("CNT", "GLo", 0, 4, r("K7", 40, 44))
+        if more:
+            cp(r("P1L"), r("K0", 0, 160))
+        dd2("Lf", 256, "CRU", "EQ")
+        tt(r("INV", 4, 8), r("K7", 36, 40), r("INV", 0, 4), O.add)
+        ts(r(gs, 64, 68), r("INV", 4, 8), 4096.0, None, O.min)
+        cp(r(gs, 68, 72), r("K7", 40, 44))
+        dst = T.cores[(rank + 1 + t % 3) % N]
+        rid, pid, _ = topo.addr(dst)
+        mask = sum(1 << e for e in topo.engines(core, dst)[:8])
+        op("g", lambda: G.remote_dma(out_ap=T["GR%d" % t][:], in_ap=T[gs][:], remote_sem=T.sem["ua%d" % t], local_sem=T.sem["ul%d" % t],
+                                     pid=pid, routing_id=rid, dma_engine_mask=mask), [r(gs)], [], ("ul%d" % t, 8))
+        if more:
+            act(r("E1", 2560, 3328), r("E", 2560, 3328))
+            act(r("E2", 2560, 3328), r("E", 2560, 3328))
+            red(r("HS", 0, 1), r("K6", 0, 16))
+            cp(r("HI", 0, 1), r("HS", 0, 1))
+            ts(r("HI", 1, 2), r("HI", 0, 1), 1, None, O.bitwise_and)
+            ts(r("TH", 2 * t + 2, 2 * t + 3), r("HI", 1, 2), 41.0, None, O.add)
+            ts(r("TH", 2 * t + 3, 2 * t + 4), r("HI", 1, 2), 9.0, None, O.add)
+        dd3(256, "WIN")
+    escat()
+    sel(15, [(8, 1), (9, 16), (10, 256)])
+    dd4("Lf", 256, "POSS", r("XS"))
+    ts(r("YT"), r("CNT", 128, 256), col(15), None, O.mult)
+    tt(r("YW"), r("FD", 0, 128), r("YT"), O.add)
+    guest1(RO - 1)
+    guest2(RO - 1)
+    for c in range(5):
+        K = ("K0", "K1")[c % 2]
+        mm(r(K), [(r("YW"), r("E", 512 * c, 512 * c + 512))])
+        act(r("OUT", 512 * c, 512 * c + 512), r(K))
+    dma("y", whole("yof"), rp("OUT", 0, 0, 2560))
+    dma("y", whole("yan"), rp("OUT", 1, 0, 2560))
+    guest3(RO - 1)
+    guest4(RO - 1)
+    dd2("Lg", 64, "CRUg", "EQg")
+    dd3(64, "WINg")
+    dd4("Lg", 64, "POSQ", r("GR%d" % (RO - 1), 0, 64))
+    dma("y", whole("ys"), r("S", 0, 4096))
+    for c in sorted(cnt):
+        if known["g"].get(c, 0) < cnt[c]:
+            G.wait_ge(T.sem[c], cnt[c])

@@ -2,16 +2,20 @@ from concourse.bass import DstId, RemoteDMATransfer
 from concourse.mybir import AluOpType as O, AxisListType, ActivationFunctionType as F
 
 RO = 4
-NE = 6672
+U = 2.0 ** 18
+F0, G0, NW = 16, 2576, 3344
+SC, VC = (0, 64), ((64, 112), (112, 160))
+NS = 96
 SCRATCH, PACK = {}, {}
-FILL = {"float32": 0, "bfloat16": 0, "int32": 0, "uint16": 0}
-OWN = "AN WK X S OF SNDI WP OFb ANb AN0b E E1 E2 B OUT ONE B16 R2 CR".split()
+WIDE = {"float32": 4, "bfloat16": 2, "int32": 4, "uint16": 2}
+FILL = dict.fromkeys(WIDE, 0)
+OWN = "AN WK X S OF SNDI WP ST E E1 E2 B0 B1 DR GD GSW OUT ONE B16 R2 CR DH DLO GT0".split()
 
 
 def _b(names, cols, d="float32", w="sbuf"):
     for n in names.split():
-        if w == "psum" or isinstance(cols, list) or n in OWN or n[:2] in ("GS", "GR"):
-            SCRATCH[n] = (w, [128] + (cols if isinstance(cols, list) else [cols]), d)
+        if w == "psum" or n in OWN or n[:2] in ("LA", "GR"):
+            SCRATCH[n] = (w, [128, cols], d)
         else:
             PACK[n] = ("pk_" + d, FILL[d], cols)
             FILL[d] += (cols + 15) // 16 * 16
@@ -19,58 +23,58 @@ def _b(names, cols, d="float32", w="sbuf"):
 
 
 _b("K0 K1 K2 K3 K4 K5 K6 K7", 512, "float32", "psum")
-_b("CNT FD FF FP FV HC PFX", 2048, "bfloat16")
-_b("ONE B16 ID LT MB I16 IM1 IM1K B32 B40 B4 BW ZER I7 IM2K CR YW YT M16b", 128, "bfloat16")
-_b("M16 B16f ONEf A00 A01 A10 A11", 128)
-_b("E", NE + 256, "bfloat16")
-_b("E1 E2", NE, "bfloat16")
-_b("E3 CMP B", 2560, "bfloat16")
-_b("WP", 3344, "bfloat16")
+_b("CNT HC FD FF FP FV", 2048, "bfloat16")
+_b("ONE B16 ID IDM IDU IM1 LT LE M16b I7 IM2K CR ZER B32 BD BW B4 LTS UBS IDB IDN ONES SEL0 I768 I8K GT0 "
+   "A00 A01 A10 A11 H00 H01 H10 H11", 128, "bfloat16")
+_b("M16 IDF", 128)
+_b("E", F0 + 4096 + 2560, "bfloat16")
+_b("E1 E2 WP", NW, "bfloat16")
+_b("G3 DR XE", 2560, "bfloat16")
+_b("B0 B1 GT", 1536, "bfloat16")
 _b("X", 2576, "bfloat16")
 _b("S", 4368, "bfloat16")
-_b("WK XE CM", 4096, "bfloat16")
+_b("WK CM", 4096, "bfloat16")
 _b("CT", 4112)
 _b("EQ", 2176, "bfloat16")
-_b("GT", 1024, "bfloat16")
-_b("N1b C1 C2 EQS DGH DGL XS EV Q WIN", 256, "bfloat16")
-_b("N1f MASK MD THP M256 CS COMB TR U RX", 256)
-_b("IC ON160 P2F P4F ISG R720 W1 DLT FPm RK1", 160)
-_b("CO DGf", 64)
-_b("DM10 TH TMPc T10 W2 RED VF NT NTL NLE G64 E1t PE_ T1 VA LS LS2 PS RR BAD RM GP INV HS TG Lg", 16)
-_b("INC RKM", 176)
-_b("TT Lf", 48)
-_b("GX", 24)
-_b("CSg CBg TRg Ug RXg", 64)
-_b("RI YI BI MI CI HI", 16, "int32")
-_b("AN LOI HII N1I PLI T4I P2I P4I DI DI2 DI3", 160, "int32")
+_b("ST", 6 * 224, "bfloat16")
+_b("N1S C1 C2 EQS DGH DGL EV Q NEGM", 256, "bfloat16")
+_b("XD R2 SG0 SG1", 512, "bfloat16")
+_b("N1F MASK M256 CS TR UU UX", 256)
+_b("IC", 208)
+_b("ON160 W1 T1", 160)
+_b("RKM", 176)
+_b("CO", 64)
+_b("TH W2 VF NL0 NL1 DUMP DG2 T14 T6 LF LG PM Z1 Z2 Z3 PW", 16)
+_b("CSg TRg UUg", 64)
+_b("PI YI HI", 16, "int32")
+_b("AN LOI HII SHI PLI DI DM", 160, "int32")
 _b("OF", 208, "int32")
 _b("OFd", 624, "int32")
-_b("ANd AN0d", 480, "int32")
-_b("SNDI DQ", 48, "int32")
-_b("OFb", 624, "bfloat16")
-_b("ANb AN0b", 480, "bfloat16")
-_b("N1H P2H P2B P4H P4B BT", 160, "bfloat16")
-_b("R2 SG0 SG1", 512, "bfloat16")
-_b("DH DLO", 176, "bfloat16")
-_b("B16v C16v RFB", 16, "bfloat16")
-_b("NG", 320, "bfloat16")
-_b("HALF GH GLo WINg", 64, "bfloat16")
+_b("SNDI SA SB", 48, "int32")
+_b("HM P2H P2B P4H P4B BT", 160, "bfloat16")
+_b("RS DH DLO", 176, "bfloat16")
+_b("B16v C16v INV JJ MT RF RFg", 16, "bfloat16")
+_b("RR", 32, "bfloat16")
+_b("Qg EVg", 64, "bfloat16")
 _b("GD", 768, "bfloat16")
-_b("XGE CMg", 1024, "bfloat16")
+_b("XGE CMg GSW", 1024, "bfloat16")
 _b("EQg", 160, "bfloat16")
-_b("IDL PL P1L P2L P4L DL", 160, "uint16")
-_b("BL CL DNL VL REP POSE POSS POSG NL DGN POSQ", 16, "uint16")
-_b("SL CgL CRUg", 64, "uint16")
+_b("IDL", 208, "uint16")
+_b("PL P1L P2L P4L DL", 160, "uint16")
+_b("BL CL DNL VL POSE POSS DGN", 16, "uint16")
+_b("POSG", 32, "uint16")
+_b("SL CgL CRUg REPX", 64, "uint16")
 _b("CAN CRU", 256, "uint16")
-_b("GI3", [3, 16], "int32")
-_b("DI4", [3, 3, 16], "int32")
-_b("OUT", 2560)
+_b("OUT", 320)
 for _t in range(RO):
-    _b("GM%d LAND%d" % (_t, _t), [3, 3, 16], "bfloat16")
-    _b("GS%d GR%d" % (_t, _t), 72, "bfloat16")
+    _b("GR%d" % _t, 128, "bfloat16")
+    if _t < RO - 1:
+        _b("LA%d" % _t, 768, "bfloat16")
 
-SEMAPHORES = ["cv", "cs", "cp", "cg"] + ["d%d" % k for k in range(90)] + \
+SEMAPHORES = ["cv", "cs", "cp", "cg"] + ["d%d" % k for k in range(60)] + \
     ["%s%d" % (k, t) for k in ("ga", "gl", "ua", "ul") for t in range(RO)]
+
+CYC, PE, GAT, SCA, WAKE, LOCAL, RATE, REMOTE = 0.00083, 0.00055, 1.4, 3.0, 0.15, 2.0, 200e3, 3.0
 
 
 def rank_program(g, core, T, topo):
@@ -80,121 +84,96 @@ def rank_program(g, core, T, topo):
     N = len(T.cores)
     V, S, P, G = g.vector, g.scalar, g.tensor, g
     QU = {"v": V, "s": S, "p": P, "g": G, "y": g.sync}
-    cnt = {"cv": 0, "cs": 0, "cp": 0, "cg": 0}
-    known = {q: {} for q in QU}
-    acc, bank, nd = {}, {}, [0]
+    acc, bank, calls = {}, {}, []
 
-    def r(name, lo=0, hi=None, step=1, part=None):
+    def r(name, lo=0, hi=None, step=1):
         ph, o, w = PACK.get(name, (name, 0, None))
         if hi is None:
             hi = w or T[name].shape[1]
         ap = T[ph][:, o + lo:o + hi:step] if step > 1 else T[ph][:, o + lo:o + hi]
-        return (ap, name, lo, hi, step, lo % step, part)
+        return (ap, name, lo, hi, step, lo % step, None, (hi - lo + step - 1) // step, WIDE[SCRATCH[ph][2]], 128)
 
-    def rp(name, row, lo, hi):
-        return (T[name][row::16, lo:hi], name, lo, hi, 1, 0, row)
+    def rp(name, row, step, lo, hi, part=None):
+        return (T[name][row::step, lo:hi], name, lo, hi, 1, 0, part, hi - lo, WIDE[SCRATCH[name][2]], 128 // step)
 
-    def whole(name, ap=None, part=None):
-        return (T[name][:] if ap is None else ap, name, 0, 1 << 30, 1, 0, part)
+    def half(name, h, hi):
+        return (T[name][64 * h:64 * h + 64, :], name, 0, hi, 1, 0, h, hi, 2, 64)
+
+    def hbm(name):
+        return (T[name][:], name, 0, 1, 1, 0, None, 1, 0, 0)
 
     def ind(win, off):
-        return (win[0].indirect(off[0]), [win, off])
+        return (win[0].indirect(off[0]), [win, off], 16 * off[7])
 
     def col(c):
         return r("CO", c, c + 1)
 
-    def flat(x):
-        if x is None or isinstance(x, (int, float)):
-            return []
-        return list(x[1]) if isinstance(x[1], list) else [x]
+    def flat(*xs):
+        o = []
+        for x in xs:
+            if not (x is None or isinstance(x, (int, float))):
+                o += list(x[1]) if isinstance(x[1], list) else [x]
+        return o
 
     def lap(a, b):
         if a[1] <= b[0] or b[1] <= a[0] or (a[2] > 1 and a[2] == b[2] and a[3] != b[3]):
             return False
         return a[4] is None or b[4] is None or a[4] == b[4]
 
-    def need(q, evs):
-        for e in sorted(evs, key=lambda e: -sum(e[2].values())):
-            if known[q].get(e[0], 0) >= e[1]:
-                continue
-            QU[q].wait_ge(T.sem[e[0]], e[1])
-            for k, v in list(e[2].items()) + [(e[0], e[1])]:
-                if known[q].get(k, 0) < v:
-                    known[q][k] = v
-
-    def op(q, call, reads, writes, dma=None):
-        deps = {}
-
-        def dep(e):
-            if e[0] not in deps or deps[e[0]][1] < e[1]:
-                deps[e[0]] = e
-        tag = q if dma is None else "dma"
+    def op(q, call, reads, writes, cost, sem=None, after=(), hold=None):
+        me, deps = len(calls), dict.fromkeys(after, 0)
         both = [(x, 0) for x in reads] + [(x, 1) for x in writes]
         for R, isw in both:
             if R[1][0] == "K":
                 for qq, e in bank.get(R[1], {}).items():
-                    if qq != q:
-                        dep(e)
-                continue
-            for a in acc.get(R[1], []):
-                if (isw or a[1]) and lap(a[0], R[2:7]):
-                    dep(a[3])
-        if q == "g" and dma is None and cnt["cg"]:
-            dep(("cg", cnt["cg"], {}))
-        need(q, list(deps.values()))
-        inst = call()
-        if dma is None:
-            c, n = "c" + q, cnt["c" + q] + 1
-            inst.then_inc(T.sem[c], 1)
-        elif dma == "local":
-            c, n = "d%d" % nd[0], 16
-            nd[0] += 1
-            inst.then_inc(T.sem[c], 16)
-        else:
-            c, n = dma
-        cnt[c] = n
-        ev = (c, n, dict(known[q]))
+                    deps[e] = max(deps.get(e, 0), int(qq != q))
+            else:
+                for a in acc.get(R[1], []):
+                    if (isw or a[1]) and lap(a[0], R[2:7]):
+                        deps[a[2]] = 1
+        calls.append({"q": q, "call": call, "deps": deps, "cost": cost, "sem": sem, "hold": cost if hold is None else hold})
         for R, isw in both:
             if R[1][0] == "K":
-                bank.setdefault(R[1], {})[q] = ev
+                bank.setdefault(R[1], {})[q] = me
                 continue
-            reg = R[2:7]
-            L = acc.get(R[1], [])
-            if isw and reg[2] == 1 and reg[4] is None:
+            reg, L = R[2:7], acc.get(R[1], [])
+            if isw and reg[2] == 1 and reg[4] is None and R[9] == 128:
                 L = [a for a in L if not (reg[0] <= a[0][0] and a[0][1] <= reg[1])]
-            elif not isw:
-                L = [a for a in L if a[1] or a[2] != tag or tag == "dma" or a[0] != reg]
-            L.append((reg, isw, tag, ev))
-            acc[R[1]] = L
-
-    def arrive(R, sem, n):
-        cnt[sem] = n
-        acc.setdefault(R[1], []).append((R[2:7], 1, "dma", (sem, n, {})))
+            acc[R[1]] = L + [(reg, isw, me)]
+        return me
 
     def ap(x):
         return x if x is None or isinstance(x, (int, float)) else x[0]
 
+    def vc(o, a, *more, w=None):
+        if isinstance(o[1], list):
+            return 0.05 + o[2] * SCA * CYC
+        if isinstance(a[1], list):
+            return 0.06 + a[2] * GAT * CYC
+        return max(64, a[7] * (w or (0.5 if all(x[8] == 2 for x in (o, a) + more) else 1))) * CYC
+
     def tt(o, a, b, f):
-        op("v", lambda: V.tensor_tensor(o[0], a[0], b[0], f), flat(a) + flat(b), flat(o))
+        w = 1 if "K" in (a[1][0], b[1][0]) else 2
+        op("v", lambda: V.tensor_tensor(o[0], a[0], b[0], f), flat(a, b), flat(o), vc(o, a, w=w))
 
     def ts(o, a, s1, s2, f, f2=None):
         more = () if f2 is None else (f2,)
-        op("v", lambda: V.tensor_scalar(o[0], a[0], ap(s1), ap(s2), f, *more), flat(a) + flat(s1) + flat(s2), flat(o))
+        op("v", lambda: V.tensor_scalar(o[0], a[0], ap(s1), ap(s2), f, *more), flat(a, s1, s2), flat(o), vc(o, a))
 
     def cp(o, a):
-        op("v", lambda: V.tensor_copy(o[0], a[0]), flat(a), flat(o))
+        op("v", lambda: V.tensor_copy(o[0], a[0]), flat(a), flat(o), vc(o, a))
 
-    def ms(o, v, apx=None):
-        op("v", lambda: V.memset(o[0] if apx is None else apx, v), [], flat(o))
+    def ms(o, v):
+        op("v", lambda: V.memset(o[0], v), [], [o], vc(o, o))
 
     def tr(o, a):
-        op("v", lambda: V.transpose(o[0], a[0]), flat(a), flat(o))
+        op("v", lambda: V.transpose(o[0], a[0]), [a], [o], vc(o, a))
 
     def scan(o, d0, d1, init, f0, f1):
-        op("v", lambda: V.tensor_tensor_scan(o[0], d0[0], d1[0], init, f0, f1), flat(d0) + flat(d1), flat(o))
+        op("v", lambda: V.tensor_tensor_scan(o[0], d0[0], d1[0], init, f0, f1), [d0, d1], [o], vc(o, d0, d1))
 
     def red(o, a):
-        op("v", lambda: V.tensor_reduce(o[0], a[0], AxisListType.X, O.add), flat(a), flat(o))
+        op("v", lambda: V.tensor_reduce(o[0], a[0], AxisListType.X, O.add), [a], [o], vc(o, a, w=1))
 
     def act(o, a, f=F.Copy, bias=None, scale=None):
         kw = {}
@@ -202,551 +181,496 @@ def rank_program(g, core, T, topo):
             kw["bias"] = ap(bias)
         if scale is not None:
             kw["scale"] = ap(scale)
-        op("s", lambda: S.activation(o[0], a[0], f, **kw), flat(a) + flat(bias) + flat(scale), flat(o))
+        op("s", lambda: S.activation(o[0], a[0], f, **kw), flat(a, bias, scale), [o], vc(o, a, w=1))
 
-    def mm(o, pairs, start=True, stop=True):
+    def mm(o, pairs, start=True, stop=True, outs=None):
         def call():
             i = None
             for k, (l, x) in enumerate(pairs):
-                i = P.matmul(o[0], l[0], x[0], start and k == 0, stop and k == len(pairs) - 1)
+                i = P.matmul((outs[k] if outs else o)[0], l[0], x[0], start and k == 0, stop and k == len(pairs) - 1)
             return i
-        op("p", call, [z for l, x in pairs for z in (l, x)], [o])
+        op("p", call, [z for l, x in pairs for z in (l, x)], [o], sum(max(64, x[7]) * (x[8] * x[8] // 4) for l, x in pairs) * PE)
 
-    def fam(f, src, c0, c1):
-        return [(r(f, 128 * i, 128 * i + 128), r(src, 16 * c0 + i, 16 * c1, 16)) for i in range(16)]
+    def one(f, i):
+        return r(f, 128 * i, 128 * i + 128)
 
-    def conv(f, src, c0, c1, o, extra=()):
-        mm(o, list(extra) + fam(f, src, c0, c1))
+    def fam(f, src, c0, c1, o=0):
+        return [(one(f, i), r(src, o + 16 * c0 + i, o + 16 * c1, 16)) for i in range(16)]
 
     def dma(q, o, a):
-        op(q, lambda: QU[q].dma_start(o[0], a[0]), [a], [o], "local")
+        x = o if o[9] else a
+        return op(q, lambda: QU[q].dma_start(o[0], a[0]), [a], [o], LOCAL + x[7] * x[8] * x[9] / RATE, "local", hold=0.05)
 
-    def iota(o, pat, base=0, cm=0, apx=None):
-        kw = {} if o[1] == "PI32" else {"allow_small_or_imprecise_dtypes": True}
-        op("g", lambda: G.iota(o[0] if apx is None else apx, pat, base, cm, **kw), [], [o])
+    def iota(o, pat, base=0, cm=0):
+        kw = {} if o[1] == "PI" else {"allow_small_or_imprecise_dtypes": True}
+        op("g", lambda: G.iota(o[0], pat, base, cm, **kw), [], [o], 0.13 + 2 * CYC * o[7])
 
     def gsel(o, a, pat, base, cm):
-        op("g", lambda: G.affine_select(o[0], a[0], pat, O.is_ge, 0.0, base, cm), [a], [o])
+        op("g", lambda: G.affine_select(o[0], a[0], pat, O.is_ge, 0.0, base, cm), [a], [o], 0.17 + 2 * CYC * o[7])
 
-    def sel(dst, items):
-        for k, (row, val) in enumerate(items):
-            ts(col(dst) if k == 0 else col(40 + k), col(0), float(row), float(val), O.is_equal, O.mult)
-        for k in range(1, len(items)):
-            tt(col(dst), col(dst), col(40 + k), O.add)
+    def send(call, src, dst, left, landed, n, time):
+        s = op("g", call, [src], [], time, (left, n), hold=0.5)
+        op(None, None, [], [dst], time, (landed, n), after=[s])
 
-    dma("y", r("OF"), whole("of0"))
-    dma("s", r("AN"), whole("an0"))
-    dma("y", r("WK"), whole("wk"))
-    dma("s", r("SNDI"), whole("snd"))
-    dma("y", r("X", 0, 2560), whole("x"))
-    dma("s", r("S", 0, 4096), whole("s0"))
-    def pidx(n):
-        o = PACK["RI"][1]
-        return (T["pk_int32"][:, o:o + n], "PI32", 0, n, 1, 0, None)
-    iota(pidx(2), [[0, 2]], 0, 1)
-    ms(r("ONE"), 1.0)
+    def sel(dst, rows, val):
+        for k, row in enumerate(rows):
+            ts(col(dst) if k == 0 else col(63), col(0), float(row), val, O.is_equal, O.mult)
+            if k:
+                tt(col(dst), col(dst), col(63), O.add)
+
+    def scaled(o, a, s, q="v"):
+        for c in range(0, o[7], 512):
+            x, y = r(o[1], o[2] + c, min(o[3], o[2] + c + 512)), r(a[1], a[2] + c, min(a[3], a[2] + c + 512))
+            if q == "v":
+                ts(x, y, s, None, O.mult)
+            else:
+                act(x, y, F.Identity, scale=s)
+
+    dma("y", r("OF"), hbm("of0"))
+    dma("s", r("AN"), hbm("an0"))
+    dma("s", r("SNDI"), hbm("snd"))
+    dma("y", r("WK"), hbm("wk"))
+    iota(r("PI", 0, 2), [[0, 2]], 0, 1)
     iota(r("M16"), [[0, 8], [1, 16]])
+    iota(r("IC"), [[1, 208]])
+    ms(r("ONE"), 1.0)
     gsel(r("B16"), r("ONE"), [[-16, 8], [0, 16]], 0, 1)
     gsel(r("B16"), r("B16"), [[16, 8], [0, 16]], 15, -1)
-    iota(r("WP", 0, 2560), [[0, 2560]])
-    iota(r("IC"), [[1, 160]])
-    iota(r("R2", part="lo"), [[1, 32], [0, 16]], apx=T.R2[0:64, :])
-    iota(r("R2", part="hi"), [[0, 32], [1, 16]], apx=T.R2[64:128, :])
+    iota(half("R2", 0, 512), [[1, 32], [0, 16]])
+    iota(half("R2", 1, 512), [[0, 32], [1, 16]])
     iota(r("M256"), [[0, 16], [1, 16]])
-    iota(r("N1f"), [[1, 256]], 1)
-    iota(r("NT"), [[32, 8], [0, 2]], 4096)
-    iota(r("NTL"), [[16, 16]], 4096)
-    iota(r("T10"), [[1, 16]])
-    iota(r("E", 3344, NE), [[0, NE - 3344]])
-    ts(r("YI", 0, 1), pidx(1), 31, None, O.bitwise_and)
-    ts(r("YI", 1, 2), pidx(1), 15, None, O.bitwise_and)
-    cp(col(0), r("YI", 1, 2))
-    cp(col(1), r("YI", 0, 1))
-    ms(r("WP", 2560, 3344), 0.0)
-    sel(7, [(6, 13)])
-    ts(r("WP", 2560, 3344), r("WP", 2560, 3344), col(7), None, O.add)
-    ms(r("CNT"), 0.0)
-    ts(r("LOI"), r("AN"), 15, None, O.bitwise_and)
-    ts(r("HII"), r("AN"), 4, None, O.arith_shift_right)
-    for k in range(2):
-        ts(r("OFd", 208 * k, 208 * k + 208), r("OF"), 4 * k, 15, O.arith_shift_right, O.bitwise_and)
-    ts(r("OFd", 416, 624), r("OF"), 8, None, O.arith_shift_right)
-    ts(r("W1"), r("LOI"), 48, 2400, O.mult, O.add)
-    ts(r("R720"), r("HII"), 208, 720, O.is_ge, O.mult)
-    cp(r("OFb"), r("OFd"))
-    tt(r("W1"), r("W1"), r("HII"), O.add)
-    ts(r("ISG"), r("HII"), 160, None, O.is_ge)
-    ts(r("AN0d", 0, 160), r("AN"), 15, None, O.bitwise_and)
-    tt(r("W1"), r("W1"), r("R720"), O.add)
-    ts(r("AN0d", 160, 320), r("AN"), 4, 15, O.arith_shift_right, O.bitwise_and)
-    tt(r("DLT"), r("W1"), r("AN"), O.subtract)
-    ts(r("AN0d", 320, 480), r("AN"), 8, None, O.arith_shift_right)
-    tt(r("DLT"), r("DLT"), r("ISG"), O.mult)
-    cp(r("AN0b"), r("AN0d"))
-    tt(r("N1I"), r("DLT"), r("AN"), O.add)
-    ts(r("FPm"), r("LOI"), 160, None, O.mult)
-    ts(r("ANd", 0, 160), r("N1I"), 15, None, O.bitwise_and)
-    ts(r("ANd", 160, 320), r("N1I"), 4, 15, O.arith_shift_right, O.bitwise_and)
-    ts(r("ANd", 320, 480), r("N1I"), 8, None, O.arith_shift_right)
-    tt(r("FPm"), r("FPm"), r("HII"), O.add)
-    cp(r("ANb"), r("ANd"))
-    for k in range(3):
-        dma("ysy"[k], rp("WP", k, 0, 2560), r("OFb", 208 * k, 208 * k + 160))
-        dma("sys"[k], rp("WP", k, 2560, 3328), r("OFb", 208 * k + 160, 208 * k + 208))
-        dma("ysy"[k], rp("WP", 8 + k, 0, 2560), r("AN0b", 160 * k, 160 * k + 160))
-        dma("sys"[k], rp("WP", 4 + k, 0, 2560), r("ANb", 160 * k, 160 * k + 160))
-    tt(r("DLT"), r("W1"), r("FPm"), O.subtract)
-    ts(col(13), col(0), 160.0, None, O.mult)
-    tt(r("DLT"), r("DLT"), r("ISG"), O.mult)
-    ts(r("IDL"), r("IC"), col(13), None, O.add)
-    tt(r("PLI"), r("DLT"), r("FPm"), O.add)
-    ts(col(8), col(0), 3.5, None, O.is_lt)
-    ts(col(9), col(0), 6.5, None, O.is_gt)
-    cp(r("PL"), r("PLI"))
-    tt(col(8), col(8), col(9), O.add)
+    iota(r("N1F"), [[1, 256]], 1)
+    iota(r("NL0"), [[16, 16]])
+    for n in ("B1", "DR", "B0"):
+        for c in range(0, T[n].shape[1], 512):
+            iota(r(n, c, c + 512), [[0, 512]])
+    for k, m in enumerate((15, 31, 3)):
+        ts(r("YI", k, k + 1), r("PI", 0, 1), m, None, O.bitwise_and)
+    cp(r("CO", 0, 3), r("YI", 0, 3))
+    for c in range(0, NW, 1120):
+        ms(r("WP", c, min(NW, c + 1120)), 0.0)
+    ms(r("ST"), 0.0)
+    for c in range(0, 2048, 1024):
+        ms(r("CNT", c, c + 1024), 0.0)
     for q in range(8):
-        cp(r("CNT", 16 * q, 2048, 129), r("B16", 16 * q, 16 * q + 16))
-    sel(5, [(4, 1), (5, 16), (6, 256)])
-    act(r("E1", 2560, 3344), r("WP", 2560, 3344))
-
-    def consts(j):
-        if j == 0:
-            ts(r("FP"), r("CNT"), col(5), None, O.mult)
-            ts(r("M16b"), r("M16"), col(0), None, O.is_equal)
-            tt(r("ID"), r("M16b"), r("B16"), O.mult)
-            ts(r("I7"), r("ID"), 7.0, None, O.mult)
-            ts(r("IM2K"), r("ID"), -2048.0, None, O.mult)
-            ms(r("CR", part="lo"), 0.25, T.CR[0:64, :])
-            ms(r("CR", part="hi"), 1.0 / 64, T.CR[64:128, :])
-            for b in range(8):
-                ms(col(48 + b), 512.0 * b - 4095.5)
-                ms(col(56 + b), 512.0 * b - 2048.0)
-        if j == 1:
-            sel(4, [(0, 1), (1, 16), (2, 256)])
-            ts(r("FD"), r("CNT"), col(4), None, O.mult)
-            ts(r("IM1"), r("ID"), -1.0, None, O.mult)
-            ts(r("HC"), r("CNT"), 0.5, None, O.mult)
-            ms(r("HALF"), 0.5)
-            ms(col(30), 2.0 ** -112)
-            ms(col(31), -2.0 ** -112)
-            ts(r("MB"), r("M16"), col(0), None, O.is_gt)
-            tt(r("LT"), r("MB"), r("B16"), O.mult)
-            ts(r("MB"), r("M16"), 1.0, None, O.add)
-            tt(r("MB"), r("MB"), r("B16"), O.mult)
-            ms(r("ON160"), 1.0)
-            ms(r("INC", 0, 1), 1.0)
-            ms(r("RKM", 160, 176), 0.0)
-            ms(r("W2", 10, 16), 1e6)
-            ms(r("DH", 160, 176), 0.0)
-            ms(r("DLO", 160, 176), 0.0)
-            ms(r("X", 2560, 2576), 0.0)
-            ms(r("CT", 4096, 4112), -4194304.0)
-            cp(r("SL", 0, 48), r("SNDI"))
-            for i in range(16):
-                ts(r("PFX", 128 * i, 128 * i + 128), r("MB"), float(i + 1), None, O.is_ge)
-        if j == 2:
-            ts(r("N1b"), r("N1f"), 1.0, None, O.mult)
-            ts(r("FV"), r("CNT"), col(0), None, O.mult)
-            ts(col(10), col(0), 9.5, None, O.is_lt)
-            ts(r("DM10"), r("T10"), col(0), None, O.is_equal)
-            ts(r("B32"), r("B16"), 32.0, None, O.mult)
-            ts(r("B40"), r("B16"), 40.0, None, O.mult)
-            ts(col(9), col(0), -0.0625, 0.9375, O.mult, O.add)
-            ts(r("MASK"), r("M256"), 0.5, None, O.is_gt)
-            ts(r("NT"), r("NT"), col(1), None, O.add)
-            ts(r("NTL"), r("NTL"), col(0), None, O.add)
-            ts(r("NLE"), r("NTL"), float(NE - 4096), None, O.add)
-            ts(r("G64"), r("NTL"), -4032.0, None, O.add)
-            ms(r("TH", 0, 1), 41.0)
-            ms(r("TH", 1, 2), 9.0)
-            ts(r("MD"), r("M256"), col(0), None, O.is_equal)
-            cp(r("REP"), r("T10"))
-            cp(r("B16f"), r("B16"))
-        if j == 3:
-            ts(col(2), col(1), 15.5, None, O.is_gt)
-            ts(col(3), col(1), 15.5, None, O.is_lt)
-            ms(r("A01", 0, 16), 0.0)
-            ms(r("A10", 112, 128), 0.0)
-            ts(r("A00"), r("ID"), col(3), None, O.mult)
-            ts(r("A01", 16, 128), r("ID", 0, 112), col(3), None, O.mult)
-            ts(r("A10", 0, 112), r("ID", 16, 128), col(2), None, O.mult)
-            ts(r("A11"), r("ID"), col(2), None, O.mult)
-            tt(r("RX"), r("M256"), r("M256"), O.mult)
-            ts(r("TR"), r("RX"), 9.0, 128.0, O.is_equal, O.mult)
-            ts(r("RX"), r("RX"), 100.0, 13.0, O.is_equal, O.mult)
-            tt(r("Q"), r("TR"), r("RX"), O.add)
-            ts(r("IM1K"), r("ID"), -1024.0, None, O.mult)
-            ts(r("I16"), r("ID"), 16.0, None, O.mult)
-            sel(6, [(3, 26)])
-            ts(r("FF"), r("CNT"), col(6), None, O.mult)
-        if j == 4:
-            act(r("E", 2560, 3344), r("WP", 2560, 3344))
-            dma("y", r("E1", 3344, NE), r("E", 3344, NE))
-            dma("y", r("E2", 3344, NE), r("E", 3344, NE))
-            for k in range(4):
-                ts(r("BI", 0, 1), r("YI", 1, 2), k, 1, O.arith_shift_right, O.bitwise_and)
-                ts(col(20 + k), r("BI", 0, 1), 2.0 ** -(1 << k) - 1.0, 1.0, O.mult, O.add)
-            tt(col(20), col(20), col(21), O.mult)
-            tt(col(22), col(22), col(23), O.mult)
-            tt(col(20), col(20), col(22), O.mult)
-            ts(r("BW"), r("B16"), col(20), None, O.mult)
-            ts(r("B4"), r("B16"), 4.0, None, O.mult)
-            ms(r("ZER"), 0.0)
-            for i in range(16):
-                ms(r("THP", i, 256, 16), 2.0 ** (1 - i))
-            ms(r("ONEf"), 1.0)
-            ts(r("T4I"), r("N1I"), 4, None, O.arith_shift_right)
-            cp(r("N1H"), r("T4I"))
-            for h, l, f, i in (("P2H", "P2B", "P2F", "P2I"), ("P4H", "P4B", "P4F", "P4I")):
-                cp(r(i), r(f))
-                ts(r("DI3"), r(i), 4, None, O.arith_shift_right)
-                cp(r(h), r("DI3"))
-                ts(r("DI3"), r(i), 15, None, O.bitwise_and)
-                cp(r(l), r("DI3"))
+        ts(r("CNT", 16 * q, 2048, 129), r("B16", 16 * q, 16 * q + 16), U, None, O.mult)
+    ts(r("M16b"), r("M16"), col(0), None, O.is_equal)
+    tt(r("ID"), r("M16b"), r("B16"), O.mult)
+    ts(col(3), col(2), 0.0, None, O.is_equal)
+    ts(r("IDM"), r("ID"), col(3), None, O.mult)
+    sel(4, (2, 3), 1 / U)
+    ts(col(5), col(4), -U, 1.0, O.mult, O.add)
+    scaled(r("FP"), r("CNT"), col(4))
+    sel(6, (1,), 1.0)
+    tt(col(6), col(6), col(3), O.add)
+    ts(col(6), col(6), 1 / U, None, O.mult)
+    scaled(r("FD"), r("CNT"), col(6), "s")
+    sel(7, (12,), -1 / U)
+    scaled(r("FF"), r("CNT"), col(7), "s")
+    scaled(r("HC"), r("CNT"), 0.5, "s")
+    ts(col(8), col(0), 1 / U, None, O.mult)
+    scaled(r("FV"), r("CNT"), col(8), "s")
+    for n, s in (("IDU", U), ("IM1", -1.0), ("I7", 7.0), ("IM2K", -2048.0), ("IDB", 0.125), ("IDN", -0.125), ("I768", 768.0),
+                 ("I8K", 8192.0), ("IDF", 1.0)):
+        act(r(n), r("ID"), F.Identity, scale=s)
+    for n, s in (("B32", -32 * U), ("B4", 4.0), ("ZER", 0.0)):
+        act(r(n), r("B16"), F.Identity, scale=s)
+    ts(r("LE"), r("M16"), col(0), None, O.is_gt)
+    tt(r("LT"), r("LE"), r("B16"), O.mult)
+    tt(r("LE"), r("LT"), r("ID"), O.add)
+    act(r("LTS"), r("LT"), F.Identity, scale=2.0 ** -13)
+    tt(r("UBS"), r("B16"), r("LT"), O.subtract)
+    act(r("UBS"), r("UBS"), F.Identity, scale=2.0 ** -13)
+    act(r("ONES"), r("ONE"), F.Identity, scale=2.0 ** -13)
+    sel(9, (0,), 1.0)
+    act(r("SEL0"), r("ONE"), F.Identity, scale=col(9))
+    sel(10, (0, 12), 1.0)
+    act(r("BD"), r("B16"), F.Identity, scale=col(10))
+    ts(col(11), col(0), 9.5, None, O.is_lt)
+    ts(col(12), col(1), 15.5, None, O.is_lt)
+    ts(col(13), col(1), 15.5, None, O.is_gt)
+    for a, s in (("A", 1.0), ("H", 0.5)):
+        ms(r(a + "01", 0, 16), 0.0)
+        ms(r(a + "10", 112, 128), 0.0)
+        ts(r(a + "00"), r("ID"), col(12), s, O.mult, O.mult)
+        ts(r(a + "01", 16, 128), r("ID", 0, 112), col(12), s, O.mult, O.mult)
+        ts(r(a + "10", 0, 112), r("ID", 16, 128), col(13), s, O.mult, O.mult)
+        ts(r(a + "11"), r("ID"), col(13), s, O.mult, O.mult)
+    ms(r("ON160"), 1.0)
+    ms(r("Z1"), 0.5)
+    ms(r("Z2"), 0.0)
+    scan(r("PW"), r("Z1"), r("Z2"), 4.0, O.mult, O.add)
+    tt(r("PW"), r("PW"), r("M16b", 0, 16), O.mult)
+    red(col(14), r("PW"))
+    ts(r("BW"), r("B16"), col(14), 0.5, O.mult, O.mult)
+    ms(half("CR", 0, 128), 0.25)
+    ms(half("CR", 1, 128), 1.0 / 64)
+    for b in range(8):
+        if b > 3:
+            ms(col(40 + b), 512.0 * b - 4095.5)
+        ms(col(48 + b), 512.0 * b - (2048.0 if b > 3 else 0.0))
+    ms(col(15), 2.0 ** -112)
+    ms(col(16), -2.0 ** -112)
+    ms(col(17), float(F0))
+    for c, e in ((18, 32), (19, 40), (20, 0)):
+        ts(col(c), col(0), -16384.0, 15 * 16384.0 + 4096.0 + e * U, O.mult, O.add)
+    ts(r("N1S"), r("N1F"), U, None, O.mult)
+    ts(r("MASK"), r("M256"), 0.5, None, O.is_gt)
+    ts(r("NEGM"), r("M256"), col(0), -2048.0, O.not_equal, O.mult)
+    ts(r("NL0"), r("NL0"), col(0), None, O.add)
+    ts(r("NL1"), r("NL0"), 1.0, None, O.add)
+    ts(r("DUMP"), r("NL0"), 8192.0, None, O.add)
+    ts(r("DG2"), r("NL0"), 256.0 - 1024.0, None, O.add)
+    ts(r("REPX"), r("IC", 0, 64), 2.0, None, O.mult)
+    ms(r("TH", 0, 1), 9 * U)
+    ms(r("RS", 0, 1), 0.0)
+    ms(r("RR", 0, 1), 0.0)
+    ms(r("RKM", 160, 176), 0.0)
+    ms(r("W2", 10, 16), 1e12)
+    ms(r("DH", 160, 176), 0.0)
+    ms(r("DLO", 160, 176), 0.0)
+    ms(r("X", 2560, 2576), 0.0)
+    ms(r("CT", 4096, 4112), -2.0 ** 24)
+    for n in ("E", "E1", "E2"):
+        ms(r(n, 0, F0), 0.0)
+    ms(r("Q"), 0.0)
+    ms(r("Qg"), 0.0)
+    ms(r("Q", 1, 256, 16), -4096.0)
+    ms(r("Q", 5, 256, 16), 3328.0)
+    ms(r("GT0"), 0.0)
+    sel(21, (12,), 4096.0)
+    ts(r("GT0", 1, 128, 2), r("GT0", 1, 128, 2), col(21), None, O.add)
+    for k in range(3):
+        ts(r("OFd", 208 * k, 208 * k + 208), r("OF"), 15 << 4 * k, None, O.bitwise_and)
+        cp(r("ST", 224 * k, 224 * k + 208), r("OFd", 208 * k, 208 * k + 208))
+    FH, LO, HI = (r("ST", 224 * k, 224 * k + 160) for k in (3, 4, 5))
+    ts(r("LOI"), r("AN"), 15, None, O.bitwise_and)
+    ts(r("HII"), r("AN"), 4080, None, O.bitwise_and)
+    ts(r("SHI"), r("AN"), 4, None, O.arith_shift_right)
+    cp(LO, r("LOI"))
+    cp(HI, r("HII"))
+    ts(r("T1"), r("HII"), 3328, 3344, O.is_lt, O.mult)
+    ts(r("HM"), r("HII"), -3328, None, O.add)
+    tt(FH, r("T1"), r("HM"), O.add)
+    laid = [dma("ys"[k % 2], rp("WP", row, 16, 0, NW, row), r("ST", 224 * seg, 224 * seg + 209))
+            for k, (row, seg) in enumerate(((0, 0), (4, 1), (8, 2), (3, 4), (6, 4), (5, 5), (2, 3)))]
+    for q, o, n in (("y", r("X", 0, 2560), "x"), ("s", r("S", 0, 4096), "s0")):
+        op(q, lambda q=q, o=o, n=n: QU[q].dma_start(o[0], T[n][:]), [], [o], 2 * LOCAL + o[7] * 256 / RATE, "local", after=laid, hold=0.05)
+    ts(r("W1"), r("LOI"), 209, None, O.mult)
+    tt(r("PLI"), r("W1"), r("SHI"), O.add)
+    cp(r("PL"), r("PLI"))
+    ts(col(22), col(0), 209.0, None, O.mult)
+    ts(r("IDL"), r("IC"), col(22), None, O.add)
+    ts(r("SA"), r("SNDI"), 15, None, O.bitwise_and)
+    ts(r("SB"), r("SNDI"), 4, None, O.arith_shift_right)
+    ts(r("SA"), r("SA"), 160, None, O.mult)
+    tt(r("SA"), r("SA"), r("SB"), O.add)
+    cp(r("SL", 0, 48), r("SA"))
 
     def ctab(b):
         K, sg = ("K4", "K5")[b % 2], "SG%d" % (b % 2)
         tv = [(r("I7"), r("WK", 512 * b, 512 * b + 512)), (r("CR"), r("R2"))]
         mm(r(K), tv)
-        act(r(sg), r(K), F.Sign, bias=col(48 + b))
-        mm(r(K), tv + [(r("IM2K"), r(sg))])
-        act(r("CT", 512 * b, 512 * b + 512), r(K), F.Identity, bias=col(56 + b))
+        if b > 3:
+            act(r(sg), r(K), F.Sign, bias=col(40 + b))
+            mm(r(K), tv + [(r("IM2K"), r(sg))])
+        act(r("CT", 512 * b, 512 * b + 512), r(K), F.Identity, bias=col(48 + b))
 
-    VC = [(32, 96), (96, 160)]
+    CH = (SC,) + VC
+    BK = dict(zip(CH, ("K0", "K7", "K6")))
 
-    def addend(name, c0, c1):
-        dma("y", r("B", 16 * c0, 16 * c1), r(name, 16 * c0, 16 * c1))
+    def fe(n, c0, c1):
+        return r(n, F0 + 16 * c0, F0 + 16 * c1)
 
-    def level(win, lst, out, f, extra, fill=None):
-        W = r(win, 0, NE)
+    def addend(b, src):
+        for c0, c1 in VC:
+            dma("y", rp(b, 0, 4, 16 * (c0 - SC[1]), 16 * (c1 - SC[1])), rp(src, 0, 4, F0 + 16 * c0, F0 + 16 * c1))
 
-        def cv(c0, c1):
-            conv(f, out, c0, c1, r("K0", c0, c1), [(r(l), r(x, c0, c1)) for l, x in extra])
+    def lists(f, src, lst, hi, lo, first):
+        for c in CH:
+            K = r(BK[c], 0, c[1] - c[0])
+            extra = [] if first else [(r("ID"), r(x[1], x[2] + c[0], x[2] + c[1])) for x in (hi, lo)]
+            mm(K, extra + fam(f, src, *c, F0))
+            cp(r(lst, *c), K)
+            if first:
+                cp(r(hi[1], *c), K)
+                tt(r(lo[1], *c), K, r(hi[1], *c), O.subtract)
 
-        def vec(c0, c1):
-            tt(r(out, 16 * c0, 16 * c1), ind(W, r(lst, c0, c1)), r("B", 16 * c0, 16 * c1), O.add)
-            if out != "E3":
-                addend(out, c0, c1)
-        act(r("GT", 0, 512), ind(W, r(lst, 0, 32)))
-        vec(*VC[0])
-        mm(r("K1"), [(r("ID"), r("GT", 0, 512)), (r("ID"), r(win, 0, 512))])
-        act(r(out, 0, 512), r("K1"))
-        cv(*VC[0])
-        if fill:
-            fill()
-        vec(*VC[1])
-        cv(0, 32)
-        cv(*VC[1])
+    def shared(win, lst, src, o, sign, out, f, bias=None):
+        for j, K in enumerate(("K1", "K2")):
+            act(r("GT", 512 * j, 512 * j + 512), ind(win, r(lst, 32 * j, 32 * j + 32)))
+        for j, K in enumerate(("K1", "K2")):
+            mm(r(K), [(r(sign[0]), r(src, o + 512 * j, o + 512 * j + 512))], stop=False)
+            mm(r(K), [(r(sign[1]), r("GT", 512 * j, 512 * j + 512))], start=False)
+            act(r(out, o + 512 * j, o + 512 * j + 512), r(K), f, bias=bias)
 
-    def ttol(src, n, K, k0):
-        for m2, (a0, a1) in enumerate((("A00", "A01"), ("A10", "A11"))):
-            mm(r(K, k0 + m2, k0 + n, 2), [(r(a0), r(src, 0, n, 2)), (r(a1), r(src, 1, n, 2))])
+    def level(win, lst, b, out):
+        W = r(win, 0, NW)
+        shared(W, lst, win, F0, ("IDM", "ID"), out, F.Copy)
+        for c0, c1 in VC:
+            tt(fe(out, c0, c1), ind(W, r(lst, c0, c1)), r(b, 16 * (c0 - SC[1]), 16 * (c1 - SC[1])), O.add)
 
-    def dd1(L, n, RXn):
-        tt(r(RXn, 0, n), ind(r(L, 0, n // 16), r("REP", 0, n // 16)), r("MD", 0, n), O.mult)
-        mm(r("K5", 0, n), [(r("B16f"), r(RXn, 0, n))])
+    def tl(a, src, m2, o=0, step=1):
+        return [(r("%s%d%d" % (a, m2, h)), r(src[1], src[2] + step * h, src[3], 2 * step)) for h in range(2)]
 
-    def dd2(L, n, CRn, EQn):
-        cp(r(CRn, 0, n), r("K5", 0, n))
-        z = [(r("ZER"), r("N1b", 0, n))]
-        mm(r("K5", 256, 256 + n), z, stop=False)
-        o = 0
-        for m in range(n // 16):
-            w = n - 16 * m
-            ts(r(EQn, o, o + w), r(CRn, 16 * m, n), r(L, m, m + 1), None, O.is_equal)
-            mm(r("K5", 256 + 16 * m, 272 + 16 * m), [(r("BW"), r(EQn, o, o + 16))], start=False, stop=False)
-            if w > 16:
-                mm(r("K5", 272 + 16 * m, 256 + n), [(r("B4"), r(EQn, o + 16, o + w))], start=False, stop=False)
-            o += w
-        mm(r("K5", 256, 256 + n), z, start=False)
-
-    def dd3(n, WINn):
-        tt(r(WINn, 0, n), r("K5", 256, 256 + n), r("THP", 0, n), O.is_lt)
-        conv("CNT", WINn, 0, n // 16, r("K3", 48, 48 + n // 16))
-
-    def dd4(L, n, posn, xs):
+    def choose(K, n, tn, un, rf, q, ev, th):
         k = n // 16
-        ts(r("LS", 0, k), r("K3", 48, 48 + k), 8.0, None, O.is_lt)
-        tt(r("LS2", 0, k), r("LS", 0, k), r("NTL", 0, k), O.mult)
-        tt(r("PS", 0, k), r("LS2", 0, k), r(L, 0, k), O.max)
-        cp(r(posn, 0, k), r("PS", 0, k))
-        cp(ind(r("S"), r(posn, 0, k)), xs)
+        tr(r(tn), K)
+        scan(r(un), r("MASK", 0, n), r(tn), 0.0, O.mult, O.max)
+        M = r(un, 15, n, 16)
+        ts(r(rf, 0, k), M, th, 8192.0 if n == 256 else 16384.0, O.is_lt, O.mult)
+        ts(r("T6", 0, k), M, 1.5 * 2.0 ** 29, 1.5 * 2.0 ** 29, O.add, O.subtract)
+        ts(r("T14", 0, k), M, 1.5 * 2.0 ** 37, 1.5 * 2.0 ** 37, O.add, O.subtract)
+        tt(r(q, 0, n, 16), M, r("T6", 0, k), O.subtract)
+        tt(r(q, 12, n, 16), r("T6", 0, k), r("T14", 0, k), O.subtract)
+        tr(r(ev), r(q))
 
-    def guest1(t):
+    def settle(n, q, rf, ev, L, cr, eq, xs, inv):
+        k = n // 16
+        for m2 in range(2):
+            mm(r("K5", m2, k, 2), ([(r("I8K"), r("INV", m2, k, 2))] if inv else []) + tl("A", r(rf, 0, k), m2)
+               + tl("A", r(q, 0, n), m2, step=16) + tl("A", r(q, 12, n), m2, step=16))
+        tt(r(L, 0, k), r("K5", 0, k), r("DUMP", 0, k), O.min)
+        mm(r("K5", 256, 256 + n), [(r("BD"), r(ev))])
+        cp(r(cr, 0, n), r("K5", 256, 256 + n))
+        mm(r("K4", 0, n), [(r("ID"), r("NEGM", 0, n))], stop=False)
+        o = 0
+        for m in range(k):
+            w = n - 16 * m
+            ts(r(eq, o, o + w), r(cr, 16 * m, n), r(L, m, m + 1), None, O.is_equal)
+            mm(r("K4", 16 * m, 16 * m + 16), [(r("BW"), r(eq, o, o + 16))], start=False, stop=False)
+            if w > 16:
+                mm(r("K4", 16 * m + 16, n), [(r("B4"), r(eq, o + 16, o + w))], start=False, stop=False)
+            o += w
+        mm(r("K4", 0, n), [(r("ZER"), r("NEGM", 0, n))], start=False)
+        scan(r("UX", 0, n), r("MASK", 0, n), r("K4", 0, n), 0.0, O.mult, O.max)
+        ts(r("Z1", 0, k), r("UX", 15, n, 16), col(14), 16384.0, O.is_ge, O.mult)
+        tt(r("Z2", 0, k), r("Z1", 0, k), r(L, 0, k), O.max)
+        tt(r("Z3", 0, k), r("Z2", 0, k), r("DUMP", 0, k), O.min)
+        ts(r("POSS", 0, k), r("Z3", 0, k), -4096.0, None, O.add)
+        cp(ind(r("S"), r("POSS", 0, k)), xs)
+
+    def guests(t):
         gr = "GR%d" % t
-        arrive(r(gr), "ua%d" % t, 8)
-        tt(r("DGf", 0, 4), r(gr, 64, 68), r(gr, 68, 72), O.add)
-        cp(r("DGN", 0, 4), r("DGf", 0, 4))
+        mm(r("K3", 64, 68), [(one("FD", i), r(gr, 2 * i + 1, 128, 32)) for i in range(16)])
+        cp(r("DGN", 0, 4), r("K3", 64, 68))
         cp(r("CgL"), ind(r("CT"), r("DGN", 0, 4)))
-        for k in range(16):
-            if k % 3 == 2:
-                act(r("XGE", k, 1024, 16), r(gr, 0, 64))
-            else:
-                cp(r("XGE", k, 1024, 16), r(gr, 0, 64))
-        act(r("CSg"), ind(r("CT"), r("DGN", 0, 4)), F.Identity, bias=col(9), scale=2.0 ** -16)
-
-    def guest2(t):
+        act(r("XGE"), ind(r(gr), r("REPX")))
+        act(r("CSg"), ind(r("CT"), r("DGN", 0, 4)), F.Identity, bias=col(20))
+        mm(r("K4", 256, 320), [(r("IDF"), r("CSg"))], stop=False)
         tt(r("CMg"), ind(r("S", 0, 4096), r("CgL")), r("XGE"), O.is_lt)
-        conv("CNT", "CMg", 0, 64, r("K4", 256, 320))
+        mm(r("K4", 256, 320), fam("CNT", "CMg", 0, 64), start=False)
+        choose(r("K4", 256, 320), 64, "TRg", "UUg", "RFg", "Qg", "EVg", r("TH", t, t + 1))
+        settle(64, "Qg", "RFg", "EVg", "LG", "CRUg", "EQg", r(gr, 0, 128, 2), False)
 
-    def guest3(t):
-        tt(r("CBg"), r("K4", 256, 320), r("CSg"), O.add)
-        tr(r("TRg"), r("CBg"))
-        scan(r("Ug"), r("MASK", 0, 64), r("TRg"), 0.0, O.mult, O.max)
-        M = r("Ug", 15, 64, 16)
-        ts(r("MI", 0, 4), M, 65536.0, None, O.mult)
-        ts(r("T1", 0, 4), M, r("TH", 2 * t + 1, 2 * t + 2), None, O.is_lt)
-        ts(r("CI", 0, 4), r("MI", 0, 4), 4095, None, O.bitwise_and)
-        tt(r("VA", 0, 4), r("T1", 0, 4), r("NT", 0, 4), O.mult)
-        tt(r("TG", 0, 4), r("VA", 0, 4), r("CI", 0, 4), O.max)
-        ttol("TG", 4, "K6", 112)
-
-    def guest4(t):
-        cp(r("Lg", 0, 4), r("K6", 112, 116))
-        dd1("Lg", 64, "RXg")
-
-    CH = ((0, 64), (64, 128), (128, 160))
     for t in range(RO):
         more = t < RO - 1
         if t == 0:
-            for c0, c1 in CH:
-                act(r("E", 16 * c0, 16 * c1), ind(r("WP"), r("IDL", c0, c1)), F.Identity, scale=col(8))
-                tt(r("E1", 16 * c0, 16 * c1), ind(r("WP"), r("PL", c0, c1)), r("E", 16 * c0, 16 * c1), O.add)
-                addend("E1", c0, c1)
-            act(r("E2", 2560, 3344), r("WP", 2560, 3344))
-            consts(0)
-            for c0, c1 in CH:
-                conv("FP", "E1", c0, c1, r("K0", c0, c1))
-            ctab(0)
-            ctab(1)
-            cp(r("P2L"), r("K0", 0, 160))
-            cp(r("P2F"), r("K0", 0, 160))
-            for win, lst, out, f in (("E1", "P2L", "E2", "FP"), ("E2", "P4L", "E3", "FD")):
-                for c0, c1 in CH:
-                    tt(r(out, 16 * c0, 16 * c1), ind(r(win, 0, 3344), r(lst, c0, c1)), r("B", 16 * c0, 16 * c1), O.add)
-                    if out == "E2":
-                        addend("E2", c0, c1)
-                    elif c0 == 0:
-                        ctab(4)
-                        ctab(5)
-                    conv(f, out, c0, c1, r("K0", c0, c1))
-                if out == "E2":
-                    ctab(2)
-                    ctab(3)
-                    consts(1)
-                    tt(r("P4F"), r("K0", 0, 160), r("P2F"), O.subtract)
-                    cp(r("P4L"), r("P4F"))
-            consts(2)
+            ts(r("E", G0, NW), ind(r("WP"), r("IDL", 160, 208)), col(5), None, O.mult)
+            for n in ("E1", "E2"):
+                dma("y", r(n, G0, NW), r("E", G0, NW))
+            for c0, c1 in ((0, 32), (32, 64)) + VC:
+                act(fe("E", c0, c1), ind(r("WP"), r("IDL", c0, c1)), F.Identity, scale=col(5))
+                tt(fe("E1", c0, c1), ind(r("WP"), r("PL", c0, c1)), fe("E", c0, c1), O.add)
         else:
-            level("E", "P1L", "E1", "FF", [("I16", "P2H"), ("ID", "P2B")])
-            dd4("Lf", 256, "POSS", r("XS"))
-            guest1(t - 1)
-            cp(r("P2L"), r("K0", 0, 160))
-            level("E1", "P2L", "E2", "FF", [("I16", "P4H"), ("ID", "P4B")])
-            guest2(t - 1)
-            cp(r("P4L"), r("K0", 0, 160))
-            level("E2", "P4L", "E3", "FD", [], lambda: guest3(t - 1))
-            guest4(t - 1)
-        cp(r("DI"), r("K0", 0, 160))
-        ts(r("DI"), r("DI"), 4095, None, O.bitwise_and)
-        if t:
-            dd2("Lg", 64, "CRUg", "EQg")
-        cp(r("DL"), r("DI"))
-        ts(r("DI2"), r("DI"), 4080, None, O.bitwise_and)
-        ts(r("DI3"), r("DI"), 15, None, O.bitwise_and)
-        if t:
-            dd3(64, "WINg")
-        cp(r("DH", 0, 160), r("DI2"))
-        cp(r("DLO", 0, 160), r("DI3"))
-        if t:
-            dd4("Lg", 64, "POSQ", r("GR%d" % (t - 1), 0, 64))
-        else:
-            ctab(6)
-        W = r("S", 0, 4096)
-        act(r("GT", 0, 512), ind(W, r("DL", 0, 32)))
-        for j, (c0, c1) in enumerate(VC):
-            tt(r("CMP", 16 * c0, 16 * c1), ind(W, r("DL", c0, c1)), r("X", 16 * c0, 16 * c1), O.is_le)
-            if j == 0:
-                mm(r("K2"), [(r("ID"), r("X", 0, 512)), (r("IM1"), r("GT", 0, 512))])
-                act(r("CMP", 0, 512), r("K2"), F.Sign, bias=col(30))
-            else:
-                conv("HC", "CMP", 0, 32, r("K1", 0, 32), [(r("B16"), r("HALF", 0, 32))])
-            conv("CNT", "CMP", c0, c1, r("K1", c0, c1))
-        if more:
-            act(r("GD"), ind(r("E3"), r("SL", 0, 48)))
+            level("E", "P1L", "B0", "E1")
+        addend("B1", "E1")
+        lists("FF" if t else "FP", "E1", "P2L", r("P2H"), r("P2B"), t == 0)
+        level("E1", "P2L", "B1", "E2")
+        lists("FF" if t else "FP", "E2", "P4L", r("P4H"), r("P4B"), t == 0)
+        W = r("E2", 0, NW)
+        for c in CH:
+            mm(r(BK[c], 128, 128 + c[1] - c[0]), fam("FD", "E2", *c, F0), stop=False)
+        for j, c in enumerate(CH):
+            (act if j < 2 else cp)(r("G3", 16 * c[0], 16 * c[1]), ind(W, r("P4L", *c)))
+            K = r(BK[c], 128, 128 + c[1] - c[0])
+            mm(K, fam("FD", "G3", *c), start=False)
+            cp(r("DI", *c), K)
+        ts(r("DM"), r("DI"), 4095, None, O.bitwise_and)
+        cp(r("DL"), r("DM"))
+        cp(r("DH", 0, 160), r("DM"))
+        tt(r("DLO", 0, 160), r("DM"), r("DH", 0, 160), O.subtract)
         if t == 0:
-            ctab(7)
-            consts(3)
-        ts(r("BT"), r("K1", 0, 160), 4.5, None, O.is_lt)
-        mm(r("K0", 160, 320), [(r("B16"), r("BT"))])
-        mm(r("K2", 0, 160), [(r("LT"), r("BT"))])
-        mm(r("K2", 320, 330), [(r("PFX", 128 * i, 128 * i + 128), r("BT", i, 160, 16)) for i in range(16)])
-        scan(r("INC", 1, 161), r("ON160"), r("K0", 160, 320), 1.0, O.mult, O.add)
-        tt(r("TMPc", 0, 10), r("INC", 16, 161, 16), r("DM10", 0, 10), O.mult)
-        red(r("RED", 0, 1), r("TMPc", 0, 10))
-        ts(r("C1"), r("N1b"), r("RED", 0, 1), col(10), O.is_ge, O.mult)
-        conv("CNT", "C1", 0, 16, r("K3", 0, 16))
+            for b in range(8):
+                ctab(b)
         if more:
-            conv("FD", "GD", 0, 48, r("K7", 64, 112))
-        tt(r("W2", 0, 10), r("K2", 320, 330), r("INC", 0, 160, 16), O.add)
-        tt(r("RK1"), r("K2", 0, 160), r("INC", 0, 160), O.add)
-        tt(r("RKM", 0, 160), r("RK1"), r("BT"), O.mult)
-        cp(r("BL"), r("K3", 0, 16))
-        ts(r("B16v"), r("K3", 0, 16), 16.0, None, O.mult)
-        tt(r("C2"), ind(r("W2"), r("BL")), r("N1f"), O.is_le)
-        conv("CNT", "C2", 0, 16, r("K3", 16, 32), [(r("ID"), r("B16v"))])
-        if more:
-            for d in range(3):
-                cp(whole("GI3", T.GI3[:, d, :]), r("K7", 64 + 16 * d, 80 + 16 * d))
-            for k in range(3):
-                ts(whole("DI4", T.DI4[:, :, k, :], k), whole("GI3"), 4 * k, 15, O.arith_shift_right, O.bitwise_and)
-        cp(r("CL"), r("K3", 16, 32))
-        ts(r("C16v"), r("K3", 16, 32), 16.0, None, O.mult)
-        tt(r("EQS"), ind(r("RKM"), r("CL")), r("N1f"), O.is_equal)
-        conv("FV", "EQS", 0, 16, r("K3", 32, 48), [(r("ID"), r("C16v"))])
-        tt(r("DGH"), ind(r("DH"), r("CL")), r("EQS"), O.mult)
-        tt(r("DGL"), ind(r("DLO"), r("CL")), r("EQS"), O.mult)
-        conv("CNT", "DGL", 0, 16, r("K6", 0, 16), fam("CNT", "DGH", 0, 16))
-        cp(r("VL"), r("K3", 32, 48))
-        cp(r("XS"), ind(r("X"), r("VL")))
-        for k in (0, 4, 8, 12):
-            act(r("XE", k, 4096, 16), r("XS"))
-        for k in (1, 5, 9):
-            gsel(r("XE", k, 4096, 16), r("XS"), [[0, 256]], 1, 0)
-        if more:
-            gm, ld = "GM%d" % t, "LAND%d" % t
-            cp(whole(gm), whole("DI4"))
-            tl = []
+            dma("y", rp("DR", 12, 16, 0, 2560, 12), r("DH", 0, 160))
+            dma("y", rp("DR", 0, 16, 0, 2560, 0), r("DLO", 0, 160))
+            act(r("GD"), ind(r("DR"), r("SL", 0, 48)))
+            la, tls = "LA%d" % t, []
             for d in range(1, N):
                 dst = T.cores[(rank + d) % N]
                 rid, pid, _ = topo.addr(dst)
                 e = topo.engines(core, dst)
-                tl.append(RemoteDMATransfer(src=T[gm][:, d - 1], dst=T[ld][:, d - 1], dst_ids=[DstId(rid=rid, pnc=pid)],
-                                            dma_engine_mask=(1 << e[2 * d - 2]) | (1 << e[2 * d - 1]), remote_sem=T.sem["ga%d" % t]))
-            op("g", lambda: G.remote_dma_fused(tl, local_sem=T.sem["gl%d" % t]), [whole(gm)], [], ("gl%d" % t, 6))
-            arrive(whole(ld), "ga%d" % t, 6)
-        for k in (2, 3, 6, 7, 10):
-            cp(r("XE", k, 4096, 16), r("XS"))
-        cp(r("DNL"), r("K6", 0, 16))
+                tls.append(RemoteDMATransfer(src=T.GD[:, 256 * d - 256:256 * d], dst=T[la][:, 256 * d - 256:256 * d], dst_ids=[DstId(rid=rid, pnc=pid)],
+                                             dma_engine_mask=(1 << e[d - 1]) | (1 << e[d + 3]), remote_sem=T.sem["ga%d" % t]))
+            send(lambda tls=tls, t=t: G.remote_dma_fused(tls, local_sem=T.sem["gl%d" % t]), r("GD"), r(la), "gl%d" % t, "ga%d" % t, 6, 2 * REMOTE)
+            for n in ("E", "E1", "E2"):
+                dma("y", rp(n, 0, 4, G0, NW), rp(la, 0, 4, 0, 768))
+        W = r("S", 0, 4096)
+        shared(W, "DL", "X", 0, ("ID", "IM1"), "CM", F.Sign, col(15))
+        for c0, c1 in VC:
+            tt(r("CM", 16 * c0, 16 * c1), ind(W, r("DL", c0, c1)), r("X", 16 * c0, 16 * c1), O.is_le)
+        for c in CH:
+            K = r(BK[c], 256, 256 + c[1] - c[0])
+            mm(K, fam("HC" if c == SC else "CNT", "CM", *c))
+            ts(r("BT", *c), K, (-3.5 if c == SC else 4.5) * U, None, O.is_lt)
+        scan(r("RS", 1, 161), r("ON160"), r("BT"), 0.0, O.mult, O.add)
+        mm(r("K3", 0, 1), [(one("CNT", b), r("RS", 16 * b + 16, 16 * b + 17)) for b in range(10)])
+        mm(r("K5", 0, 10), fam("CNT", "RS", 0, 10, 1))
+        mm(r("K4", 0, 160), [(r("B16"), r("RS", 0, 160)), (r("LE"), r("BT"))])
+        mm(r("K0", 400, 401), [(r("B16"), r("RS", 160, 161))])
+        ts(r("C1"), r("N1S"), r("K3", 0, 1), col(11), O.is_gt, O.mult)
+        act(r("W2", 0, 10), r("K5", 0, 10))
+        tt(r("RKM", 0, 160), r("K4", 0, 160), r("BT"), O.mult)
+        TOT = r("K0", 400, 401)
+        ts(r("INV"), r("NL0"), TOT, None, O.is_ge)
+        ts(r("JJ"), r("NL1"), TOT, 0.0, O.subtract, O.max)
+        if more:
+            ts(r("MT", 0, 1), TOT, 256.0, None, O.min)
+        mm(r("K3", 16, 32), fam("CNT", "C1", 0, 16))
+        ts(r("BL"), r("K3", 16, 32), 1 / U, None, O.mult)
+        ts(r("B16v"), r("K3", 16, 32), 16 / U, None, O.mult)
+        tt(r("C2"), ind(r("W2"), r("BL")), r("N1S"), O.is_lt)
+        mm(r("K3", 32, 48), [(r("IDU"), r("B16v"))] + fam("CNT", "C2", 0, 16))
+        ts(r("CL"), r("K3", 32, 48), 1 / U, None, O.mult)
+        ts(r("C16v"), r("K3", 32, 48), 16 / U, None, O.mult)
+        tt(r("EQS"), ind(r("RKM"), r("CL")), r("N1F"), O.is_equal)
+        tt(r("DGH"), ind(r("DH"), r("CL")), r("EQS"), O.mult)
+        tt(r("DGL"), ind(r("DLO"), r("CL")), r("EQS"), O.mult)
+        mm(r("K3", 48, 64), [(r("ID"), r("C16v"))] + fam("FV", "EQS", 0, 16))
+        mm(r("K5", 16, 32), fam("CNT", "DGH", 0, 16), stop=False)
+        mm(r("K5", 16, 32), fam("CNT", "DGL", 0, 16), start=False)
+        cp(r("VL"), r("K3", 48, 64))
+        act(r("VF"), r("K3", 48, 64), F.Identity, bias=col(17))
+        ts(r("DNL"), r("K5", 16, 32), 1 / U, None, O.mult)
+        act(r("XD", 0, 256), ind(r("X"), r("VL")))
         cp(r("CAN"), ind(r("CT"), r("DNL")))
-        act(r("VF"), r("K3", 32, 48))
-        for k in (11, 13, 14, 15):
-            cp(r("XE", k, 4096, 16), r("XS"))
-
-        def ecnt(n0, n1, bon, f):
-            conv(f, "CM", n0, n1, r("K4", n0, n1), [(r(bon), r("EQS", n0, n1))])
-        for j in range(2):
-            act(r("GT", 512 * j, 512 * j + 512), ind(W, r("CAN", 32 * j, 32 * j + 32)))
-        for j in range(3):
-            n0 = 64 + 64 * j
-            tt(r("CM", 16 * n0, 16 * n0 + 1024), ind(W, r("CAN", n0, n0 + 64)), r("XE", 16 * n0, 16 * n0 + 1024), O.is_lt)
-            if j < 2:
-                K = ("K1", "K2")[j]
-                mm(r(K), [(r("ID"), r("XE", 512 * j, 512 * j + 512)), (r("IM1"), r("GT", 512 * j, 512 * j + 512))])
-                act(r("CM", 512 * j, 512 * j + 512), r(K), F.Sign, bias=col(31))
+        mm(r("K1", 0, 256), [(one("CNT", 12), r("DGH")), (one("CNT", 0), r("DGL"))])
+        act(r("XD", 256, 512), r("K1", 0, 256), F.Identity, scale=1 / U)
+        mm(r("K0", 0, 16), [(r("IDF"), r("VF")), (r("I768"), r("INV"))], stop=False)
+        for k in range(16):
+            x, y = r("XE", k, 16 * (256 - NS), 16), r("XD", NS, 256)
+            if k % 5 == 4:
+                gsel(x, y, [[0, 256 - NS]], 1, 0)
             else:
-                ecnt(0, 64, "B40", "HC")
-            ecnt(n0, n0 + 64, "B32", "CNT")
-        act(r("CS"), ind(r("CT"), r("DNL")), F.Identity, bias=col(9), scale=2.0 ** -16)
-        if t == 0:
-            consts(4)
+                cp(x, y)
+        for j, K in enumerate(("K2", "K3", "K1")):
+            act(r("GT", 512 * j, 512 * j + 512), ind(W, r("CAN", 32 * j, 32 * j + 32)))
+            mm(r(K), [(r("ZER"), r("X", 0, 512))] + [(r("ID"), r("XD", 32 * j, 32 * j + 32))] * 16, stop=False,
+               outs=[r(K)] + [r(K, k, 512, 16) for k in range(16)])
+            mm(r(K), [(r("IM1"), r("GT", 512 * j, 512 * j + 512))], start=False)
+            act(r("CM", 512 * j, 512 * j + 512), r(K), F.Sign, bias=col(16))
+        act(r("CS", NS, 256), ind(r("CT"), r("DNL", NS // 16, 16)), F.Identity, bias=col(18))
+        act(r("CS", 0, NS), ind(r("CT"), r("DNL", 0, NS // 16)), F.Identity, bias=col(19))
+        for n0, n1 in ((NS, 192), (192, 256)):
+            tt(r("CM", 16 * n0, 16 * n1), ind(W, r("CAN", n0, n1)), r("XE", 16 * (n0 - NS), 16 * (n1 - NS)), O.is_lt)
+        for n0, n1 in ((NS, 192), (0, NS), (192, 256)):
+            mm(r("K4", n0, n1), [(r("IDF"), r("CS", n0, n1)), (r("B32"), r("EQS", n0, n1))], stop=False)
+            mm(r("K4", n0, n1), fam("CNT" if n0 else "HC", "CM", n0, n1), start=False)
+        choose(r("K4", 0, 256), 256, "TR", "UU", "RF", "Q", "EV", r("TH", t, t + 1))
+        mm(r("K0", 0, 16), tl("H", r("RF"), 0) + tl("H", r("RF"), 1) + [(r("ID"), r("JJ"))], start=False,
+           outs=[r("K0", 0, 16, 2)] * 2 + [r("K0", 1, 16, 2)] * 2 + [r("K0", 0, 16)])
+        cp(r("POSE"), r("K0", 0, 16))
+        cp(ind(r("E"), r("POSE")), r("EV"))
         if more:
-            for k in range(3):
-                dma("y", rp("E", k, 2560, 3328), whole(ld, T[ld][:, :, k, :]))
-        tt(r("COMB"), r("K4", 0, 256), r("CS"), O.add)
-        tr(r("TR"), r("COMB"))
-        scan(r("U"), r("MASK"), r("TR"), 0.0, O.mult, O.max)
-        M = r("U", 15, 256, 16)
-        ts(r("TT", 16, 32), M, r("TH", 2 * t, 2 * t + 1), None, O.is_lt)
-        ts(r("MI"), M, 65536.0, None, O.mult)
-        ts(r("VA"), M, 32.0, None, O.is_ge)
-        ts(r("CI"), r("MI"), 4095, None, O.bitwise_and)
-        tt(r("T1"), r("TT", 16, 32), r("NT"), O.mult)
-        tt(r("TT", 32, 48), r("TT", 16, 32), r("VA"), O.mult)
-        tt(r("TT", 0, 16), r("T1"), r("CI"), O.max)
-        ttol("TT", 48, "K6", 64)
-        ts(r("DQ", 0, 16), r("CI"), 15, None, O.bitwise_and)
-        ts(r("DQ", 16, 32), r("CI"), 4, 15, O.arith_shift_right, O.bitwise_and)
-        ts(r("DQ", 32, 48), r("CI"), 8, None, O.arith_shift_right)
-        for k in range(3):
-            cp(r("Q", k, 256, 16), r("DQ", 16 * k, 16 * k + 16))
-        tr(r("EV"), r("Q"))
-        cp(r("Lf"), r("K6", 64, 112))
-        cp(r("RFB"), r("Lf", 32, 48))
-        tt(r("E1t"), r("Lf", 16, 32), r("NLE"), O.mult)
-        mm(r("K7", 16, 32), [(r("B16"), r("RFB"))])
-        mm(r("K7", 0, 16), [(r("LT"), r("RFB")), (r("IM1K"), r("RFB"))])
-        tt(r("PE_"), r("E1t"), r("VF"), O.max)
-        dd1("Lf", 256, "RX")
-        cp(r("POSE"), r("PE_"))
-
-        def escat():
-            cp(ind(r("E"), r("POSE")), r("EV"))
-        if more:
-            escat()
-            for c0, c1 in VC:
-                addend("E", c0, c1)
-            conv("FF", "E", 0, 160, r("K0", 0, 160), [(r("I16"), r("N1H")), (r("ID"), r("ANb", 0, 160))])
-        ms(r("GX", 0, 1), 1024.0)
-        scan(r("GX", 1, 17), r("ON160", 0, 16), r("K7", 16, 32), 1024.0, O.mult, O.add)
-        ms(r("NG", 0, 64), 0.0)
-        tt(r("RR"), r("K7", 0, 16), r("GX", 0, 16), O.add)
-        ts(r("BAD"), r("RR"), 63.5, None, O.is_gt)
-        ts(r("RM"), r("RR"), 63.0, None, O.min)
-        tt(r("BAD"), r("BAD"), r("G64"), O.mult)
-        tt(r("GP"), r("BAD"), r("RM"), O.max)
-        cp(r("POSG"), r("GP"))
-        cp(ind(r("NG"), r("POSG")), r("N1b"))
-        conv("CNT", "NG", 0, 4, r("K7", 32, 36))
-        if more:
-            mm(r("K6", 0, 16), [(r("ONEf"), r("TT", 16, 32))])
-        ts(r("NL", 0, 4), r("K7", 32, 36), 0.0625, -1.0, O.mult, O.add)
-        ts(r("INV", 0, 4), r("K7", 32, 36), 0.5, 8192.0, O.is_lt, O.mult)
-        gs = "GS%d" % t
-        act(r("GH"), ind(r("DGH"), r("NL", 0, 4)))
-        act(r("GLo"), ind(r("DGL"), r("NL", 0, 4)))
-        act(r(gs, 0, 64), ind(r("XS"), r("NL", 0, 4)))
-        conv("CNT", "GH", 0, 4, r("K7", 36, 40))
-        conv("CNT", "GLo", 0, 4, r("K7", 40, 44))
-        if more:
-            cp(r("P1L"), r("K0", 0, 160))
-        dd2("Lf", 256, "CRU", "EQ")
-        tt(r("INV", 4, 8), r("K7", 36, 40), r("INV", 0, 4), O.add)
-        ts(r(gs, 64, 68), r("INV", 4, 8), 4096.0, None, O.min)
-        cp(r(gs, 68, 72), r("K7", 40, 44))
+            addend("B0", "E")
+            lists("FF", "E", "P1L", FH, LO, False)
+        for m2 in range(2):
+            mm(r("K3", m2, 16, 2), tl("A", r("RF"), m2))
+        scan(r("RR", 1, 17), r("ON160", 0, 16), r("K3", 0, 16), 0.0, O.mult, O.add)
+        a, b = r("RR", 1, 17), r("RR", 0, 16)
+        mm(r("K3", 16, 32), [(r("LTS"), a), (r("UBS"), b), (r("IDN"), a), (r("IDB"), b)])
+        tt(r("PM"), r("K3", 16, 32), r("DG2"), O.min)
+        ts(r("POSG", 0, 16), r("PM"), 2.0, 2048.0, O.mult, O.add)
+        ts(r("POSG", 16, 32), r("PM"), 2.0, 2049.0, O.mult, O.add)
+        gsel(r("GSW", 0, 128), r("GT0"), [[0, 128]], 1, 0)
+        cp(ind(r("GSW"), r("POSG")), r("XD"))
         dst = T.cores[(rank + 1 + t % 3) % N]
         rid, pid, _ = topo.addr(dst)
         mask = sum(1 << e for e in topo.engines(core, dst)[:8])
-        op("g", lambda: G.remote_dma(out_ap=T["GR%d" % t][:], in_ap=T[gs][:], remote_sem=T.sem["ua%d" % t], local_sem=T.sem["ul%d" % t],
-                                     pid=pid, routing_id=rid, dma_engine_mask=mask), [r(gs)], [], ("ul%d" % t, 8))
+        send(lambda t=t, rid=rid, pid=pid, mask=mask: G.remote_dma(
+            out_ap=T["GR%d" % t][:], in_ap=T.GSW[:, 0:128], remote_sem=T.sem["ua%d" % t], local_sem=T.sem["ul%d" % t],
+            pid=pid, routing_id=rid, dma_engine_mask=mask), r("GSW", 0, 128), r("GR%d" % t), "ul%d" % t, "ua%d" % t, 8, REMOTE)
         if more:
-            act(r("E1", 2560, 3328), r("E", 2560, 3328))
-            act(r("E2", 2560, 3328), r("E", 2560, 3328))
-            red(r("HS", 0, 1), r("K6", 0, 16))
-            cp(r("HI", 0, 1), r("HS", 0, 1))
+            mm(r("K3", 40, 41), [(r("ONES"), r("RR", 16, 17)), (r("SEL0"), r("MT", 0, 1))])
+            cp(r("HI", 0, 1), r("K3", 40, 41))
             ts(r("HI", 1, 2), r("HI", 0, 1), 1, None, O.bitwise_and)
-            ts(r("TH", 2 * t + 2, 2 * t + 3), r("HI", 1, 2), 41.0, None, O.add)
-            ts(r("TH", 2 * t + 3, 2 * t + 4), r("HI", 1, 2), 9.0, None, O.add)
-        dd3(256, "WIN")
-    escat()
-    sel(15, [(8, 1), (9, 16), (10, 256)])
-    dd4("Lf", 256, "POSS", r("XS"))
-    ts(r("YT"), r("CNT", 128, 256), col(15), None, O.mult)
-    tt(r("YW"), r("FD", 0, 128), r("YT"), O.add)
-    guest1(RO - 1)
-    guest2(RO - 1)
-    for c in range(5):
-        K = ("K0", "K1")[c % 2]
-        mm(r(K), [(r("YW"), r("E", 512 * c, 512 * c + 512))])
-        act(r("OUT", 512 * c, 512 * c + 512), r(K))
-    dma("y", whole("yof"), rp("OUT", 0, 0, 2560))
-    dma("y", whole("yan"), rp("OUT", 1, 0, 2560))
-    guest3(RO - 1)
-    guest4(RO - 1)
-    dd2("Lg", 64, "CRUg", "EQg")
-    dd3(64, "WINg")
-    dd4("Lg", 64, "POSQ", r("GR%d" % (RO - 1), 0, 64))
-    dma("y", whole("ys"), r("S", 0, 4096))
-    for c in sorted(cnt):
-        if known["g"].get(c, 0) < cnt[c]:
-            G.wait_ge(T.sem[c], cnt[c])
+            ts(r("TH", t + 1, t + 2), r("HI", 1, 2), U, 9 * U, O.mult, O.add)
+        settle(256, "Q", "RF", "EV", "LF", "CRU", "EQ", r("XD", 0, 256), True)
+        guests(t)
+        if t == 0:
+            sel(23, (5, 6), 1 / U)
+            scaled(r("FP"), r("CNT"), col(23), "s")
+    mm(r("K1", 0, 320), [(one(f, 2 * c + k), r("E", F0 + 320 * c, F0 + 320 * c + 320)) for c in range(8) for k, f in enumerate(("FD", "FP"))])
+    act(r("OUT"), r("K1", 0, 320))
+    dma("s", hbm("yof"), rp("OUT", 0, 2, 0, 320))
+    dma("s", hbm("yan"), rp("OUT", 1, 2, 0, 320))
+    dma("y", hbm("ys"), r("S", 0, 4096))
+
+    nxt = [[] for c in calls]
+    for i, c in enumerate(calls):
+        for d in c["deps"]:
+            nxt[d].append(i)
+    for i in range(len(calls) - 1, -1, -1):
+        calls[i]["way"] = calls[i]["cost"] + max([WAKE * calls[j]["deps"][i] + calls[j]["way"] for j in nxt[i]] + [0])
+    free, left, order = dict.fromkeys(list(QU) + [None], 0.0), [len(c["deps"]) for c in calls], []
+    pool = {q: [] for q in free}
+
+    def offer(i):
+        c = calls[i]
+        c["from"] = max([calls[d]["end"] + WAKE if w else calls[d]["at"] for d, w in c["deps"].items()] + [0])
+        pool[c["q"]].append(i)
+    for i in range(len(calls)):
+        if not left[i]:
+            offer(i)
+    while len(order) < len(calls):
+        q = min((q for q in pool if pool[q]), key=lambda q: max(free[q], min(calls[i]["from"] for i in pool[q])))
+        now = max(free[q], min(calls[i]["from"] for i in pool[q]))
+        i = max((i for i in pool[q] if calls[i]["from"] <= now), key=lambda i: calls[i]["way"])
+        j = max((j for j in pool[q] if calls[j]["from"] < now + calls[i]["hold"]), key=lambda j: calls[j]["way"] - calls[j]["from"])
+        if calls[j]["way"] > calls[i]["way"] + calls[j]["from"] - now + calls[j]["hold"]:
+            i = j
+        c = calls[i]
+        pool[q].remove(i)
+        c["at"] = max(now, c["from"])
+        c["end"] = c["at"] + c["cost"]
+        if q:
+            free[q] = c["at"] + c["hold"]
+        order.append(i)
+        for j in nxt[i]:
+            left[j] -= 1
+            if not left[j]:
+                offer(j)
+
+    cnt, known, nd = {"cv": 0, "cs": 0, "cp": 0, "cg": 0}, {q: {} for q in QU}, 0
+    for i in order:
+        c = calls[i]
+        q = c["q"]
+        if q is None:
+            c["ev"] = c["sem"] + ({},)
+            cnt[c["sem"][0]] = c["sem"][1]
+            continue
+        evs = [calls[d]["ev"] for d, w in c["deps"].items() if w]
+        if q == "g" and c["sem"] is None and cnt["cg"]:
+            evs.append(("cg", cnt["cg"], {}))
+        for e in sorted(evs, key=lambda e: (-sum(e[2].values()), -e[1])):
+            if known[q].get(e[0], 0) < e[1]:
+                QU[q].wait_ge(T.sem[e[0]], e[1])
+                for k, v in list(e[2].items()) + [(e[0], e[1])]:
+                    known[q][k] = max(v, known[q].get(k, 0))
+        inst = c["call"]()
+        if c["sem"] is None:
+            s, n = "c" + q, cnt["c" + q] + 1
+            inst.then_inc(T.sem[s], 1)
+        elif c["sem"] == "local":
+            s, n = "d%d" % nd, 16
+            nd += 1
+            inst.then_inc(T.sem[s], 16)
+        else:
+            s, n = c["sem"]
+        cnt[s] = n
+        c["ev"] = (s, n, dict(known[q]))
+    for s in sorted(cnt):
+        if known["g"].get(s, 0) < cnt[s]:
+            G.wait_ge(T.sem[s], cnt[s])

@@ -4,17 +4,21 @@ from concourse.mybir import AluOpType as O, AxisListType, ActivationFunctionType
 RO = 4
 U = 2.0 ** 18
 F0, G0, NW = 16, 2576, 3344
-SC, VC = (0, 64), ((64, 112), (112, 160))
+CH = ((0, 80), (80, 120), (120, 160))
+CD = ((0, 96), (96, 160))
+C3 = ("sv", "ss")
+CC = ((0, 64), (64, 112), (112, 160))
 NS = 96
+CN = (("K4", 96, 192), ("K5", 192, 256), ("K6", 0, NS))
 SCRATCH, PACK = {}, {}
 WIDE = {"float32": 4, "bfloat16": 2, "int32": 4, "uint16": 2}
 FILL = dict.fromkeys(WIDE, 0)
-OWN = "AN WK X S OF SNDI WP ST E E1 E2 B0 B1 DR GD GSW OUT ONE B16 R2 CR DH DLO GT0".split()
+OWN = "AN WK X S OF SNDI WP ST E E1 E2 B0 B1 DR GD NG XS DNL OUT ONE B16 R2 CR DH DLO".split()
 
 
 def _b(names, cols, d="float32", w="sbuf"):
     for n in names.split():
-        if w == "psum" or n in OWN or n[:2] in ("LA", "GR"):
+        if w == "psum" or n in OWN or n[:2] in ("LA", "GR", "GX", "GN"):
             SCRATCH[n] = (w, [128, cols], d)
         else:
             PACK[n] = ("pk_" + d, FILL[d], cols)
@@ -24,7 +28,7 @@ def _b(names, cols, d="float32", w="sbuf"):
 
 _b("K0 K1 K2 K3 K4 K5 K6 K7", 512, "float32", "psum")
 _b("CNT HC FD FF FP FV", 2048, "bfloat16")
-_b("ONE B16 ID IDM IDU IM1 LT LE M16b I7 IM2K CR ZER B32 BD BW B4 LTS UBS IDB IDN ONES SEL0 I768 I8K GT0 "
+_b("ONE B16 ID IDM IDU IM1 LT LE M16b I7 IM2K CR B32 BD BW B4 LTS UBS IDB IDN ONES SEL0 I768 I8K "
    "A00 A01 A10 A11 H00 H01 H10 H11", 128, "bfloat16")
 _b("M16 IDF", 128)
 _b("E", F0 + 4096 + 2560, "bfloat16")
@@ -34,17 +38,17 @@ _b("B0 B1 GT", 1536, "bfloat16")
 _b("X", 2576, "bfloat16")
 _b("S", 4368, "bfloat16")
 _b("WK CM", 4096, "bfloat16")
-_b("CT", 4112)
+_b("CT", 4096)
 _b("EQ", 2176, "bfloat16")
 _b("ST", 6 * 224, "bfloat16")
-_b("N1S C1 C2 EQS DGH DGL EV Q NEGM", 256, "bfloat16")
-_b("XD R2 SG0 SG1", 512, "bfloat16")
+_b("N1S N0 C1 C2 EQS DGH DGL EV Q NEGM POSM XS", 256, "bfloat16")
+_b("R2 SG0 SG1 NG ZR", 512, "bfloat16")
 _b("N1F MASK M256 CS TR UU UX", 256)
-_b("IC", 208)
+_b("CAG", 272)
 _b("ON160 W1 T1", 160)
 _b("RKM", 176)
 _b("CO", 64)
-_b("TH W2 VF NL0 NL1 DUMP DG2 T14 T6 LF LG PM Z1 Z2 Z3 PW", 16)
+_b("TH W2 VF NL0 NL1 DUMP DG2 T14 T6 PM Z1 Z2 Z3 PW", 16)
 _b("CSg TRg UUg", 64)
 _b("PI YI HI", 16, "int32")
 _b("AN LOI HII SHI PLI DI DM", 160, "int32")
@@ -55,26 +59,26 @@ _b("HM P2H P2B P4H P4B BT", 160, "bfloat16")
 _b("RS DH DLO", 176, "bfloat16")
 _b("B16v C16v INV JJ MT RF RFg", 16, "bfloat16")
 _b("RR", 32, "bfloat16")
-_b("Qg EVg", 64, "bfloat16")
+_b("Qg EVg NONE XG", 64, "bfloat16")
 _b("GD", 768, "bfloat16")
-_b("XGE CMg GSW", 1024, "bfloat16")
+_b("XGE CMg", 1024, "bfloat16")
 _b("EQg", 160, "bfloat16")
-_b("IDL", 208, "uint16")
 _b("PL P1L P2L P4L DL", 160, "uint16")
-_b("BL CL DNL VL POSE POSS DGN", 16, "uint16")
-_b("POSG", 32, "uint16")
-_b("SL CgL CRUg REPX", 64, "uint16")
+_b("BL CL DNL VL POSE POSS POSG NL", 16, "uint16")
+_b("SL CgL CRUg NGU", 64, "uint16")
 _b("CAN CRU", 256, "uint16")
 _b("OUT", 320)
 for _t in range(RO):
-    _b("GR%d" % _t, 128, "bfloat16")
+    _b("GR%d" % _t, 64, "bfloat16")
+    _b("GX%d" % _t, 272, "bfloat16")
+    _b("GN%d" % _t, 16, "uint16")
     if _t < RO - 1:
         _b("LA%d" % _t, 768, "bfloat16")
 
-SEMAPHORES = ["cv", "cs", "cp", "cg"] + ["d%d" % k for k in range(60)] + \
-    ["%s%d" % (k, t) for k in ("ga", "gl", "ua", "ul") for t in range(RO)]
+SEMAPHORES = ["cv", "cs", "cp", "cg"] + ["d%d" % k for k in range(70)] + \
+    ["%s%d" % (k, t) for k in ("ga", "gl", "GRa", "GRl", "GXa", "GXl", "GNa", "GNl") for t in range(RO)]
 
-CYC, PE, GAT, SCA, WAKE, LOCAL, RATE, REMOTE = 0.00083, 0.00055, 1.4, 3.0, 0.15, 2.0, 200e3, 3.0
+CYC, PE, GAT, SCA, WAKE, LOCAL, RATE, REMOTE, SWEEPS = 0.00083, 0.00042, 1.4, 3.0, 0.15, 2.0, 200e3, 3.0, 2
 
 
 def rank_program(g, core, T, topo):
@@ -99,8 +103,8 @@ def rank_program(g, core, T, topo):
     def half(name, h, hi):
         return (T[name][64 * h:64 * h + 64, :], name, 0, hi, 1, 0, h, hi, 2, 64)
 
-    def hbm(name):
-        return (T[name][:], name, 0, 1, 1, 0, None, 1, 0, 0)
+    def hbm(name, lo=None, hi=None):
+        return (T[name][:] if lo is None else T[name][:, lo:hi], name, lo or 0, hi or 1, 1, 0, None, 1, 0, 0)
 
     def ind(win, off):
         return (win[0].indirect(off[0]), [win, off], 16 * off[7])
@@ -183,11 +187,12 @@ def rank_program(g, core, T, topo):
             kw["scale"] = ap(scale)
         op("s", lambda: S.activation(o[0], a[0], f, **kw), flat(a, bias, scale), [o], vc(o, a, w=1))
 
-    def mm(o, pairs, start=True, stop=True, outs=None):
+    def mm(o, pairs, start=True, stop=True, outs=None, each=None):
         def call():
             i = None
             for k, (l, x) in enumerate(pairs):
-                i = P.matmul((outs[k] if outs else o)[0], l[0], x[0], start and k == 0, stop and k == len(pairs) - 1)
+                i = P.matmul((outs[k] if outs else o)[0], l[0], x[0], start and k % (each or 999) == 0,
+                             stop and (k + 1) % (each or len(pairs)) == 0)
             return i
         op("p", call, [z for l, x in pairs for z in (l, x)], [o], sum(max(64, x[7]) * (x[8] * x[8] // 4) for l, x in pairs) * PE)
 
@@ -199,7 +204,7 @@ def rank_program(g, core, T, topo):
 
     def dma(q, o, a):
         x = o if o[9] else a
-        return op(q, lambda: QU[q].dma_start(o[0], a[0]), [a], [o], LOCAL + x[7] * x[8] * x[9] / RATE, "local", hold=0.05)
+        op(q, lambda: QU[q].dma_start(o[0], a[0]), [a], [o], LOCAL + x[7] * x[8] * x[9] / RATE, "local", hold=0.05)
 
     def iota(o, pat, base=0, cm=0):
         kw = {} if o[1] == "PI" else {"allow_small_or_imprecise_dtypes": True}
@@ -211,6 +216,14 @@ def rank_program(g, core, T, topo):
     def send(call, src, dst, left, landed, n, time):
         s = op("g", call, [src], [], time, (left, n), hold=0.5)
         op(None, None, [], [dst], time, (landed, n), after=[s])
+
+    def visit(t, src, name, time):
+        dst = T.cores[(rank + 1 + t % 3) % N]
+        rid, pid, _ = topo.addr(dst)
+        mask = sum(1 << e for e in topo.engines(core, dst)[:8])
+        out = r("%s%d" % (name, t), 0, src[7])
+        send(lambda: G.remote_dma(out_ap=out[0], in_ap=src[0], remote_sem=T.sem["%sa%d" % (name, t)], local_sem=T.sem["%sl%d" % (name, t)],
+                                  pid=pid, routing_id=rid, dma_engine_mask=mask), src, out, "%sl%d" % (name, t), "%sa%d" % (name, t), 8, time)
 
     def sel(dst, rows, val):
         for k, row in enumerate(rows):
@@ -227,12 +240,13 @@ def rank_program(g, core, T, topo):
                 act(x, y, F.Identity, scale=s)
 
     dma("y", r("OF"), hbm("of0"))
-    dma("s", r("AN"), hbm("an0"))
-    dma("s", r("SNDI"), hbm("snd"))
-    dma("y", r("WK"), hbm("wk"))
+    dma("y", r("AN"), hbm("an0"))
+    dma("y", r("SNDI"), hbm("snd"))
+    for n, x, w, k in (("X", "x", 2560, 1280), ("S", "s0", 4096, 1024), ("WK", "wk", 4096, 1024)):
+        for c in range(0, w, k):
+            dma("y", r(n, c, c + k), hbm(x, c, c + k))
     iota(r("PI", 0, 2), [[0, 2]], 0, 1)
     iota(r("M16"), [[0, 8], [1, 16]])
-    iota(r("IC"), [[1, 208]])
     ms(r("ONE"), 1.0)
     gsel(r("B16"), r("ONE"), [[-16, 8], [0, 16]], 0, 1)
     gsel(r("B16"), r("B16"), [[16, 8], [0, 16]], 15, -1)
@@ -240,16 +254,20 @@ def rank_program(g, core, T, topo):
     iota(half("R2", 1, 512), [[0, 32], [1, 16]])
     iota(r("M256"), [[0, 16], [1, 16]])
     iota(r("N1F"), [[1, 256]], 1)
+    iota(r("N0"), [[1, 256]])
     iota(r("NL0"), [[16, 16]])
-    for n in ("B1", "DR", "B0"):
-        for c in range(0, T[n].shape[1], 512):
-            iota(r(n, c, c + 512), [[0, 512]])
+    for n, w in (("B0", 16 * (160 - CH[0][1])), ("DR", 2560)):
+        for c in range(0, w, 640):
+            iota(r(n, c, min(w, c + 640)), [[0, min(w, c + 640) - c]])
     for k, m in enumerate((15, 31, 3)):
         ts(r("YI", k, k + 1), r("PI", 0, 1), m, None, O.bitwise_and)
     cp(r("CO", 0, 3), r("YI", 0, 3))
-    for c in range(0, NW, 1120):
-        ms(r("WP", c, min(NW, c + 1120)), 0.0)
-    ms(r("ST"), 0.0)
+    ms(r("ZR"), 0.0)
+    for c in range(0, NW, 512):
+        act(r("WP", c, min(NW, c + 512)), r("ZR", 0, min(NW, c + 512) - c))
+    ms(r("ST", 208, 672, 224), 0.0)
+    for k in (3, 4, 5):
+        ms(r("ST", 224 * k + 160, 224 * k + 209), 0.0)
     for c in range(0, 2048, 1024):
         ms(r("CNT", c, c + 1024), 0.0)
     for q in range(8):
@@ -273,7 +291,7 @@ def rank_program(g, core, T, topo):
     for n, s in (("IDU", U), ("IM1", -1.0), ("I7", 7.0), ("IM2K", -2048.0), ("IDB", 0.125), ("IDN", -0.125), ("I768", 768.0),
                  ("I8K", 8192.0), ("IDF", 1.0)):
         act(r(n), r("ID"), F.Identity, scale=s)
-    for n, s in (("B32", -32 * U), ("B4", 4.0), ("ZER", 0.0)):
+    for n, s in (("B32", -32 * U), ("B4", 2.0 ** 32)):
         act(r(n), r("B16"), F.Identity, scale=s)
     ts(r("LE"), r("M16"), col(0), None, O.is_gt)
     tt(r("LT"), r("LE"), r("B16"), O.mult)
@@ -299,10 +317,10 @@ def rank_program(g, core, T, topo):
     ms(r("ON160"), 1.0)
     ms(r("Z1"), 0.5)
     ms(r("Z2"), 0.0)
-    scan(r("PW"), r("Z1"), r("Z2"), 4.0, O.mult, O.add)
+    scan(r("PW"), r("Z1"), r("Z2"), 2.0 ** 31, O.mult, O.add)
     tt(r("PW"), r("PW"), r("M16b", 0, 16), O.mult)
     red(col(14), r("PW"))
-    ts(r("BW"), r("B16"), col(14), 0.5, O.mult, O.mult)
+    act(r("BW"), r("B16"), F.Identity, scale=col(14))
     ms(half("CR", 0, 128), 0.25)
     ms(half("CR", 1, 128), 1.0 / 64)
     for b in range(8):
@@ -314,14 +332,17 @@ def rank_program(g, core, T, topo):
     ms(col(17), float(F0))
     for c, e in ((18, 32), (19, 40), (20, 0)):
         ts(col(c), col(0), -16384.0, 15 * 16384.0 + 4096.0 + e * U, O.mult, O.add)
-    ts(r("N1S"), r("N1F"), U, None, O.mult)
+    act(r("N1S"), r("N1F"), F.Identity, scale=U)
     ts(r("MASK"), r("M256"), 0.5, None, O.is_gt)
-    ts(r("NEGM"), r("M256"), col(0), -2048.0, O.not_equal, O.mult)
+    ts(r("POSM"), r("M256"), col(0), None, O.is_equal)
+    ts(r("C1"), r("POSM"), col(14), -2.0, O.mult, O.mult)
+    ts(r("C2"), r("M256"), col(0), -2.0 ** 42, O.not_equal, O.mult)
+    tt(r("NEGM"), r("C1"), r("C2"), O.add)
+    ts(r("POSM"), r("POSM"), 16384.0, None, O.mult)
     ts(r("NL0"), r("NL0"), col(0), None, O.add)
     ts(r("NL1"), r("NL0"), 1.0, None, O.add)
     ts(r("DUMP"), r("NL0"), 8192.0, None, O.add)
     ts(r("DG2"), r("NL0"), 256.0 - 1024.0, None, O.add)
-    ts(r("REPX"), r("IC", 0, 64), 2.0, None, O.mult)
     ms(r("TH", 0, 1), 9 * U)
     ms(r("RS", 0, 1), 0.0)
     ms(r("RR", 0, 1), 0.0)
@@ -330,16 +351,16 @@ def rank_program(g, core, T, topo):
     ms(r("DH", 160, 176), 0.0)
     ms(r("DLO", 160, 176), 0.0)
     ms(r("X", 2560, 2576), 0.0)
-    ms(r("CT", 4096, 4112), -2.0 ** 24)
+    ms(r("CAG", 256, 272), -2.0 ** 24)
+    ms(r("NONE"), 256.0)
+    for t in range(RO):
+        ms(r("GX%d" % t, 256, 272), 0.0)
     for n in ("E", "E1", "E2"):
         ms(r(n, 0, F0), 0.0)
     ms(r("Q"), 0.0)
     ms(r("Qg"), 0.0)
     ms(r("Q", 1, 256, 16), -4096.0)
     ms(r("Q", 5, 256, 16), 3328.0)
-    ms(r("GT0"), 0.0)
-    sel(21, (12,), 4096.0)
-    ts(r("GT0", 1, 128, 2), r("GT0", 1, 128, 2), col(21), None, O.add)
     for k in range(3):
         ts(r("OFd", 208 * k, 208 * k + 208), r("OF"), 15 << 4 * k, None, O.bitwise_and)
         cp(r("ST", 224 * k, 224 * k + 208), r("OFd", 208 * k, 208 * k + 208))
@@ -352,15 +373,11 @@ def rank_program(g, core, T, topo):
     ts(r("T1"), r("HII"), 3328, 3344, O.is_lt, O.mult)
     ts(r("HM"), r("HII"), -3328, None, O.add)
     tt(FH, r("T1"), r("HM"), O.add)
-    laid = [dma("ys"[k % 2], rp("WP", row, 16, 0, NW, row), r("ST", 224 * seg, 224 * seg + 209))
-            for k, (row, seg) in enumerate(((0, 0), (4, 1), (8, 2), (3, 4), (6, 4), (5, 5), (2, 3)))]
-    for q, o, n in (("y", r("X", 0, 2560), "x"), ("s", r("S", 0, 4096), "s0")):
-        op(q, lambda q=q, o=o, n=n: QU[q].dma_start(o[0], T[n][:]), [], [o], 2 * LOCAL + o[7] * 256 / RATE, "local", after=laid, hold=0.05)
+    for row, seg in ((0, 0), (4, 1), (8, 2), (3, 4), (6, 4), (5, 5), (2, 3)):
+        dma("y", rp("WP", row, 16, 0, NW, row), r("ST", 224 * seg, 224 * seg + 209))
     ts(r("W1"), r("LOI"), 209, None, O.mult)
     tt(r("PLI"), r("W1"), r("SHI"), O.add)
     cp(r("PL"), r("PLI"))
-    ts(col(22), col(0), 209.0, None, O.mult)
-    ts(r("IDL"), r("IC"), col(22), None, O.add)
     ts(r("SA"), r("SNDI"), 15, None, O.bitwise_and)
     ts(r("SB"), r("SNDI"), 4, None, O.arith_shift_right)
     ts(r("SA"), r("SA"), 160, None, O.mult)
@@ -376,19 +393,21 @@ def rank_program(g, core, T, topo):
             mm(r(K), tv + [(r("IM2K"), r(sg))])
         act(r("CT", 512 * b, 512 * b + 512), r(K), F.Identity, bias=col(48 + b))
 
-    CH = (SC,) + VC
-    BK = dict(zip(CH, ("K0", "K7", "K6")))
+    SC, VC, BK = CH[0][1], CH[1:], ("K0", "K7", "K6")
 
     def fe(n, c0, c1):
         return r(n, F0 + 16 * c0, F0 + 16 * c1)
 
-    def addend(b, src):
+    def addend(b, src, first=False):
         for c0, c1 in VC:
-            dma("y", rp(b, 0, 4, 16 * (c0 - SC[1]), 16 * (c1 - SC[1])), rp(src, 0, 4, F0 + 16 * c0, F0 + 16 * c1))
+            if first:
+                ts(r(b, 16 * (c0 - SC), 16 * (c1 - SC)), fe(src, c0, c1), col(3), None, O.mult)
+            else:
+                dma("y", rp(b, 0, 4, 16 * (c0 - SC), 16 * (c1 - SC)), rp(src, 0, 4, F0 + 16 * c0, F0 + 16 * c1))
 
     def lists(f, src, lst, hi, lo, first):
-        for c in CH:
-            K = r(BK[c], 0, c[1] - c[0])
+        for B, c in zip(BK, CH):
+            K = r(B, 0, c[1] - c[0])
             extra = [] if first else [(r("ID"), r(x[1], x[2] + c[0], x[2] + c[1])) for x in (hi, lo)]
             mm(K, extra + fam(f, src, *c, F0))
             cp(r(lst, *c), K)
@@ -396,98 +415,112 @@ def rank_program(g, core, T, topo):
                 cp(r(hi[1], *c), K)
                 tt(r(lo[1], *c), K, r(hi[1], *c), O.subtract)
 
-    def shared(win, lst, src, o, sign, out, f, bias=None):
-        for j, K in enumerate(("K1", "K2")):
-            act(r("GT", 512 * j, 512 * j + 512), ind(win, r(lst, 32 * j, 32 * j + 32)))
-        for j, K in enumerate(("K1", "K2")):
-            mm(r(K), [(r(sign[0]), r(src, o + 512 * j, o + 512 * j + 512))], stop=False)
-            mm(r(K), [(r(sign[1]), r("GT", 512 * j, 512 * j + 512))], start=False)
-            act(r(out, o + 512 * j, o + 512 * j + 512), r(K), f, bias=bias)
+    def shared(n, win, lst, src, o, sign, out, f, bias=None):
+        for j, K in enumerate(("K1", "K2", "K1")[:(n + 31) // 32]):
+            a, b = 512 * j, min(16 * n, 512 * j + 512)
+            act(r("GT", a, b), ind(win, r(lst, a // 16, b // 16)))
+            mm(r(K, 0, b - a), [(r(sign[0]), r(src, o + a, o + b))], stop=False)
+            mm(r(K, 0, b - a), [(r(sign[1]), r("GT", a, b))], start=False)
+            act(r(out, o + a, o + b), r(K, 0, b - a), f, bias=bias)
 
-    def level(win, lst, b, out):
+    def level(win, lst, own, b, o, out):
         W = r(win, 0, NW)
-        shared(W, lst, win, F0, ("IDM", "ID"), out, F.Copy)
+        shared(SC, W, lst, own, F0, ("IDM", "ID"), out, F.Copy)
         for c0, c1 in VC:
-            tt(fe(out, c0, c1), ind(W, r(lst, c0, c1)), r(b, 16 * (c0 - SC[1]), 16 * (c1 - SC[1])), O.add)
+            tt(fe(out, c0, c1), ind(W, r(lst, c0, c1)), r(b, 16 * c0 + o, 16 * c1 + o), O.add)
 
-    def tl(a, src, m2, o=0, step=1):
+    def tl(a, src, m2, step=1):
         return [(r("%s%d%d" % (a, m2, h)), r(src[1], src[2] + step * h, src[3], 2 * step)) for h in range(2)]
 
     def choose(K, n, tn, un, rf, q, ev, th):
         k = n // 16
-        tr(r(tn), K)
-        scan(r(un), r("MASK", 0, n), r(tn), 0.0, O.mult, O.max)
+        for B, n0, n1 in K:
+            tr(r(tn, n0, n1), r(B, 128 + n0, 128 + n1))
+            scan(r(un, n0, n1), r("MASK", 0, n1 - n0), r(tn, n0, n1), 0.0, O.mult, O.max)
         M = r(un, 15, n, 16)
-        ts(r(rf, 0, k), M, th, 8192.0 if n == 256 else 16384.0, O.is_lt, O.mult)
+        ts(r(rf, 0, k), M, th, 8192.0, O.is_lt, O.mult)
         ts(r("T6", 0, k), M, 1.5 * 2.0 ** 29, 1.5 * 2.0 ** 29, O.add, O.subtract)
         ts(r("T14", 0, k), M, 1.5 * 2.0 ** 37, 1.5 * 2.0 ** 37, O.add, O.subtract)
         tt(r(q, 0, n, 16), M, r("T6", 0, k), O.subtract)
         tt(r(q, 12, n, 16), r("T6", 0, k), r("T14", 0, k), O.subtract)
         tr(r(ev), r(q))
 
-    def settle(n, q, rf, ev, L, cr, eq, xs, inv):
+    def settle(n, q, rf, ev, cr, eq, xs, inv):
         k = n // 16
         for m2 in range(2):
-            mm(r("K5", m2, k, 2), ([(r("I8K"), r("INV", m2, k, 2))] if inv else []) + tl("A", r(rf, 0, k), m2)
+            mm(r("K5", m2, k, 2), ([(r("I8K"), r("INV", m2, k, 2))] if inv else tl("A", r(rf, 0, k), m2)) + tl("A", r(rf, 0, k), m2)
                + tl("A", r(q, 0, n), m2, step=16) + tl("A", r(q, 12, n), m2, step=16))
-        tt(r(L, 0, k), r("K5", 0, k), r("DUMP", 0, k), O.min)
-        mm(r("K5", 256, 256 + n), [(r("BD"), r(ev))])
-        cp(r(cr, 0, n), r("K5", 256, 256 + n))
+        mm(r("K3", 256, 256 + n), [(r("BD"), r(ev))])
+        cp(r(cr, 0, n), r("K3", 256, 256 + n))
         mm(r("K4", 0, n), [(r("ID"), r("NEGM", 0, n))], stop=False)
         o = 0
         for m in range(k):
             w = n - 16 * m
-            ts(r(eq, o, o + w), r(cr, 16 * m, n), r(L, m, m + 1), None, O.is_equal)
+            ts(r(eq, o, o + w), r(cr, 16 * m, n), r("K5", m, m + 1), None, O.is_equal)
             mm(r("K4", 16 * m, 16 * m + 16), [(r("BW"), r(eq, o, o + 16))], start=False, stop=False)
             if w > 16:
                 mm(r("K4", 16 * m + 16, n), [(r("B4"), r(eq, o + 16, o + w))], start=False, stop=False)
             o += w
-        mm(r("K4", 0, n), [(r("ZER"), r("NEGM", 0, n))], start=False)
+        mm(r("K4", 0, n), [(r("ID"), r("POSM", 0, n))], start=False)
         scan(r("UX", 0, n), r("MASK", 0, n), r("K4", 0, n), 0.0, O.mult, O.max)
-        ts(r("Z1", 0, k), r("UX", 15, n, 16), col(14), 16384.0, O.is_ge, O.mult)
-        tt(r("Z2", 0, k), r("Z1", 0, k), r(L, 0, k), O.max)
+        tt(r("Z2", 0, k), r("UX", 15, n, 16), r("K5", 0, k), O.max)
         tt(r("Z3", 0, k), r("Z2", 0, k), r("DUMP", 0, k), O.min)
         ts(r("POSS", 0, k), r("Z3", 0, k), -4096.0, None, O.add)
         cp(ind(r("S"), r("POSS", 0, k)), xs)
 
+    def signs(n, banks, xs, gt, cm, K):
+        per = 512 // n
+        for j, B in enumerate(banks[:(15 + per) // per]):
+            ks = range(per * j, min(16, per * j + per))
+            mm(r(B), [p for k in ks for p in ((r("ID"), xs), (r("IM1"), r(gt, k, 16 * n, 16)))], each=2,
+               outs=[r(B, n * (k - ks[0]), n * (k - ks[0] + 1)) for k in ks for p in range(2)])
+            act(r(cm, n * ks[0], n * ks[-1] + n), r(B, 0, n * len(ks)), F.Sign, bias=col(16))
+            mm(K, [(one("HC", k), r(cm, n * k, n * k + n)) for k in ks], start=False, stop=ks[-1] == 15)
+
     def guests(t):
-        gr = "GR%d" % t
-        mm(r("K3", 64, 68), [(one("FD", i), r(gr, 2 * i + 1, 128, 32)) for i in range(16)])
-        cp(r("DGN", 0, 4), r("K3", 64, 68))
-        cp(r("CgL"), ind(r("CT"), r("DGN", 0, 4)))
-        act(r("XGE"), ind(r(gr), r("REPX")))
-        act(r("CSg"), ind(r("CT"), r("DGN", 0, 4)), F.Identity, bias=col(20))
-        mm(r("K4", 256, 320), [(r("IDF"), r("CSg"))], stop=False)
+        gr, gx = "GR%d" % t, "GX%d" % t
+        act(r("CAG", 0, 256), ind(r("CT"), r("GN%d" % t)))
+        cp(r("NGU"), r(gr))
+        mm(r("K3", 64, 68), fam("FF", gr, 0, 4))
+        ts(r("NL", 0, 4), r("K3", 64, 68), -1.0, None, O.mult)
+        act(r("XGE"), ind(r(gx), r("NGU")))
+        cp(r("CgL"), ind(r("CAG"), r("NL", 0, 4)))
+        act(r("CSg"), ind(r("CAG"), r("NL", 0, 4)), F.Identity, bias=col(20))
+        act(r("XG"), ind(r(gx), r("NL", 0, 4)))
+        mm(r("K3", 128, 192), [(r("IDF"), r("CSg"))], stop=False)
         tt(r("CMg"), ind(r("S", 0, 4096), r("CgL")), r("XGE"), O.is_lt)
-        mm(r("K4", 256, 320), fam("CNT", "CMg", 0, 64), start=False)
-        choose(r("K4", 256, 320), 64, "TRg", "UUg", "RFg", "Qg", "EVg", r("TH", t, t + 1))
-        settle(64, "Qg", "RFg", "EVg", "LG", "CRUg", "EQg", r(gr, 0, 128, 2), False)
+        mm(r("K3", 128, 192), fam("CNT", "CMg", 0, 64), start=False)
+        choose([("K3", 0, 64)], 64, "TRg", "UUg", "RFg", "Qg", "EVg", r("TH", t, t + 1))
+        settle(64, "Qg", "RFg", "EVg", "CRUg", "EQg", r("XG"), False)
 
     for t in range(RO):
         more = t < RO - 1
         if t == 0:
-            ts(r("E", G0, NW), ind(r("WP"), r("IDL", 160, 208)), col(5), None, O.mult)
+            for i in range(16):
+                x, y = r("E", F0 + i, NW, 16), r("WP", 209 * i, 209 * i + 208)
+                if i % 4 == 3:
+                    act(x, y, F.Identity, scale=col(5))
+                else:
+                    ts(x, y, col(5), None, O.mult)
             for n in ("E1", "E2"):
-                dma("y", r(n, G0, NW), r("E", G0, NW))
-            for c0, c1 in ((0, 32), (32, 64)) + VC:
-                act(fe("E", c0, c1), ind(r("WP"), r("IDL", c0, c1)), F.Identity, scale=col(5))
-                tt(fe("E1", c0, c1), ind(r("WP"), r("PL", c0, c1)), fe("E", c0, c1), O.add)
+                cp(r(n, G0, NW), r("E", G0, NW))
+            level("WP", "PL", "E", "E", F0, "E1")
         else:
-            level("E", "P1L", "B0", "E1")
-        addend("B1", "E1")
+            level("E", "P1L", "E", "B0", -16 * SC, "E1")
+        addend("B1", "E1", t == 0)
         lists("FF" if t else "FP", "E1", "P2L", r("P2H"), r("P2B"), t == 0)
-        level("E1", "P2L", "B1", "E2")
+        level("E1", "P2L", "E1", "B1", -16 * SC, "E2")
         lists("FF" if t else "FP", "E2", "P4L", r("P4H"), r("P4B"), t == 0)
         W = r("E2", 0, NW)
-        for c in CH:
-            mm(r(BK[c], 128, 128 + c[1] - c[0]), fam("FD", "E2", *c, F0), stop=False)
-        for j, c in enumerate(CH):
-            (act if j < 2 else cp)(r("G3", 16 * c[0], 16 * c[1]), ind(W, r("P4L", *c)))
-            K = r(BK[c], 128, 128 + c[1] - c[0])
+        for B, c in zip(BK, CD):
+            mm(r(B, 128, 128 + c[1] - c[0]), fam("FD", "E2", *c, F0), stop=False)
+        for B, c, q in zip(BK, CD, C3[t > 0]):
+            (act if q == "s" else cp)(r("G3", 16 * c[0], 16 * c[1]), ind(W, r("P4L", *c)))
+            K = r(B, 128, 128 + c[1] - c[0])
             mm(K, fam("FD", "G3", *c), start=False)
             cp(r("DI", *c), K)
-        ts(r("DM"), r("DI"), 4095, None, O.bitwise_and)
-        cp(r("DL"), r("DM"))
+            ts(r("DM", *c), r("DI", *c), 4095, None, O.bitwise_and)
+            cp(r("DL", *c), r("DM", *c))
         cp(r("DH", 0, 160), r("DM"))
         tt(r("DLO", 0, 160), r("DM"), r("DH", 0, 160), O.subtract)
         if t == 0:
@@ -508,13 +541,13 @@ def rank_program(g, core, T, topo):
             for n in ("E", "E1", "E2"):
                 dma("y", rp(n, 0, 4, G0, NW), rp(la, 0, 4, 0, 768))
         W = r("S", 0, 4096)
-        shared(W, "DL", "X", 0, ("ID", "IM1"), "CM", F.Sign, col(15))
-        for c0, c1 in VC:
+        shared(CC[0][1], W, "DL", "X", 0, ("ID", "IM1"), "CM", F.Sign, col(15))
+        for c0, c1 in CC[1:]:
             tt(r("CM", 16 * c0, 16 * c1), ind(W, r("DL", c0, c1)), r("X", 16 * c0, 16 * c1), O.is_le)
-        for c in CH:
-            K = r(BK[c], 256, 256 + c[1] - c[0])
-            mm(K, fam("HC" if c == SC else "CNT", "CM", *c))
-            ts(r("BT", *c), K, (-3.5 if c == SC else 4.5) * U, None, O.is_lt)
+        for B, c in zip(BK, CC):
+            K = r(B, 256, 256 + c[1] - c[0])
+            mm(K, fam("CNT" if c[0] else "HC", "CM", *c))
+            ts(r("BT", *c), K, (4.5 if c[0] else -3.5) * U, None, O.is_lt)
         scan(r("RS", 1, 161), r("ON160"), r("BT"), 0.0, O.mult, O.add)
         mm(r("K3", 0, 1), [(one("CNT", b), r("RS", 16 * b + 16, 16 * b + 17)) for b in range(10)])
         mm(r("K5", 0, 10), fam("CNT", "RS", 0, 10, 1))
@@ -544,31 +577,27 @@ def rank_program(g, core, T, topo):
         cp(r("VL"), r("K3", 48, 64))
         act(r("VF"), r("K3", 48, 64), F.Identity, bias=col(17))
         ts(r("DNL"), r("K5", 16, 32), 1 / U, None, O.mult)
-        act(r("XD", 0, 256), ind(r("X"), r("VL")))
+        act(r("XS"), ind(r("X"), r("VL")))
         cp(r("CAN"), ind(r("CT"), r("DNL")))
-        mm(r("K1", 0, 256), [(one("CNT", 12), r("DGH")), (one("CNT", 0), r("DGL"))])
-        act(r("XD", 256, 512), r("K1", 0, 256), F.Identity, scale=1 / U)
         mm(r("K0", 0, 16), [(r("IDF"), r("VF")), (r("I768"), r("INV"))], stop=False)
+        visit(t, r("XS"), "GX", 2 * REMOTE)
+        visit(t, r("DNL"), "GN", REMOTE)
         for k in range(16):
-            x, y = r("XE", k, 16 * (256 - NS), 16), r("XD", NS, 256)
-            if k % 5 == 4:
-                gsel(x, y, [[0, 256 - NS]], 1, 0)
-            else:
-                cp(x, y)
-        for j, K in enumerate(("K2", "K3", "K1")):
-            act(r("GT", 512 * j, 512 * j + 512), ind(W, r("CAN", 32 * j, 32 * j + 32)))
-            mm(r(K), [(r("ZER"), r("X", 0, 512))] + [(r("ID"), r("XD", 32 * j, 32 * j + 32))] * 16, stop=False,
-               outs=[r(K)] + [r(K, k, 512, 16) for k in range(16)])
-            mm(r(K), [(r("IM1"), r("GT", 512 * j, 512 * j + 512))], start=False)
-            act(r("CM", 512 * j, 512 * j + 512), r(K), F.Sign, bias=col(16))
+            x, y = r("XE", k, 16 * (256 - NS), 16), r("XS", NS, 256)
+            cp(x, y)
+        act(r("GT", 0, 16 * NS), ind(W, r("CAN", 0, NS)))
         act(r("CS", NS, 256), ind(r("CT"), r("DNL", NS // 16, 16)), F.Identity, bias=col(18))
         act(r("CS", 0, NS), ind(r("CT"), r("DNL", 0, NS // 16)), F.Identity, bias=col(19))
-        for n0, n1 in ((NS, 192), (192, 256)):
+        for B, n0, n1 in CN[:-1]:
             tt(r("CM", 16 * n0, 16 * n1), ind(W, r("CAN", n0, n1)), r("XE", 16 * (n0 - NS), 16 * (n1 - NS)), O.is_lt)
-        for n0, n1 in ((NS, 192), (0, NS), (192, 256)):
-            mm(r("K4", n0, n1), [(r("IDF"), r("CS", n0, n1)), (r("B32"), r("EQS", n0, n1))], stop=False)
-            mm(r("K4", n0, n1), fam("CNT" if n0 else "HC", "CM", n0, n1), start=False)
-        choose(r("K4", 0, 256), 256, "TR", "UU", "RF", "Q", "EV", r("TH", t, t + 1))
+        for B, n0, n1 in CN:
+            K = r(B, 128 + n0, 128 + n1)
+            mm(K, [(r("IDF"), r("CS", n0, n1)), (r("B32"), r("EQS", n0, n1))], stop=False)
+            if n0:
+                mm(K, fam("CNT", "CM", n0, n1), start=False)
+            else:
+                signs(NS, ("K1", "K2", "K3", "K7"), r("XS", 0, NS), "GT", "CM", K)
+        choose(CN, 256, "TR", "UU", "RF", "Q", "EV", r("TH", t, t + 1))
         mm(r("K0", 0, 16), tl("H", r("RF"), 0) + tl("H", r("RF"), 1) + [(r("ID"), r("JJ"))], start=False,
            outs=[r("K0", 0, 16, 2)] * 2 + [r("K0", 1, 16, 2)] * 2 + [r("K0", 0, 16)])
         cp(r("POSE"), r("K0", 0, 16))
@@ -582,66 +611,62 @@ def rank_program(g, core, T, topo):
         a, b = r("RR", 1, 17), r("RR", 0, 16)
         mm(r("K3", 16, 32), [(r("LTS"), a), (r("UBS"), b), (r("IDN"), a), (r("IDB"), b)])
         tt(r("PM"), r("K3", 16, 32), r("DG2"), O.min)
-        ts(r("POSG", 0, 16), r("PM"), 2.0, 2048.0, O.mult, O.add)
-        ts(r("POSG", 16, 32), r("PM"), 2.0, 2049.0, O.mult, O.add)
-        gsel(r("GSW", 0, 128), r("GT0"), [[0, 128]], 1, 0)
-        cp(ind(r("GSW"), r("POSG")), r("XD"))
-        dst = T.cores[(rank + 1 + t % 3) % N]
-        rid, pid, _ = topo.addr(dst)
-        mask = sum(1 << e for e in topo.engines(core, dst)[:8])
-        send(lambda t=t, rid=rid, pid=pid, mask=mask: G.remote_dma(
-            out_ap=T["GR%d" % t][:], in_ap=T.GSW[:, 0:128], remote_sem=T.sem["ua%d" % t], local_sem=T.sem["ul%d" % t],
-            pid=pid, routing_id=rid, dma_engine_mask=mask), r("GSW", 0, 128), r("GR%d" % t), "ul%d" % t, "ua%d" % t, 8, REMOTE)
+        ts(r("POSG"), r("PM"), 1024.0, None, O.add)
+        act(r("NG", 0, 64), r("NONE"))
+        cp(ind(r("NG"), r("POSG")), r("N0"))
+        visit(t, r("NG", 0, 64), "GR", REMOTE)
         if more:
             mm(r("K3", 40, 41), [(r("ONES"), r("RR", 16, 17)), (r("SEL0"), r("MT", 0, 1))])
             cp(r("HI", 0, 1), r("K3", 40, 41))
             ts(r("HI", 1, 2), r("HI", 0, 1), 1, None, O.bitwise_and)
             ts(r("TH", t + 1, t + 2), r("HI", 1, 2), U, 9 * U, O.mult, O.add)
-        settle(256, "Q", "RF", "EV", "LF", "CRU", "EQ", r("XD", 0, 256), True)
-        guests(t)
+        settle(256, "Q", "RF", "EV", "CRU", "EQ", r("XS"), True)
         if t == 0:
             sel(23, (5, 6), 1 / U)
             scaled(r("FP"), r("CNT"), col(23), "s")
-    mm(r("K1", 0, 320), [(one(f, 2 * c + k), r("E", F0 + 320 * c, F0 + 320 * c + 320)) for c in range(8) for k, f in enumerate(("FD", "FP"))])
-    act(r("OUT"), r("K1", 0, 320))
-    dma("s", hbm("yof"), rp("OUT", 0, 2, 0, 320))
-    dma("s", hbm("yan"), rp("OUT", 1, 2, 0, 320))
+        if not more:
+            mm(r("K1", 0, 320), [(one(f, 2 * c + k), r("E", F0 + 320 * c, F0 + 320 * c + 320)) for c in range(8) for k, f in enumerate(("FD", "FP"))])
+            act(r("OUT"), r("K1", 0, 320))
+            dma("y", hbm("yof"), rp("OUT", 0, 2, 0, 320))
+            dma("y", hbm("yan"), rp("OUT", 1, 2, 0, 320))
+        guests(t)
     dma("y", hbm("ys"), r("S", 0, 4096))
 
-    nxt = [[] for c in calls]
+    lead = [LOCAL if c["sem"] == "local" else 0.0 for c in calls]
+    res = ["dma" if c["sem"] == "local" else c["q"] for c in calls]
+    hold = [c["cost"] - LOCAL if c["sem"] == "local" else c["hold"] for c in calls]
+    fwd, bwd = [[] for c in calls], [[] for c in calls]
     for i, c in enumerate(calls):
-        for d in c["deps"]:
-            nxt[d].append(i)
-    for i in range(len(calls) - 1, -1, -1):
-        calls[i]["way"] = calls[i]["cost"] + max([WAKE * calls[j]["deps"][i] + calls[j]["way"] for j in nxt[i]] + [0])
-    free, left, order = dict.fromkeys(list(QU) + [None], 0.0), [len(c["deps"]) for c in calls], []
-    pool = {q: [] for q in free}
+        for d, w in c["deps"].items():
+            lag = (calls[d]["cost"] + WAKE if w else 1e-5 if res[d] != res[i] else hold[d]) - lead[d] + lead[i]
+            fwd[i].append((d, lag))
+            bwd[d].append((i, lag + hold[i] - hold[d]))
 
-    def offer(i):
-        c = calls[i]
-        c["from"] = max([calls[d]["end"] + WAKE if w else calls[d]["at"] for d, w in c["deps"].items()] + [0])
-        pool[c["q"]].append(i)
-    for i in range(len(calls)):
-        if not left[i]:
-            offer(i)
-    while len(order) < len(calls):
-        q = min((q for q in pool if pool[q]), key=lambda q: max(free[q], min(calls[i]["from"] for i in pool[q])))
-        now = max(free[q], min(calls[i]["from"] for i in pool[q]))
-        i = max((i for i in pool[q] if calls[i]["from"] <= now), key=lambda i: calls[i]["way"])
-        j = max((j for j in pool[q] if calls[j]["from"] < now + calls[i]["hold"]), key=lambda j: calls[j]["way"] - calls[j]["from"])
-        if calls[j]["way"] > calls[i]["way"] + calls[j]["from"] - now + calls[j]["hold"]:
-            i = j
-        c = calls[i]
-        pool[q].remove(i)
-        c["at"] = max(now, c["from"])
-        c["end"] = c["at"] + c["cost"]
-        if q:
-            free[q] = c["at"] + c["hold"]
-        order.append(i)
-        for j in nxt[i]:
-            left[j] -= 1
-            if not left[j]:
-                offer(j)
+    def place(turn, before, first):
+        taken, at = {}, [0.0] * len(calls)
+        for i in turn:
+            x, L = max([at[d] + lag for d, lag in before[i]] + [first[i]]), taken.setdefault(res[i], [])
+            k, step = 0, 1024
+            while step:
+                if k + step <= len(L) and L[k + step - 1][1] <= x:
+                    k += step
+                else:
+                    step //= 2
+            while res[i] and k < len(L) and x + hold[i] > L[k][0]:
+                x = max(x, L[k][1])
+                k += 1
+            L.insert(k, (x, x + hold[i]))
+            at[i] = x
+        return at
+    way = [0.0] * len(calls)
+    for i in range(len(calls) - 1, -1, -1):
+        way[i] = max([way[j] + lag - hold[j] + hold[i] for j, lag in bwd[i]] + [hold[i]])
+    every = range(len(calls))
+    at = place(sorted(every, key=lambda i: (-way[i], i)), fwd, lead)
+    for sweep in range(SWEEPS):
+        back = place(sorted(every, key=lambda i: (-at[i] - hold[i], -i)), bwd, [0.0] * len(calls))
+        at = place(sorted(every, key=lambda i: (-back[i] - hold[i], i)), fwd, lead)
+    order = sorted(every, key=lambda i: at[i] - lead[i])
 
     cnt, known, nd = {"cv": 0, "cs": 0, "cp": 0, "cg": 0}, {q: {} for q in QU}, 0
     for i in order:

@@ -4,16 +4,18 @@ from concourse.mybir import AluOpType as O, AxisListType, ActivationFunctionType
 RO = 4
 U = 2.0 ** 18
 F0, G0, NW = 16, 2576, 3344
-CH = ((0, 80), (80, 120), (120, 160))
-CD = ((0, 96), (96, 160))
-C3 = ("sv", "ss")
+CH = ((0, 48), (48, 96), (96, 160))
+LV0 = (("s", 0, 48), ("v", 48, 96), ("s", 96, 128), ("v", 128, 160))
+LV = ((("s", 0, 48), ("v", 48, 96), ("s", 96, 160)),) * 3
+CD = ((0, 80), (80, 160))
+CS_, CV = ((0, 32), (32, 64)), ((64, 112), (112, 160))
 CC = ((0, 64), (64, 112), (112, 160))
 NS = 96
 CN = (("K4", 96, 192), ("K5", 192, 256), ("K6", 0, NS))
 SCRATCH, PACK = {}, {}
 WIDE = {"float32": 4, "bfloat16": 2, "int32": 4, "uint16": 2}
 FILL = dict.fromkeys(WIDE, 0)
-OWN = "AN WK X S OF SNDI WP ST E E1 E2 B0 B1 DR GD NG XS DNL OUT ONE B16 R2 CR DH DLO".split()
+OWN = "AN WK X S OF SNDI WP ST E E1 E2 G1 G2 DR GD NG XS DNL OUT ONE B16 R2 CR DH DLO".split()
 
 
 def _b(names, cols, d="float32", w="sbuf"):
@@ -28,43 +30,44 @@ def _b(names, cols, d="float32", w="sbuf"):
 
 _b("K0 K1 K2 K3 K4 K5 K6 K7", 512, "float32", "psum")
 _b("CNT HC FD FF FP FV", 2048, "bfloat16")
-_b("ONE B16 ID IDM IDU IM1 LT LE M16b I7 IM2K CR B32 BD BW B4 LTS UBS IDB IDN ONES SEL0 I768 I8K "
+_b("ONE B16 ID IDU IM1 LT LE M16b I7 IM2K CR B32 BD BW B4 LTS UBS IDB IDN ONES SEL0 I768 I8K "
    "A00 A01 A10 A11 H00 H01 H10 H11", 128, "bfloat16")
 _b("M16 IDF", 128)
 _b("E", F0 + 4096 + 2560, "bfloat16")
 _b("E1 E2 WP", NW, "bfloat16")
-_b("G3 DR XE", 2560, "bfloat16")
-_b("B0 B1 GT", 1536, "bfloat16")
+_b("G1 G2 G3 DR XE", 2560, "bfloat16")
+_b("GT", 1536, "bfloat16")
 _b("X", 2576, "bfloat16")
 _b("S", 4368, "bfloat16")
 _b("WK CM", 4096, "bfloat16")
 _b("CT", 4096)
 _b("EQ", 2176, "bfloat16")
-_b("ST", 6 * 224, "bfloat16")
-_b("N1S N0 C1 C2 EQS DGH DGL EV Q NEGM POSM XS", 256, "bfloat16")
+_b("ST", 5 * 224, "bfloat16")
+_b("N1S N0 C1 C2 EQS E160 DS EV Q NEGM POSM XS", 256, "bfloat16")
 _b("R2 SG0 SG1 NG ZR", 512, "bfloat16")
 _b("N1F MASK M256 CS TR UU UX", 256)
 _b("CAG", 272)
+_b("CA", 2576)
 _b("ON160 W1 T1", 160)
 _b("RKM", 176)
 _b("CO", 64)
-_b("TH W2 VF NL0 NL1 DUMP DG2 T14 T6 PM Z1 Z2 Z3 PW", 16)
+_b("DG2", 32)
+_b("TH W2 VF NL0 NL1 DUMP T14 T6 PM Z1 Z2 Z3 PW", 16)
 _b("CSg TRg UUg", 64)
 _b("PI YI HI", 16, "int32")
 _b("AN LOI HII SHI PLI DI DM", 160, "int32")
 _b("OF", 208, "int32")
-_b("OFd", 624, "int32")
 _b("SNDI SA SB", 48, "int32")
-_b("HM P2H P2B P4H P4B BT", 160, "bfloat16")
-_b("RS DH DLO", 176, "bfloat16")
-_b("B16v C16v INV JJ MT RF RFg", 16, "bfloat16")
+_b("HM P2H P2B P4H P4B BT DH DLO", 160, "bfloat16")
+_b("RS", 176, "bfloat16")
+_b("B16v C16v Cv INV JJ MT RF RFg", 16, "bfloat16")
 _b("RR", 32, "bfloat16")
 _b("Qg EVg NONE XG", 64, "bfloat16")
 _b("GD", 768, "bfloat16")
 _b("XGE CMg", 1024, "bfloat16")
 _b("EQg", 160, "bfloat16")
 _b("PL P1L P2L P4L DL", 160, "uint16")
-_b("BL CL DNL VL POSE POSS POSG NL", 16, "uint16")
+_b("BL CL DNL VP VL POSE POSS POSG NL", 16, "uint16")
 _b("SL CgL CRUg NGU", 64, "uint16")
 _b("CAN CRU", 256, "uint16")
 _b("OUT", 320)
@@ -75,10 +78,10 @@ for _t in range(RO):
     if _t < RO - 1:
         _b("LA%d" % _t, 768, "bfloat16")
 
-SEMAPHORES = ["cv", "cs", "cp", "cg"] + ["d%d" % k for k in range(70)] + \
+SEMAPHORES = ["cv", "cs", "cp", "cg"] + ["d%d" % k for k in range(110)] + \
     ["%s%d" % (k, t) for k in ("ga", "gl", "GRa", "GRl", "GXa", "GXl", "GNa", "GNl") for t in range(RO)]
 
-CYC, PE, GAT, SCA, WAKE, LOCAL, RATE, REMOTE, SWEEPS = 0.00083, 0.00042, 1.4, 3.0, 0.15, 2.0, 200e3, 3.0, 2
+CYC, PE, GAT, SCA, WAKE, LOCAL, RATE, REMOTE, SWEEPS = 0.00083, 0.00042, 1.4, 3.0, 0.22, 1.2, 200e3, 2.0, 2
 
 
 def rank_program(g, core, T, topo):
@@ -158,14 +161,14 @@ def rank_program(g, core, T, topo):
 
     def tt(o, a, b, f):
         w = 1 if "K" in (a[1][0], b[1][0]) else 2
-        op("v", lambda: V.tensor_tensor(o[0], a[0], b[0], f), flat(a, b), flat(o), vc(o, a, w=w))
+        return op("v", lambda: V.tensor_tensor(o[0], a[0], b[0], f), flat(a, b), flat(o), vc(o, a, w=w))
 
     def ts(o, a, s1, s2, f, f2=None):
         more = () if f2 is None else (f2,)
-        op("v", lambda: V.tensor_scalar(o[0], a[0], ap(s1), ap(s2), f, *more), flat(a, s1, s2), flat(o), vc(o, a))
+        return op("v", lambda: V.tensor_scalar(o[0], a[0], ap(s1), ap(s2), f, *more), flat(a, s1, s2), flat(o), vc(o, a))
 
     def cp(o, a):
-        op("v", lambda: V.tensor_copy(o[0], a[0]), flat(a), flat(o), vc(o, a))
+        return op("v", lambda: V.tensor_copy(o[0], a[0]), flat(a), flat(o), vc(o, a))
 
     def ms(o, v):
         op("v", lambda: V.memset(o[0], v), [], [o], vc(o, o))
@@ -179,13 +182,13 @@ def rank_program(g, core, T, topo):
     def red(o, a):
         op("v", lambda: V.tensor_reduce(o[0], a[0], AxisListType.X, O.add), [a], [o], vc(o, a, w=1))
 
-    def act(o, a, f=F.Copy, bias=None, scale=None):
+    def act(o, a, f=F.Copy, bias=None, scale=None, after=()):
         kw = {}
         if bias is not None:
             kw["bias"] = ap(bias)
         if scale is not None:
             kw["scale"] = ap(scale)
-        op("s", lambda: S.activation(o[0], a[0], f, **kw), flat(a, bias, scale), [o], vc(o, a, w=1))
+        return op("s", lambda: S.activation(o[0], a[0], f, **kw), flat(a, bias, scale), [o], vc(o, a, w=1), after=after)
 
     def mm(o, pairs, start=True, stop=True, outs=None, each=None):
         def call():
@@ -208,10 +211,12 @@ def rank_program(g, core, T, topo):
 
     def iota(o, pat, base=0, cm=0):
         kw = {} if o[1] == "PI" else {"allow_small_or_imprecise_dtypes": True}
-        op("g", lambda: G.iota(o[0], pat, base, cm, **kw), [], [o], 0.13 + 2 * CYC * o[7])
+        c = 0.13 + 2 * CYC * o[7]
+        op("g", lambda: G.iota(o[0], pat, base, cm, **kw), [], [o], c, hold=c + WAKE)
 
     def gsel(o, a, pat, base, cm):
-        op("g", lambda: G.affine_select(o[0], a[0], pat, O.is_ge, 0.0, base, cm), [a], [o], 0.17 + 2 * CYC * o[7])
+        c = 0.17 + 2 * CYC * o[7]
+        op("g", lambda: G.affine_select(o[0], a[0], pat, O.is_ge, 0.0, base, cm), [a], [o], c, hold=c + WAKE)
 
     def send(call, src, dst, left, landed, n, time):
         s = op("g", call, [src], [], time, (left, n), hold=0.5)
@@ -242,9 +247,9 @@ def rank_program(g, core, T, topo):
     dma("y", r("OF"), hbm("of0"))
     dma("y", r("AN"), hbm("an0"))
     dma("y", r("SNDI"), hbm("snd"))
-    for n, x, w, k in (("X", "x", 2560, 1280), ("S", "s0", 4096, 1024), ("WK", "wk", 4096, 1024)):
-        for c in range(0, w, k):
-            dma("y", r(n, c, c + k), hbm(x, c, c + k))
+    for n, x, w in (("X", "x", 2560), ("S", "s0", 4096), ("WK", "wk", 4096)):
+        for c in range(0, w, 512):
+            dma("y", r(n, c, c + 512), hbm(x, c, c + 512))
     iota(r("PI", 0, 2), [[0, 2]], 0, 1)
     iota(r("M16"), [[0, 8], [1, 16]])
     ms(r("ONE"), 1.0)
@@ -256,17 +261,16 @@ def rank_program(g, core, T, topo):
     iota(r("N1F"), [[1, 256]], 1)
     iota(r("N0"), [[1, 256]])
     iota(r("NL0"), [[16, 16]])
-    for n, w in (("B0", 16 * (160 - CH[0][1])), ("DR", 2560)):
-        for c in range(0, w, 640):
-            iota(r(n, c, min(w, c + 640)), [[0, min(w, c + 640) - c]])
+    for c in range(0, 2560, 640):
+        iota(r("DR", c, c + 640), [[0, 640]])
     for k, m in enumerate((15, 31, 3)):
         ts(r("YI", k, k + 1), r("PI", 0, 1), m, None, O.bitwise_and)
     cp(r("CO", 0, 3), r("YI", 0, 3))
     ms(r("ZR"), 0.0)
     for c in range(0, NW, 512):
         act(r("WP", c, min(NW, c + 512)), r("ZR", 0, min(NW, c + 512) - c))
-    ms(r("ST", 208, 672, 224), 0.0)
-    for k in (3, 4, 5):
+    ms(r("ST", 208, 448, 224), 0.0)
+    for k in (2, 3, 4):
         ms(r("ST", 224 * k + 160, 224 * k + 209), 0.0)
     for c in range(0, 2048, 1024):
         ms(r("CNT", c, c + 1024), 0.0)
@@ -275,15 +279,10 @@ def rank_program(g, core, T, topo):
     ts(r("M16b"), r("M16"), col(0), None, O.is_equal)
     tt(r("ID"), r("M16b"), r("B16"), O.mult)
     ts(col(3), col(2), 0.0, None, O.is_equal)
-    ts(r("IDM"), r("ID"), col(3), None, O.mult)
-    sel(4, (2, 3), 1 / U)
-    ts(col(5), col(4), -U, 1.0, O.mult, O.add)
+    sel(4, (1, 3), 1 / U)
     scaled(r("FP"), r("CNT"), col(4))
-    sel(6, (1,), 1.0)
-    tt(col(6), col(6), col(3), O.add)
-    ts(col(6), col(6), 1 / U, None, O.mult)
-    scaled(r("FD"), r("CNT"), col(6), "s")
-    sel(7, (12,), -1 / U)
+    sel(7, (4, 6), -1 / U)
+    sel(5, (4,), 4096.0)
     scaled(r("FF"), r("CNT"), col(7), "s")
     scaled(r("HC"), r("CNT"), 0.5, "s")
     ts(col(8), col(0), 1 / U, None, O.mult)
@@ -342,29 +341,28 @@ def rank_program(g, core, T, topo):
     ts(r("NL0"), r("NL0"), col(0), None, O.add)
     ts(r("NL1"), r("NL0"), 1.0, None, O.add)
     ts(r("DUMP"), r("NL0"), 8192.0, None, O.add)
-    ts(r("DG2"), r("NL0"), 256.0 - 1024.0, None, O.add)
+    ts(r("DG2", 0, 16), r("NL0"), 256.0 - 1024.0, None, O.add)
+    ts(r("DG2", 16, 32), r("NL0"), 4096.0, None, O.add)
     ms(r("TH", 0, 1), 9 * U)
     ms(r("RS", 0, 1), 0.0)
     ms(r("RR", 0, 1), 0.0)
     ms(r("RKM", 160, 176), 0.0)
     ms(r("W2", 10, 16), 1e12)
-    ms(r("DH", 160, 176), 0.0)
-    ms(r("DLO", 160, 176), 0.0)
+    ms(r("CA", 2560, 2576), 0.0)
     ms(r("X", 2560, 2576), 0.0)
     ms(r("CAG", 256, 272), -2.0 ** 24)
     ms(r("NONE"), 256.0)
     for t in range(RO):
         ms(r("GX%d" % t, 256, 272), 0.0)
     for n in ("E", "E1", "E2"):
-        ms(r(n, 0, F0), 0.0)
+        ts(r(n, 0, F0), r("ZR", 0, F0), col(5), None, O.add)
     ms(r("Q"), 0.0)
     ms(r("Qg"), 0.0)
-    ms(r("Q", 1, 256, 16), -4096.0)
+    ms(r("Q", 4, 256, 16), 4096.0)
     ms(r("Q", 5, 256, 16), 3328.0)
-    for k in range(3):
-        ts(r("OFd", 208 * k, 208 * k + 208), r("OF"), 15 << 4 * k, None, O.bitwise_and)
-        cp(r("ST", 224 * k, 224 * k + 208), r("OFd", 208 * k, 208 * k + 208))
-    FH, LO, HI = (r("ST", 224 * k, 224 * k + 160) for k in (3, 4, 5))
+    cp(r("ST", 0, 208), r("OF"))
+    tt(r("ST", 224, 432), r("OF"), r("ST", 0, 208), O.subtract)
+    FH, LO, HI = (r("ST", 224 * k, 224 * k + 160) for k in (2, 3, 4))
     ts(r("LOI"), r("AN"), 15, None, O.bitwise_and)
     ts(r("HII"), r("AN"), 4080, None, O.bitwise_and)
     ts(r("SHI"), r("AN"), 4, None, O.arith_shift_right)
@@ -373,7 +371,7 @@ def rank_program(g, core, T, topo):
     ts(r("T1"), r("HII"), 3328, 3344, O.is_lt, O.mult)
     ts(r("HM"), r("HII"), -3328, None, O.add)
     tt(FH, r("T1"), r("HM"), O.add)
-    for row, seg in ((0, 0), (4, 1), (8, 2), (3, 4), (6, 4), (5, 5), (2, 3)):
+    for row, seg in ((12, 0), (0, 1), (3, 3), (7, 3), (5, 4), (1, 2)):
         dma("y", rp("WP", row, 16, 0, NW, row), r("ST", 224 * seg, 224 * seg + 209))
     ts(r("W1"), r("LOI"), 209, None, O.mult)
     tt(r("PLI"), r("W1"), r("SHI"), O.add)
@@ -393,41 +391,25 @@ def rank_program(g, core, T, topo):
             mm(r(K), tv + [(r("IM2K"), r(sg))])
         act(r("CT", 512 * b, 512 * b + 512), r(K), F.Identity, bias=col(48 + b))
 
-    SC, VC, BK = CH[0][1], CH[1:], ("K0", "K7", "K6")
+    BK = ("K0", "K7", "K6")
 
-    def fe(n, c0, c1):
-        return r(n, F0 + 16 * c0, F0 + 16 * c1)
+    def rows(dst, a, src, b, step, o, pieces):
+        for c0, c1 in pieces:
+            dma("y", rp(dst, a, step, F0 + 16 * c0, F0 + 16 * c1, a), rp(src, b, step, o + 16 * c0, o + 16 * c1))
 
-    def addend(b, src, first=False):
-        for c0, c1 in VC:
-            if first:
-                ts(r(b, 16 * (c0 - SC), 16 * (c1 - SC)), fe(src, c0, c1), col(3), None, O.mult)
-            else:
-                dma("y", rp(b, 0, 4, 16 * (c0 - SC), 16 * (c1 - SC)), rp(src, 0, 4, F0 + 16 * c0, F0 + 16 * c1))
-
-    def lists(f, src, lst, hi, lo, first):
+    def lists(f, src, o, lst, hi, lo, first):
         for B, c in zip(BK, CH):
             K = r(B, 0, c[1] - c[0])
             extra = [] if first else [(r("ID"), r(x[1], x[2] + c[0], x[2] + c[1])) for x in (hi, lo)]
-            mm(K, extra + fam(f, src, *c, F0))
+            mm(K, extra + fam(f, src, *c, o))
             cp(r(lst, *c), K)
             if first:
                 cp(r(hi[1], *c), K)
                 tt(r(lo[1], *c), K, r(hi[1], *c), O.subtract)
 
-    def shared(n, win, lst, src, o, sign, out, f, bias=None):
-        for j, K in enumerate(("K1", "K2", "K1")[:(n + 31) // 32]):
-            a, b = 512 * j, min(16 * n, 512 * j + 512)
-            act(r("GT", a, b), ind(win, r(lst, a // 16, b // 16)))
-            mm(r(K, 0, b - a), [(r(sign[0]), r(src, o + a, o + b))], stop=False)
-            mm(r(K, 0, b - a), [(r(sign[1]), r("GT", a, b))], start=False)
-            act(r(out, o + a, o + b), r(K, 0, b - a), f, bias=bias)
-
-    def level(win, lst, own, b, o, out):
-        W = r(win, 0, NW)
-        shared(SC, W, lst, own, F0, ("IDM", "ID"), out, F.Copy)
-        for c0, c1 in VC:
-            tt(fe(out, c0, c1), ind(W, r(lst, c0, c1)), r(b, 16 * c0 + o, 16 * c1 + o), O.add)
+    def level(win, lst, out, who):
+        for q, c0, c1 in who:
+            (act if q == "s" else cp)(r(out, 16 * c0, 16 * c1), ind(r(win, 0, NW), r(lst, c0, c1)))
 
     def tl(a, src, m2, step=1):
         return [(r("%s%d%d" % (a, m2, h)), r(src[1], src[2] + step * h, src[3], 2 * step)) for h in range(2)]
@@ -438,7 +420,7 @@ def rank_program(g, core, T, topo):
             tr(r(tn, n0, n1), r(B, 128 + n0, 128 + n1))
             scan(r(un, n0, n1), r("MASK", 0, n1 - n0), r(tn, n0, n1), 0.0, O.mult, O.max)
         M = r(un, 15, n, 16)
-        ts(r(rf, 0, k), M, th, 8192.0, O.is_lt, O.mult)
+        ts(r(rf, 0, k), M, th, 8192.0 if n == 256 else 16384.0, O.is_lt, O.mult)
         ts(r("T6", 0, k), M, 1.5 * 2.0 ** 29, 1.5 * 2.0 ** 29, O.add, O.subtract)
         ts(r("T14", 0, k), M, 1.5 * 2.0 ** 37, 1.5 * 2.0 ** 37, O.add, O.subtract)
         tt(r(q, 0, n, 16), M, r("T6", 0, k), O.subtract)
@@ -448,10 +430,10 @@ def rank_program(g, core, T, topo):
     def settle(n, q, rf, ev, cr, eq, xs, inv):
         k = n // 16
         for m2 in range(2):
-            mm(r("K5", m2, k, 2), ([(r("I8K"), r("INV", m2, k, 2))] if inv else tl("A", r(rf, 0, k), m2)) + tl("A", r(rf, 0, k), m2)
+            mm(r("K5", m2, k, 2), ([(r("I8K"), r("INV", m2, k, 2))] if inv else []) + tl("A", r(rf, 0, k), m2)
                + tl("A", r(q, 0, n), m2, step=16) + tl("A", r(q, 12, n), m2, step=16))
-        mm(r("K3", 256, 256 + n), [(r("BD"), r(ev))])
-        cp(r(cr, 0, n), r("K3", 256, 256 + n))
+        mm(r("K2", 256, 256 + n), [(r("BD"), r(ev))])
+        cp(r(cr, 0, n), r("K2", 256, 256 + n))
         mm(r("K4", 0, n), [(r("ID"), r("NEGM", 0, n))], stop=False)
         o = 0
         for m in range(k):
@@ -463,9 +445,15 @@ def rank_program(g, core, T, topo):
             o += w
         mm(r("K4", 0, n), [(r("ID"), r("POSM", 0, n))], start=False)
         scan(r("UX", 0, n), r("MASK", 0, n), r("K4", 0, n), 0.0, O.mult, O.max)
-        tt(r("Z2", 0, k), r("UX", 15, n, 16), r("K5", 0, k), O.max)
-        tt(r("Z3", 0, k), r("Z2", 0, k), r("DUMP", 0, k), O.min)
-        ts(r("POSS", 0, k), r("Z3", 0, k), -4096.0, None, O.add)
+        if inv:
+            tt(r("Z2", 0, k), r("UX", 15, n, 16), r("K5", 0, k), O.max)
+            tt(r("Z3", 0, k), r("Z2", 0, k), r("DUMP", 0, k), O.min)
+            ts(r("POSS", 0, k), r("Z3", 0, k), -4096.0, None, O.add)
+        else:
+            tt(r("Z2", 0, k), r("K5", 0, k), r("DUMP", 0, k), O.min)
+            ts(r("Z3", 0, k), r("Z2", 0, k), -4096.0, None, O.add)
+            for m in range(k):
+                ts(r("POSS", m, m + 1), r("UX", 16 * m + 15, 16 * m + 16), r("DG2", 16 + m, 17 + m), r("Z3", m, m + 1), O.min, O.max)
         cp(ind(r("S"), r("POSS", 0, k)), xs)
 
     def signs(n, banks, xs, gt, cm, K):
@@ -482,7 +470,7 @@ def rank_program(g, core, T, topo):
         act(r("CAG", 0, 256), ind(r("CT"), r("GN%d" % t)))
         cp(r("NGU"), r(gr))
         mm(r("K3", 64, 68), fam("FF", gr, 0, 4))
-        ts(r("NL", 0, 4), r("K3", 64, 68), -1.0, None, O.mult)
+        ts(r("NL", 0, 4), r("K3", 64, 68), -0.5, None, O.mult)
         act(r("XGE"), ind(r(gx), r("NGU")))
         cp(r("CgL"), ind(r("CAG"), r("NL", 0, 4)))
         act(r("CSg"), ind(r("CAG"), r("NL", 0, 4)), F.Identity, bias=col(20))
@@ -497,38 +485,40 @@ def rank_program(g, core, T, topo):
         more = t < RO - 1
         if t == 0:
             for i in range(16):
-                x, y = r("E", F0 + i, NW, 16), r("WP", 209 * i, 209 * i + 208)
-                if i % 4 == 3:
-                    act(x, y, F.Identity, scale=col(5))
-                else:
-                    ts(x, y, col(5), None, O.mult)
-            for n in ("E1", "E2"):
-                cp(r(n, G0, NW), r("E", G0, NW))
-            level("WP", "PL", "E", "E", F0, "E1")
-        else:
-            level("E", "P1L", "E", "B0", -16 * SC, "E1")
-        addend("B1", "E1", t == 0)
-        lists("FF" if t else "FP", "E1", "P2L", r("P2H"), r("P2B"), t == 0)
-        level("E1", "P2L", "E1", "B1", -16 * SC, "E2")
-        lists("FF" if t else "FP", "E2", "P4L", r("P4H"), r("P4B"), t == 0)
-        W = r("E2", 0, NW)
+                ts(r("E1", F0 + i, NW, 16), r("WP", 209 * i, 209 * i + 208), col(3), None, O.mult)
+            for i in range(16):
+                cp(r("E", F0 + i, NW, 16), r("WP", 209 * i, 209 * i + 208))
+            scaled(r("E2", F0, NW), r("E", F0, NW), col(3), "s")
+        who = LV if t else (LV0,) * 3
+        level("E" if t else "WP", "P1L" if t else "PL", "G1", who[0])
+        rows("E1", 2, "G1", 0, 4, 0, CH)
+        if t == 0:
+            for row in (1, 3):
+                rows("E1", row, "G1", row, 16, 0, ((0, 96), (96, 160)))
+        rows("E2", 2, "G1", 0, 4, 0, ((0, 160),))
+        lists("FF" if t else "FP", "G1", 0, "P2L", r("P2H"), r("P2B"), t == 0)
+        level("E1", "P2L", "G2", who[1])
+        rows("E2", 1, "G2", 0, 2, 0, CH)
+        lists("FF" if t else "FP", "G2", 0, "P4L", r("P4H"), r("P4B"), t == 0)
         for B, c in zip(BK, CD):
-            mm(r(B, 128, 128 + c[1] - c[0]), fam("FD", "E2", *c, F0), stop=False)
-        for B, c, q in zip(BK, CD, C3[t > 0]):
-            (act if q == "s" else cp)(r("G3", 16 * c[0], 16 * c[1]), ind(W, r("P4L", *c)))
+            mm(r(B, 128, 128 + c[1] - c[0]), fam("CNT", "E2", *c, F0), stop=False)
+        level("E2", "P4L", "G3", who[2])
+        for B, c in zip(BK, CD):
             K = r(B, 128, 128 + c[1] - c[0])
-            mm(K, fam("FD", "G3", *c), start=False)
-            cp(r("DI", *c), K)
+            mm(K, fam("CNT", "G3", *c), start=False)
+            ts(r("DI", *c), K, 1 / U, None, O.mult)
             ts(r("DM", *c), r("DI", *c), 4095, None, O.bitwise_and)
             cp(r("DL", *c), r("DM", *c))
-        cp(r("DH", 0, 160), r("DM"))
-        tt(r("DLO", 0, 160), r("DM"), r("DH", 0, 160), O.subtract)
+        cp(r("DH"), r("DM"))
+        tt(r("DLO"), r("DM"), r("DH"), O.subtract)
         if t == 0:
             for b in range(8):
                 ctab(b)
+        dma("y", rp("DR", 12, 16, 0, 2560, 12), r("DH"))
+        dma("y", rp("DR", 0, 16, 0, 2560, 0), r("DLO"))
+        for c in range(0, 160, 32):
+            act(r("CA", 16 * c, 16 * c + 512), ind(r("CT"), r("DL", c, c + 32)))
         if more:
-            dma("y", rp("DR", 12, 16, 0, 2560, 12), r("DH", 0, 160))
-            dma("y", rp("DR", 0, 16, 0, 2560, 0), r("DLO", 0, 160))
             act(r("GD"), ind(r("DR"), r("SL", 0, 48)))
             la, tls = "LA%d" % t, []
             for d in range(1, N):
@@ -541,8 +531,13 @@ def rank_program(g, core, T, topo):
             for n in ("E", "E1", "E2"):
                 dma("y", rp(n, 0, 4, G0, NW), rp(la, 0, 4, 0, 768))
         W = r("S", 0, 4096)
-        shared(CC[0][1], W, "DL", "X", 0, ("ID", "IM1"), "CM", F.Sign, col(15))
-        for c0, c1 in CC[1:]:
+        for j, (K, (c0, c1)) in enumerate(zip(("K1", "K2"), CS_)):
+            gt, K = r("GT", 512 * j, 512 * j + 16 * (c1 - c0)), r(K, 0, 16 * (c1 - c0))
+            act(gt, ind(W, r("DL", c0, c1)))
+            mm(K, [(r("ID"), r("X", 16 * c0, 16 * c1))], stop=False)
+            mm(K, [(r("IM1"), gt)], start=False)
+            act(r("CM", 16 * c0, 16 * c1), K, F.Sign, bias=col(15))
+        for c0, c1 in CV:
             tt(r("CM", 16 * c0, 16 * c1), ind(W, r("DL", c0, c1)), r("X", 16 * c0, 16 * c1), O.is_le)
         for B, c in zip(BK, CC):
             K = r(B, 256, 256 + c[1] - c[0])
@@ -569,25 +564,27 @@ def rank_program(g, core, T, topo):
         ts(r("CL"), r("K3", 32, 48), 1 / U, None, O.mult)
         ts(r("C16v"), r("K3", 32, 48), 16 / U, None, O.mult)
         tt(r("EQS"), ind(r("RKM"), r("CL")), r("N1F"), O.is_equal)
-        tt(r("DGH"), ind(r("DH"), r("CL")), r("EQS"), O.mult)
-        tt(r("DGL"), ind(r("DLO"), r("CL")), r("EQS"), O.mult)
+        ts(r("Cv"), r("K3", 32, 48), 1 / U, None, O.mult)
         mm(r("K3", 48, 64), [(r("ID"), r("C16v"))] + fam("FV", "EQS", 0, 16))
-        mm(r("K5", 16, 32), fam("CNT", "DGH", 0, 16), stop=False)
-        mm(r("K5", 16, 32), fam("CNT", "DGL", 0, 16), start=False)
         cp(r("VL"), r("K3", 48, 64))
         act(r("VF"), r("K3", 48, 64), F.Identity, bias=col(17))
-        ts(r("DNL"), r("K5", 16, 32), 1 / U, None, O.mult)
         act(r("XS"), ind(r("X"), r("VL")))
-        cp(r("CAN"), ind(r("CT"), r("DNL")))
+        cp(r("CAN", 0, NS), ind(r("CA"), r("VL", 0, NS // 16)))
+        cp(r("CAN", NS, 256), ind(r("CA"), r("VL", NS // 16, 16)))
+        act(r("E160"), r("EQS"), F.Identity, scale=160.0)
+        mm(r("K7", 0, 16), [(r("ID"), r("Cv"))] + fam("FV", "E160", 0, 16))
+        cp(r("VP"), r("K7", 0, 16))
+        act(r("DS"), ind(r("DR"), r("VP")))
+        mm(r("K7", 16, 32), fam("CNT", "DS", 0, 16))
+        ts(r("DNL"), r("K7", 16, 32), 1 / U, None, O.mult)
         mm(r("K0", 0, 16), [(r("IDF"), r("VF")), (r("I768"), r("INV"))], stop=False)
         visit(t, r("XS"), "GX", 2 * REMOTE)
         visit(t, r("DNL"), "GN", REMOTE)
         for k in range(16):
-            x, y = r("XE", k, 16 * (256 - NS), 16), r("XS", NS, 256)
-            cp(x, y)
+            cp(r("XE", k, 16 * (256 - NS), 16), r("XS", NS, 256))
         act(r("GT", 0, 16 * NS), ind(W, r("CAN", 0, NS)))
-        act(r("CS", NS, 256), ind(r("CT"), r("DNL", NS // 16, 16)), F.Identity, bias=col(18))
-        act(r("CS", 0, NS), ind(r("CT"), r("DNL", 0, NS // 16)), F.Identity, bias=col(19))
+        act(r("CS", NS, 256), ind(r("CA"), r("VL", NS // 16, 16)), F.Identity, bias=col(18))
+        act(r("CS", 0, NS), ind(r("CA"), r("VL", 0, NS // 16)), F.Identity, bias=col(19))
         for B, n0, n1 in CN[:-1]:
             tt(r("CM", 16 * n0, 16 * n1), ind(W, r("CAN", n0, n1)), r("XE", 16 * (n0 - NS), 16 * (n1 - NS)), O.is_lt)
         for B, n0, n1 in CN:
@@ -596,34 +593,38 @@ def rank_program(g, core, T, topo):
             if n0:
                 mm(K, fam("CNT", "CM", n0, n1), start=False)
             else:
-                signs(NS, ("K1", "K2", "K3", "K7"), r("XS", 0, NS), "GT", "CM", K)
+                signs(NS, ("K1", "K2", "K3", "K1"), r("XS", 0, NS), "GT", "CM", K)
         choose(CN, 256, "TR", "UU", "RF", "Q", "EV", r("TH", t, t + 1))
         mm(r("K0", 0, 16), tl("H", r("RF"), 0) + tl("H", r("RF"), 1) + [(r("ID"), r("JJ"))], start=False,
            outs=[r("K0", 0, 16, 2)] * 2 + [r("K0", 1, 16, 2)] * 2 + [r("K0", 0, 16)])
         cp(r("POSE"), r("K0", 0, 16))
         cp(ind(r("E"), r("POSE")), r("EV"))
         if more:
-            addend("B0", "E")
-            lists("FF", "E", "P1L", FH, LO, False)
+            for n in ("E1", "E2"):
+                rows(n, 0, "E", 0, 4, F0, ((0, 160),))
+            lists("FF", "E", F0, "P1L", FH, LO, False)
         for m2 in range(2):
             mm(r("K3", m2, 16, 2), tl("A", r("RF"), m2))
         scan(r("RR", 1, 17), r("ON160", 0, 16), r("K3", 0, 16), 0.0, O.mult, O.add)
         a, b = r("RR", 1, 17), r("RR", 0, 16)
         mm(r("K3", 16, 32), [(r("LTS"), a), (r("UBS"), b), (r("IDN"), a), (r("IDB"), b)])
-        tt(r("PM"), r("K3", 16, 32), r("DG2"), O.min)
+        tt(r("PM"), r("K3", 16, 32), r("DG2", 0, 16), O.min)
         ts(r("POSG"), r("PM"), 1024.0, None, O.add)
         act(r("NG", 0, 64), r("NONE"))
         cp(ind(r("NG"), r("POSG")), r("N0"))
         visit(t, r("NG", 0, 64), "GR", REMOTE)
         if more:
-            mm(r("K3", 40, 41), [(r("ONES"), r("RR", 16, 17)), (r("SEL0"), r("MT", 0, 1))])
-            cp(r("HI", 0, 1), r("K3", 40, 41))
+            mm(r("K1", 40, 41), [(r("ONES"), r("RR", 16, 17)), (r("SEL0"), r("MT", 0, 1))])
+            cp(r("HI", 0, 1), r("K1", 40, 41))
             ts(r("HI", 1, 2), r("HI", 0, 1), 1, None, O.bitwise_and)
             ts(r("TH", t + 1, t + 2), r("HI", 1, 2), U, 9 * U, O.mult, O.add)
         settle(256, "Q", "RF", "EV", "CRU", "EQ", r("XS"), True)
         if t == 0:
-            sel(23, (5, 6), 1 / U)
+            sel(23, (5, 7), 1 / U)
             scaled(r("FP"), r("CNT"), col(23), "s")
+            ts(col(6), col(5), -1 / 4096, col(10), O.mult, O.add)
+            ts(col(6), col(6), 1 / U, None, O.mult)
+            scaled(r("FD"), r("CNT"), col(6), "s")
         if not more:
             mm(r("K1", 0, 320), [(one(f, 2 * c + k), r("E", F0 + 320 * c, F0 + 320 * c + 320)) for c in range(8) for k, f in enumerate(("FD", "FP"))])
             act(r("OUT"), r("K1", 0, 320))

@@ -1,12 +1,16 @@
 from concourse.bass import DstId, RemoteDMATransfer
-from concourse.mybir import AluOpType as O, AxisListType, ActivationFunctionType as F
+from concourse.mybir import AluOpType as O, ActivationFunctionType as F
 
 RO = 4
+LN2 = 0.6931471805599453
 U = 2.0 ** 18
 F0, G0, NW = 16, 2576, 3344
-CH = ((0, 48), (48, 96), (96, 160))
-LV0 = (("s", 0, 48), ("v", 48, 96), ("s", 96, 128), ("v", 128, 160))
-LV = ((("s", 0, 48), ("v", 48, 96), ("s", 96, 160)),) * 3
+CH = ((0, 96), (96, 160))
+MERGE = (("s", 0, 32, "s"), ("s", 32, 64, "v"), ("v", 64, 96, "v"), ("s", 96, 128, "v"), ("v", 128, 160, "s"))
+LV0 = (MERGE, MERGE, (("s", 0, 48, ""), ("v", 48, 96, ""), ("s", 96, 128, ""), ("v", 128, 160, "")))
+PLAIN = (("s", 0, 48, ""), ("v", 48, 64, ""), ("v", 64, 80, ""), ("v", 80, 96, ""), ("s", 96, 160, ""))
+LV = (PLAIN,) * 3
+MOVES = {48: 0, 96: 48, 160: 96}
 CD = ((0, 80), (80, 160))
 CS_, CV = ((0, 32), (32, 64)), ((64, 112), (112, 160))
 CC = ((0, 64), (64, 112), (112, 160))
@@ -15,7 +19,7 @@ CN = (("K4", 96, 192), ("K5", 192, 256), ("K6", 0, NS))
 SCRATCH, PACK = {}, {}
 WIDE = {"float32": 4, "bfloat16": 2, "int32": 4, "uint16": 2}
 FILL = dict.fromkeys(WIDE, 0)
-OWN = "AN WK X S OF SNDI WP ST E E1 E2 G1 G2 DR GD NG XS DNL OUT ONE B16 R2 CR DH DLO".split()
+OWN = "AN WK X S OF SNDI WP ST E E1 E2 G1 G2 DR GD NG XS DNL OUT ONE B16 R2 CR DH DLO EN".split()
 
 
 def _b(names, cols, d="float32", w="sbuf"):
@@ -29,10 +33,12 @@ def _b(names, cols, d="float32", w="sbuf"):
 
 
 _b("K0 K1 K2 K3 K4 K5 K6 K7", 512, "float32", "psum")
-_b("CNT HC FD FF FP FV", 2048, "bfloat16")
-_b("ONE B16 ID IDU IM1 LT LE M16b I7 IM2K CR B32 BD BW B4 LTS UBS IDB IDN ONES SEL0 I768 I8K "
+_b("CNT HC FD FP FV FW", 2048, "bfloat16")
+_b("ONE B16 ID IM1 LT LE M16b I7 IM2K CR B32 BD BW B4 LTS UBS IDB IDN ONES SEL0 I768 I8K IBG IDM SH1 EV0 SH2 "
    "A00 A01 A10 A11 H00 H01 H10 H11", 128, "bfloat16")
-_b("M16 IDF", 128)
+_b("M16 IDF I160 IM25", 128)
+SCRATCH["C1"] = ("sbuf", [128, 16, 128], "bfloat16")
+SCRATCH["N1B"] = ("sbuf", [128, 16, 16], "bfloat16")
 _b("E", F0 + 4096 + 2560, "bfloat16")
 _b("E1 E2 WP", NW, "bfloat16")
 _b("G1 G2 G3 DR XE", 2560, "bfloat16")
@@ -42,34 +48,36 @@ _b("S", 4368, "bfloat16")
 _b("WK CM", 4096, "bfloat16")
 _b("CT", 4096)
 _b("EQ", 2176, "bfloat16")
-_b("ST", 5 * 224, "bfloat16")
-_b("N1S N0 C1 C2 EQS E160 DS EV Q NEGM POSM XS", 256, "bfloat16")
-_b("R2 SG0 SG1 NG ZR", 512, "bfloat16")
-_b("N1F MASK M256 CS TR UU UX", 256)
+_b("ST", 4 * 224, "bfloat16")
+_b("N0 DS EV2 Q2 CRB EV Q NEGM POSM XS", 256, "bfloat16")
+_b("R2 SG0 SG1 NG ZR EQS", 512, "bfloat16")
+_b("N1F MASK CS TR UU UX", 256)
 _b("CAG", 272)
 _b("CA", 2576)
 _b("ON160 W1 T1", 160)
 _b("RKM", 176)
 _b("CO", 64)
 _b("DG2", 32)
-_b("TH W2 VF NL0 NL1 DUMP T14 T6 PM Z1 Z2 Z3 PW", 16)
+_b("TH VC1 VC2 VF NL0 NL1 DUMP T14 T6 PM Z2 Z3", 16)
 _b("CSg TRg UUg", 64)
 _b("PI YI HI", 16, "int32")
 _b("AN LOI HII SHI PLI DI DM", 160, "int32")
 _b("OF", 208, "int32")
 _b("SNDI SA SB", 48, "int32")
-_b("HM P2H P2B P4H P4B BT DH DLO", 160, "bfloat16")
+_b("HM BT DH DLO", 160, "bfloat16")
 _b("RS", 176, "bfloat16")
-_b("B16v C16v Cv INV JJ MT RF RFg", 16, "bfloat16")
+_b("C32v CB PW2 L96 RFN LB INV JJ MT RF RFg", 16, "bfloat16")
 _b("RR", 32, "bfloat16")
+_b("EN", 8, "bfloat16")
 _b("Qg EVg NONE XG", 64, "bfloat16")
 _b("GD", 768, "bfloat16")
 _b("XGE CMg", 1024, "bfloat16")
 _b("EQg", 160, "bfloat16")
 _b("PL P1L P2L P4L DL", 160, "uint16")
-_b("BL CL DNL VP VL POSE POSS POSG NL", 16, "uint16")
+_b("DNL VP VL POSE POSS POSG NL", 16, "uint16")
+_b("CL", 32, "uint16")
 _b("SL CgL CRUg NGU", 64, "uint16")
-_b("CAN CRU", 256, "uint16")
+_b("CAN", 256, "uint16")
 _b("OUT", 320)
 for _t in range(RO):
     _b("GR%d" % _t, 64, "bfloat16")
@@ -165,7 +173,7 @@ def rank_program(g, core, T, topo):
 
     def ts(o, a, s1, s2, f, f2=None):
         more = () if f2 is None else (f2,)
-        return op("v", lambda: V.tensor_scalar(o[0], a[0], ap(s1), ap(s2), f, *more), flat(a, s1, s2), flat(o), vc(o, a))
+        return op("v", lambda: V.tensor_scalar(o[0], a[0], ap(s1), ap(s2), f, *more), flat(a, s1, s2), flat(o), vc(o, a, *flat(s1, s2)))
 
     def cp(o, a):
         return op("v", lambda: V.tensor_copy(o[0], a[0]), flat(a), flat(o), vc(o, a))
@@ -179,16 +187,16 @@ def rank_program(g, core, T, topo):
     def scan(o, d0, d1, init, f0, f1):
         op("v", lambda: V.tensor_tensor_scan(o[0], d0[0], d1[0], init, f0, f1), [d0, d1], [o], vc(o, d0, d1))
 
-    def red(o, a):
-        op("v", lambda: V.tensor_reduce(o[0], a[0], AxisListType.X, O.add), [a], [o], vc(o, a, w=1))
-
-    def act(o, a, f=F.Copy, bias=None, scale=None, after=()):
+    def act(o, a, f=F.Copy, bias=None, scale=None, after=(), once=0.0):
         kw = {}
         if bias is not None:
             kw["bias"] = ap(bias)
         if scale is not None:
             kw["scale"] = ap(scale)
-        return op("s", lambda: S.activation(o[0], a[0], f, **kw), flat(a, bias, scale), [o], vc(o, a, w=1), after=after)
+        return op("s", lambda: S.activation(o[0], a[0], f, **kw), flat(a, bias, scale), [o], vc(o, a, w=1) + once, after=after)
+
+    def copy(q, o, a):
+        return (act if q == "s" else cp)(o, a)
 
     def mm(o, pairs, start=True, stop=True, outs=None, each=None):
         def call():
@@ -205,14 +213,17 @@ def rank_program(g, core, T, topo):
     def fam(f, src, c0, c1, o=0):
         return [(one(f, i), r(src, o + 16 * c0 + i, o + 16 * c1, 16)) for i in range(16)]
 
-    def dma(q, o, a):
+    def dma(q, o, a, after=()):
         x = o if o[9] else a
-        op(q, lambda: QU[q].dma_start(o[0], a[0]), [a], [o], LOCAL + x[7] * x[8] * x[9] / RATE, "local", hold=0.05)
+        return op(q, lambda: QU[q].dma_start(o[0], a[0]), [a], [o], LOCAL + x[7] * x[8] * x[9] / RATE, "local", after, 0.05)
 
     def iota(o, pat, base=0, cm=0):
         kw = {} if o[1] == "PI" else {"allow_small_or_imprecise_dtypes": True}
         c = 0.13 + 2 * CYC * o[7]
         op("g", lambda: G.iota(o[0], pat, base, cm, **kw), [], [o], c, hold=c + WAKE)
+
+    def fill(o, v):
+        iota(o, [[0, o[7]]], int(v))
 
     def gsel(o, a, pat, base, cm):
         c = 0.17 + 2 * CYC * o[7]
@@ -247,9 +258,10 @@ def rank_program(g, core, T, topo):
     dma("y", r("OF"), hbm("of0"))
     dma("y", r("AN"), hbm("an0"))
     dma("y", r("SNDI"), hbm("snd"))
-    for n, x, w in (("X", "x", 2560), ("S", "s0", 4096), ("WK", "wk", 4096)):
-        for c in range(0, w, 512):
-            dma("y", r(n, c, c + 512), hbm(x, c, c + 512))
+    last = ()
+    for n, x, w in (("WK", "wk", 4096), ("S", "s0", 4096), ("X", "x", 2560)):
+        for c in sorted(range(0, w, 512), key=lambda c: n == "WK" and c < 2048):
+            last = [dma("y", r(n, c, c + 512), hbm(x, c, c + 512), last)]
     iota(r("PI", 0, 2), [[0, 2]], 0, 1)
     iota(r("M16"), [[0, 8], [1, 16]])
     ms(r("ONE"), 1.0)
@@ -257,20 +269,21 @@ def rank_program(g, core, T, topo):
     gsel(r("B16"), r("B16"), [[16, 8], [0, 16]], 15, -1)
     iota(half("R2", 0, 512), [[1, 32], [0, 16]])
     iota(half("R2", 1, 512), [[0, 32], [1, 16]])
-    iota(r("M256"), [[0, 16], [1, 16]])
     iota(r("N1F"), [[1, 256]], 1)
+    n1b = (T.N1B[0:80], "N1B", 0, 256, 1, 0, None, 256, 2, 128)
+    iota((T.N1B[:],) + n1b[1:], [[16, 16], [1, 16]], 1)
     iota(r("N0"), [[1, 256]])
     iota(r("NL0"), [[16, 16]])
     for c in range(0, 2560, 640):
-        iota(r("DR", c, c + 640), [[0, 640]])
-    for k, m in enumerate((15, 31, 3)):
+        fill(r("DR", c, c + 640), 0)
+    for k, m in enumerate((15, 31, 3, 1)):
         ts(r("YI", k, k + 1), r("PI", 0, 1), m, None, O.bitwise_and)
     cp(r("CO", 0, 3), r("YI", 0, 3))
     ms(r("ZR"), 0.0)
     for c in range(0, NW, 512):
         act(r("WP", c, min(NW, c + 512)), r("ZR", 0, min(NW, c + 512) - c))
     ms(r("ST", 208, 448, 224), 0.0)
-    for k in (2, 3, 4):
+    for k in (2, 3):
         ms(r("ST", 224 * k + 160, 224 * k + 209), 0.0)
     for c in range(0, 2048, 1024):
         ms(r("CNT", c, c + 1024), 0.0)
@@ -279,16 +292,27 @@ def rank_program(g, core, T, topo):
     ts(r("M16b"), r("M16"), col(0), None, O.is_equal)
     tt(r("ID"), r("M16b"), r("B16"), O.mult)
     ts(col(3), col(2), 0.0, None, O.is_equal)
-    sel(4, (1, 3), 1 / U)
-    scaled(r("FP"), r("CNT"), col(4))
+    sel(4, (1, 9), 1 / U)
     sel(7, (4, 6), -1 / U)
+    tt(r("CB", 0, 1), col(7), col(4), O.add)
+    scaled(r("FP"), r("CNT"), r("CB", 0, 1))
     sel(5, (4,), 4096.0)
-    scaled(r("FF"), r("CNT"), col(7), "s")
-    scaled(r("HC"), r("CNT"), 0.5, "s")
+    act(r("IDM"), r("ID"), F.Identity, scale=col(3))
+    ts(col(24), col(3), 2.0, col(0), O.mult, O.add)
+    ts(col(25), col(4), U, col(3), O.mult, O.add)
+    ts(r("SH1"), r("M16"), col(24), col(25), O.is_equal, O.mult)
+    tt(r("SH1"), r("SH1"), r("B16"), O.mult)
+    ts(col(26), r("YI", 3, 4), -1.0, 1.0, O.mult, O.add)
+    act(r("EV0"), r("ID"), F.Identity, scale=col(26))
+    ms(r("SH2", 0, 1), 0.0)
+    act(r("SH2", 1, 128), r("EV0", 0, 127))
+    scaled(r("HC"), r("CNT"), 0.5)
     ts(col(8), col(0), 1 / U, None, O.mult)
     scaled(r("FV"), r("CNT"), col(8), "s")
-    for n, s in (("IDU", U), ("IM1", -1.0), ("I7", 7.0), ("IM2K", -2048.0), ("IDB", 0.125), ("IDN", -0.125), ("I768", 768.0),
-                 ("I8K", 8192.0), ("IDF", 1.0)):
+    ts(r("CB", 1, 2), col(8), 16 / U, None, O.add)
+    scaled(r("FW"), r("CNT"), r("CB", 1, 2))
+    for n, s in (("IM1", -1.0), ("I7", 7.0), ("IM2K", -2048.0), ("IDB", 0.125), ("IDN", -0.125), ("I768", 768.0),
+                 ("I8K", 8192.0), ("IBG", -2.0 ** 90), ("IDF", 1.0), ("I160", 160.0), ("IM25", -2559.0)):
         act(r(n), r("ID"), F.Identity, scale=s)
     for n, s in (("B32", -32 * U), ("B4", 2.0 ** 32)):
         act(r(n), r("B16"), F.Identity, scale=s)
@@ -303,75 +327,64 @@ def rank_program(g, core, T, topo):
     act(r("SEL0"), r("ONE"), F.Identity, scale=col(9))
     sel(10, (0, 12), 1.0)
     act(r("BD"), r("B16"), F.Identity, scale=col(10))
-    ts(col(11), col(0), 9.5, None, O.is_lt)
     ts(col(12), col(1), 15.5, None, O.is_lt)
     ts(col(13), col(1), 15.5, None, O.is_gt)
     for a, s in (("A", 1.0), ("H", 0.5)):
-        ms(r(a + "01", 0, 16), 0.0)
-        ms(r(a + "10", 112, 128), 0.0)
+        fill(r(a + "01", 0, 16), 0)
+        fill(r(a + "10", 112, 128), 0)
         ts(r(a + "00"), r("ID"), col(12), s, O.mult, O.mult)
         ts(r(a + "01", 16, 128), r("ID", 0, 112), col(12), s, O.mult, O.mult)
         ts(r(a + "10", 0, 112), r("ID", 16, 128), col(13), s, O.mult, O.mult)
         ts(r(a + "11"), r("ID"), col(13), s, O.mult, O.mult)
-    ms(r("ON160"), 1.0)
-    ms(r("Z1"), 0.5)
-    ms(r("Z2"), 0.0)
-    scan(r("PW"), r("Z1"), r("Z2"), 2.0 ** 31, O.mult, O.add)
-    tt(r("PW"), r("PW"), r("M16b", 0, 16), O.mult)
-    red(col(14), r("PW"))
+    fill(r("ON160"), 1)
+    ms(col(32), 30 * LN2)
+    ms(col(33), -64 * LN2)
+    act(r("CB", 2, 3), col(0), F.Exp, scale=-LN2, bias=col(32), once=1.3)
+    cp(col(14), r("CB", 2, 3))
     act(r("BW"), r("B16"), F.Identity, scale=col(14))
     ms(half("CR", 0, 128), 0.25)
     ms(half("CR", 1, 128), 1.0 / 64)
-    for b in range(8):
-        if b > 3:
-            ms(col(40 + b), 512.0 * b - 4095.5)
-        ms(col(48 + b), 512.0 * b - (2048.0 if b > 3 else 0.0))
+    for b in range(4, 8):
+        ms(col(40 + b), 512.0 * b - 4095.5)
+    iota(r("CO", 48, 56), [[0, 2], [512, 4]])
     ms(col(15), 2.0 ** -112)
     ms(col(16), -2.0 ** -112)
-    ms(col(17), float(F0))
+    fill(col(17), F0)
     for c, e in ((18, 32), (19, 40), (20, 0)):
         ts(col(c), col(0), -16384.0, 15 * 16384.0 + 4096.0 + e * U, O.mult, O.add)
-    act(r("N1S"), r("N1F"), F.Identity, scale=U)
-    ts(r("MASK"), r("M256"), 0.5, None, O.is_gt)
-    ts(r("POSM"), r("M256"), col(0), None, O.is_equal)
-    ts(r("C1"), r("POSM"), col(14), -2.0, O.mult, O.mult)
-    ts(r("C2"), r("M256"), col(0), -2.0 ** 42, O.not_equal, O.mult)
-    tt(r("NEGM"), r("C1"), r("C2"), O.add)
-    ts(r("POSM"), r("POSM"), 16384.0, None, O.mult)
+    ms(col(28), 1.5 * 2.0 ** 23)
+    ms(col(29), -1.5 * 2.0 ** 23 - 1)
+    ms(col(30), -7.5 / 16)
+    ts(col(21), col(14), -2.0, 2.0 ** 40, O.mult, O.add)
+    ms(col(22), -2.0 ** 40)
+    for c in (0, 128):
+        act(r("MASK", c, c + 128), r("M16"), F.Sign)
+        act(r("POSM", c, c + 128), r("M16b"), F.Identity, scale=16384.0)
+        act(r("NEGM", c, c + 128), r("M16b"), F.Identity, scale=col(21), bias=col(22))
     ts(r("NL0"), r("NL0"), col(0), None, O.add)
     ts(r("NL1"), r("NL0"), 1.0, None, O.add)
     ts(r("DUMP"), r("NL0"), 8192.0, None, O.add)
     ts(r("DG2", 0, 16), r("NL0"), 256.0 - 1024.0, None, O.add)
     ts(r("DG2", 16, 32), r("NL0"), 4096.0, None, O.add)
-    ms(r("TH", 0, 1), 9 * U)
-    ms(r("RS", 0, 1), 0.0)
-    ms(r("RR", 0, 1), 0.0)
-    ms(r("RKM", 160, 176), 0.0)
-    ms(r("W2", 10, 16), 1e12)
-    ms(r("CA", 2560, 2576), 0.0)
-    ms(r("X", 2560, 2576), 0.0)
-    ms(r("CAG", 256, 272), -2.0 ** 24)
-    ms(r("NONE"), 256.0)
-    for t in range(RO):
-        ms(r("GX%d" % t, 256, 272), 0.0)
+    fill(r("TH", 0, 1), 9 * U)
+    for x in [r("RS", 0, 1), r("RR", 0, 1), r("RKM", 160, 176), r("CA", 2560, 2576), r("X", 2560, 2576), r("Q"), r("Q2"), r("Qg")] + \
+            [r("GX%d" % t, 256, 272) for t in range(RO)]:
+        fill(x, 0)
+    fill(r("CAG", 256, 272), 1 - 2 ** 24)
+    fill(r("NONE"), 256)
     for n in ("E", "E1", "E2"):
         ts(r(n, 0, F0), r("ZR", 0, F0), col(5), None, O.add)
-    ms(r("Q"), 0.0)
-    ms(r("Qg"), 0.0)
-    ms(r("Q", 4, 256, 16), 4096.0)
-    ms(r("Q", 5, 256, 16), 3328.0)
+    fill(r("Q", 4, 256, 16), 4096)
     cp(r("ST", 0, 208), r("OF"))
     tt(r("ST", 224, 432), r("OF"), r("ST", 0, 208), O.subtract)
-    FH, LO, HI = (r("ST", 224 * k, 224 * k + 160) for k in (2, 3, 4))
     ts(r("LOI"), r("AN"), 15, None, O.bitwise_and)
     ts(r("HII"), r("AN"), 4080, None, O.bitwise_and)
     ts(r("SHI"), r("AN"), 4, None, O.arith_shift_right)
-    cp(LO, r("LOI"))
-    cp(HI, r("HII"))
+    cp(r("ST", 672, 832), r("LOI"))
     ts(r("T1"), r("HII"), 3328, 3344, O.is_lt, O.mult)
     ts(r("HM"), r("HII"), -3328, None, O.add)
-    tt(FH, r("T1"), r("HM"), O.add)
-    for row, seg in ((12, 0), (0, 1), (3, 3), (7, 3), (5, 4), (1, 2)):
+    tt(r("ST", 448, 608), r("T1"), r("HM"), O.add)
+    for row, seg in ((12, 0), (0, 1), (9, 3), (1, 2)):
         dma("y", rp("WP", row, 16, 0, NW, row), r("ST", 224 * seg, 224 * seg + 209))
     ts(r("W1"), r("LOI"), 209, None, O.mult)
     tt(r("PLI"), r("W1"), r("SHI"), O.add)
@@ -393,23 +406,26 @@ def rank_program(g, core, T, topo):
 
     BK = ("K0", "K7", "K6")
 
-    def rows(dst, a, src, b, step, o, pieces):
-        for c0, c1 in pieces:
-            dma("y", rp(dst, a, step, F0 + 16 * c0, F0 + 16 * c1, a), rp(src, b, step, o + 16 * c0, o + 16 * c1))
+    def rows(dst, a, src, b, step, o, c0, c1):
+        dma("y", rp(dst, a, step, F0 + 16 * c0, F0 + 16 * c1, a), rp(src, b, step, o + 16 * c0, o + 16 * c1))
 
-    def lists(f, src, o, lst, hi, lo, first):
+    def lists(src, o, lst):
         for B, c in zip(BK, CH):
             K = r(B, 0, c[1] - c[0])
-            extra = [] if first else [(r("ID"), r(x[1], x[2] + c[0], x[2] + c[1])) for x in (hi, lo)]
-            mm(K, extra + fam(f, src, *c, o))
+            mm(K, fam("FP", src, *c, o))
             cp(r(lst, *c), K)
-            if first:
-                cp(r(hi[1], *c), K)
-                tt(r(lo[1], *c), K, r(hi[1], *c), O.subtract)
 
-    def level(win, lst, out, who):
-        for q, c0, c1 in who:
-            (act if q == "s" else cp)(r(out, 16 * c0, 16 * c1), ind(r(win, 0, NW), r(lst, c0, c1)))
+    def level(win, lst, out, who, nxt=None, own=None, keep=None, shift=None, row=0, step=0):
+        for q, c0, c1, p in who:
+            copy(q, r(out, 16 * c0, 16 * c1), ind(r(win, 0, NW), r(lst, c0, c1)))
+        for k, (q, c0, c1, p) in enumerate(who if nxt else ()):
+            if p:
+                K = r(("K1", "K2", "K3")[k % (3 if who is MERGE else 2)], 0, 16 * (c1 - c0))
+                mm(K, [(r(keep), r(own, F0 + 16 * c0, F0 + 16 * c1))], stop=False)
+                mm(K, [(r(shift), r(out, 16 * c0, 16 * c1))], start=False)
+                copy(p, r(nxt, F0 + 16 * c0, F0 + 16 * c1), K)
+            elif c1 in MOVES:
+                rows(nxt, row, out, 0, step, 0, MOVES[c1], c1)
 
     def tl(a, src, m2, step=1):
         return [(r("%s%d%d" % (a, m2, h)), r(src[1], src[2] + step * h, src[3], 2 * step)) for h in range(2)]
@@ -432,13 +448,24 @@ def rank_program(g, core, T, topo):
         for m2 in range(2):
             mm(r("K5", m2, k, 2), ([(r("I8K"), r("INV", m2, k, 2))] if inv else []) + tl("A", r(rf, 0, k), m2)
                + tl("A", r(q, 0, n), m2, step=16) + tl("A", r(q, 12, n), m2, step=16))
-        mm(r("K2", 256, 256 + n), [(r("BD"), r(ev))])
-        cp(r(cr, 0, n), r("K2", 256, 256 + n))
+        if inv:
+            act(r("PW2"), r(q, 12, n, 16), F.Exp, scale=LN2 / 64, bias=col(33))
+            ts(r("L96"), r(q, 0, n, 16), 96.0, None, O.add)
+            tt(r("Q2", 0, n, 16), r("L96"), r("PW2"), O.mult)
+            tr(r("EV2"), r("Q2"))
+            mm(r("K2", 256, 512), [(r("BD"), r("EV2"))])
+            act(r(cr), r("K2", 256, 512))
+            for m2 in range(2):
+                mm(r("K1", m2, k, 2), [(r("IBG"), r("INV", m2, k, 2))] + tl("A", r("RFN"), m2) + tl("A", r("Q2"), m2, step=16))
+            act(r("LB"), r("K1", 0, k))
+        else:
+            mm(r("K3", 256, 256 + n), [(r("BD"), r(ev))])
+            cp(r(cr, 0, n), r("K3", 256, 256 + n))
         mm(r("K4", 0, n), [(r("ID"), r("NEGM", 0, n))], stop=False)
         o = 0
         for m in range(k):
             w = n - 16 * m
-            ts(r(eq, o, o + w), r(cr, 16 * m, n), r("K5", m, m + 1), None, O.is_equal)
+            ts(r(eq, o, o + w), r(cr, 16 * m, n), r("LB" if inv else "K5", m, m + 1), None, O.is_equal)
             mm(r("K4", 16 * m, 16 * m + 16), [(r("BW"), r(eq, o, o + 16))], start=False, stop=False)
             if w > 16:
                 mm(r("K4", 16 * m + 16, n), [(r("B4"), r(eq, o + 16, o + w))], start=False, stop=False)
@@ -469,8 +496,8 @@ def rank_program(g, core, T, topo):
         gr, gx = "GR%d" % t, "GX%d" % t
         act(r("CAG", 0, 256), ind(r("CT"), r("GN%d" % t)))
         cp(r("NGU"), r(gr))
-        mm(r("K3", 64, 68), fam("FF", gr, 0, 4))
-        ts(r("NL", 0, 4), r("K3", 64, 68), -0.5, None, O.mult)
+        mm(r("K3", 64, 68), fam("CNT", gr, 0, 4))
+        ts(r("NL", 0, 4), r("K3", 64, 68), 1 / (16 * U), None, O.mult)
         act(r("XGE"), ind(r(gx), r("NGU")))
         cp(r("CgL"), ind(r("CAG"), r("NL", 0, 4)))
         act(r("CSg"), ind(r("CAG"), r("NL", 0, 4)), F.Identity, bias=col(20))
@@ -485,21 +512,16 @@ def rank_program(g, core, T, topo):
         more = t < RO - 1
         if t == 0:
             for i in range(16):
-                ts(r("E1", F0 + i, NW, 16), r("WP", 209 * i, 209 * i + 208), col(3), None, O.mult)
-            for i in range(16):
                 cp(r("E", F0 + i, NW, 16), r("WP", 209 * i, 209 * i + 208))
-            scaled(r("E2", F0, NW), r("E", F0, NW), col(3), "s")
-        who = LV if t else (LV0,) * 3
-        level("E" if t else "WP", "P1L" if t else "PL", "G1", who[0])
-        rows("E1", 2, "G1", 0, 4, 0, CH)
-        if t == 0:
-            for row in (1, 3):
-                rows("E1", row, "G1", row, 16, 0, ((0, 96), (96, 160)))
-        rows("E2", 2, "G1", 0, 4, 0, ((0, 160),))
-        lists("FF" if t else "FP", "G1", 0, "P2L", r("P2H"), r("P2B"), t == 0)
-        level("E1", "P2L", "G2", who[1])
-        rows("E2", 1, "G2", 0, 2, 0, CH)
-        lists("FF" if t else "FP", "G2", 0, "P4L", r("P4H"), r("P4B"), t == 0)
+            for n in ("E1", "E2"):
+                cp(r(n, G0, NW), r("E", G0, NW))
+        who = LV if t else LV0
+        level("E" if t else "WP", "P1L" if t else "PL", "G1", who[0], "E1", "E", "IDM", "SH1", 2, 4)
+        if t:
+            rows("E2", 2, "G1", 0, 4, 0, 0, 160)
+        lists("G1", 0, "P2L")
+        level("E1", "P2L", "G2", who[1], "E2", "E1", "EV0", "SH2", 1, 2)
+        lists("G2", 0, "P4L")
         for B, c in zip(BK, CD):
             mm(r(B, 128, 128 + c[1] - c[0]), fam("CNT", "E2", *c, F0), stop=False)
         level("E2", "P4L", "G3", who[2])
@@ -512,12 +534,10 @@ def rank_program(g, core, T, topo):
         cp(r("DH"), r("DM"))
         tt(r("DLO"), r("DM"), r("DH"), O.subtract)
         if t == 0:
-            for b in range(8):
+            for b in (4, 5, 6, 7, 0, 1, 2, 3):
                 ctab(b)
         dma("y", rp("DR", 12, 16, 0, 2560, 12), r("DH"))
         dma("y", rp("DR", 0, 16, 0, 2560, 0), r("DLO"))
-        for c in range(0, 160, 32):
-            act(r("CA", 16 * c, 16 * c + 512), ind(r("CT"), r("DL", c, c + 32)))
         if more:
             act(r("GD"), ind(r("DR"), r("SL", 0, 48)))
             la, tls = "LA%d" % t, []
@@ -543,37 +563,40 @@ def rank_program(g, core, T, topo):
             K = r(B, 256, 256 + c[1] - c[0])
             mm(K, fam("CNT" if c[0] else "HC", "CM", *c))
             ts(r("BT", *c), K, (4.5 if c[0] else -3.5) * U, None, O.is_lt)
+        for c in range(0, 160, 32):
+            copy("v" if t == 0 and c % 64 else "s", r("CA", 16 * c, 16 * c + 512), ind(r("CT"), r("DL", c, c + 32)))
         scan(r("RS", 1, 161), r("ON160"), r("BT"), 0.0, O.mult, O.add)
-        mm(r("K3", 0, 1), [(one("CNT", b), r("RS", 16 * b + 16, 16 * b + 17)) for b in range(10)])
-        mm(r("K5", 0, 10), fam("CNT", "RS", 0, 10, 1))
+        ends = r("K3", 0, 8)[1:]
+        mm((T.K3[0:80, 0:8],) + ends, [(r("RS", 2, 161, 2), r("B16", 0, 128, 16))])
         mm(r("K4", 0, 160), [(r("B16"), r("RS", 0, 160)), (r("LE"), r("BT"))])
         mm(r("K0", 400, 401), [(r("B16"), r("RS", 160, 161))])
-        ts(r("C1"), r("N1S"), r("K3", 0, 1), col(11), O.is_gt, O.mult)
-        act(r("W2", 0, 10), r("K5", 0, 10))
+        ts((T.EN[0:80, :],) + r("EN")[1:], (T.K3[0:80, 0:8],) + ends, 256.0, None, O.min)
+        for k in range(8):
+            ts((T.C1[0:80, :, 16 * k:16 * k + 16], "C1", 0, 2048, 1, 0, k, 256, 2, 128), n1b, (T.EN[0:80, k:k + 1],) + r("EN")[1:], None, O.is_gt)
         tt(r("RKM", 0, 160), r("K4", 0, 160), r("BT"), O.mult)
         TOT = r("K0", 400, 401)
         ts(r("INV"), r("NL0"), TOT, None, O.is_ge)
         ts(r("JJ"), r("NL1"), TOT, 0.0, O.subtract, O.max)
         if more:
             ts(r("MT", 0, 1), TOT, 256.0, None, O.min)
-        mm(r("K3", 16, 32), fam("CNT", "C1", 0, 16))
-        ts(r("BL"), r("K3", 16, 32), 1 / U, None, O.mult)
-        ts(r("B16v"), r("K3", 16, 32), 16 / U, None, O.mult)
-        tt(r("C2"), ind(r("W2"), r("BL")), r("N1S"), O.is_lt)
-        mm(r("K3", 32, 48), [(r("IDU"), r("B16v"))] + fam("CNT", "C2", 0, 16))
-        ts(r("CL"), r("K3", 32, 48), 1 / U, None, O.mult)
-        ts(r("C16v"), r("K3", 32, 48), 16 / U, None, O.mult)
-        tt(r("EQS"), ind(r("RKM"), r("CL")), r("N1F"), O.is_equal)
-        ts(r("Cv"), r("K3", 32, 48), 1 / U, None, O.mult)
-        mm(r("K3", 48, 64), [(r("ID"), r("C16v"))] + fam("FV", "EQS", 0, 16))
+        mm(r("K5", 32, 48), [((T.C1[0:80, m, :], "C1", 0, 2048, 1, 0, None, 128, 2, 128), (T.ONE[0:80, 0:1],) + r("ONE", 0, 1)[1:]) for m in range(16)],
+           outs=[r("K5", 32 + m, 33 + m) for m in range(16)], each=1)
+        for h in range(2):
+            ts(r("CL", 16 * h, 16 * h + 16), r("K5", 32, 48), 2.0, float(h), O.mult, O.add)
+        ts(r("C32v"), r("K5", 32, 48), 32.0, None, O.mult)
+        for h in range(2):
+            tt(r("EQS", 256 * h, 256 * h + 256), ind(r("RKM"), r("CL", 16 * h, 16 * h + 16)), r("N1F"), O.is_equal)
+            mm(r("K3", 48, 64), ([] if h else [(r("ID"), r("C32v"))]) + fam(("FV", "FW")[h], "EQS", 16 * h, 16 * h + 16), h == 0, h == 1)
         cp(r("VL"), r("K3", 48, 64))
         act(r("VF"), r("K3", 48, 64), F.Identity, bias=col(17))
-        act(r("XS"), ind(r("X"), r("VL")))
+        cp(r("XS"), ind(r("X"), r("VL")))
         cp(r("CAN", 0, NS), ind(r("CA"), r("VL", 0, NS // 16)))
         cp(r("CAN", NS, 256), ind(r("CA"), r("VL", NS // 16, 16)))
-        act(r("E160"), r("EQS"), F.Identity, scale=160.0)
-        mm(r("K7", 0, 16), [(r("ID"), r("Cv"))] + fam("FV", "E160", 0, 16))
-        cp(r("VP"), r("K7", 0, 16))
+        act(r("VC1"), r("VF"), F.Identity, scale=1 / 16, bias=col(30))
+        act(r("VC1"), r("VC1"), F.Identity, bias=col(28))
+        act(r("VC2"), r("VC1"), F.Identity, bias=col(29))
+        mm(r("K7", 0, 16), [(r("I160"), r("VF")), (r("IM25"), r("VC2"))])
+        ts(r("VP"), r("K7", 0, 16), -2560.0, None, O.add)
         act(r("DS"), ind(r("DR"), r("VP")))
         mm(r("K7", 16, 32), fam("CNT", "DS", 0, 16))
         ts(r("DNL"), r("K7", 16, 32), 1 / U, None, O.mult)
@@ -582,14 +605,13 @@ def rank_program(g, core, T, topo):
         visit(t, r("DNL"), "GN", REMOTE)
         for k in range(16):
             cp(r("XE", k, 16 * (256 - NS), 16), r("XS", NS, 256))
-        act(r("GT", 0, 16 * NS), ind(W, r("CAN", 0, NS)))
-        act(r("CS", NS, 256), ind(r("CA"), r("VL", NS // 16, 16)), F.Identity, bias=col(18))
-        act(r("CS", 0, NS), ind(r("CA"), r("VL", 0, NS // 16)), F.Identity, bias=col(19))
+        keys = [act(r("CS", n0, n1), ind(r("CA"), r("VL", n0 // 16, n1 // 16)), F.Identity, bias=col(c)) for n0, n1, c in ((NS, 256, 18), (0, NS, 19))]
+        act(r("GT", 0, 16 * NS), ind(W, r("CAN", 0, NS)), after=keys)
         for B, n0, n1 in CN[:-1]:
             tt(r("CM", 16 * n0, 16 * n1), ind(W, r("CAN", n0, n1)), r("XE", 16 * (n0 - NS), 16 * (n1 - NS)), O.is_lt)
         for B, n0, n1 in CN:
             K = r(B, 128 + n0, 128 + n1)
-            mm(K, [(r("IDF"), r("CS", n0, n1)), (r("B32"), r("EQS", n0, n1))], stop=False)
+            mm(K, [(r("IDF"), r("CS", n0, n1)), (r("B32"), r("EQS", n0, n1)), (r("B32"), r("EQS", 256 + n0, 256 + n1))], stop=False)
             if n0:
                 mm(K, fam("CNT", "CM", n0, n1), start=False)
             else:
@@ -601,8 +623,8 @@ def rank_program(g, core, T, topo):
         cp(ind(r("E"), r("POSE")), r("EV"))
         if more:
             for n in ("E1", "E2"):
-                rows(n, 0, "E", 0, 4, F0, ((0, 160),))
-            lists("FF", "E", F0, "P1L", FH, LO, False)
+                rows(n, 0, "E", 0, 4, F0, 0, 160)
+            lists("E", F0, "P1L")
         for m2 in range(2):
             mm(r("K3", m2, 16, 2), tl("A", r("RF"), m2))
         scan(r("RR", 1, 17), r("ON160", 0, 16), r("K3", 0, 16), 0.0, O.mult, O.add)
@@ -613,21 +635,27 @@ def rank_program(g, core, T, topo):
         act(r("NG", 0, 64), r("NONE"))
         cp(ind(r("NG"), r("POSG")), r("N0"))
         visit(t, r("NG", 0, 64), "GR", REMOTE)
+        ts(r("RFN"), r("UU", 15, 256, 16), r("TH", t, t + 1), -2.0 ** 90, O.is_lt, O.mult)
+        settle(256, "Q", "RF", "EV", "CRB", "EQ", r("XS"), True)
         if more:
-            mm(r("K1", 40, 41), [(r("ONES"), r("RR", 16, 17)), (r("SEL0"), r("MT", 0, 1))])
-            cp(r("HI", 0, 1), r("K1", 40, 41))
+            mm(r("K5", 40, 41), [(r("ONES"), r("RR", 16, 17)), (r("SEL0"), r("MT", 0, 1))])
+            cp(r("HI", 0, 1), r("K5", 40, 41))
             ts(r("HI", 1, 2), r("HI", 0, 1), 1, None, O.bitwise_and)
             ts(r("TH", t + 1, t + 2), r("HI", 1, 2), U, 9 * U, O.mult, O.add)
-        settle(256, "Q", "RF", "EV", "CRU", "EQ", r("XS"), True)
         if t == 0:
-            sel(23, (5, 7), 1 / U)
-            scaled(r("FP"), r("CNT"), col(23), "s")
             ts(col(6), col(5), -1 / 4096, col(10), O.mult, O.add)
             ts(col(6), col(6), 1 / U, None, O.mult)
             scaled(r("FD"), r("CNT"), col(6), "s")
         if not more:
-            mm(r("K1", 0, 320), [(one(f, 2 * c + k), r("E", F0 + 320 * c, F0 + 320 * c + 320)) for c in range(8) for k, f in enumerate(("FD", "FP"))])
-            act(r("OUT"), r("K1", 0, 320))
+            for c in range(8):
+                mm(r("K1", 0, 320), [(one(f, 2 * c + k), r("E", F0 + 320 * c, F0 + 320 * c + 320)) for k, f in enumerate(("FD", "FP"))], c == 0, c == 7)
+            ts(col(23), col(26), -3344.0, 3344.0, O.mult, O.add)
+            ts(col(27), col(26), 16.0, -16.0, O.mult, O.add)
+            act(r("CA", 640, 960), r("K1", 0, 320))
+            for c in range(0, 320, 80):
+                ts(r("CA", c, c + 80), r("CA", 640 + c, 720 + c), 0.5, col(23), O.is_lt, O.mult)
+                ts(r("CA", 320 + c, 400 + c), r("CA", 640 + c, 720 + c), 0.0, col(27), O.max, O.add)
+                tt(r("OUT", c, c + 80), r("CA", c, c + 80), r("CA", 320 + c, 400 + c), O.add)
             dma("y", hbm("yof"), rp("OUT", 0, 2, 0, 320))
             dma("y", hbm("yan"), rp("OUT", 1, 2, 0, 320))
         guests(t)
@@ -697,6 +725,6 @@ def rank_program(g, core, T, topo):
             s, n = c["sem"]
         cnt[s] = n
         c["ev"] = (s, n, dict(known[q]))
-    for s in sorted(cnt):
-        if known["g"].get(s, 0) < cnt[s]:
+    for s in cnt:
+        if max(known[q].get(s, 0) for q in QU) < cnt[s]:
             G.wait_ge(T.sem[s], cnt[s])

@@ -1,21 +1,52 @@
+import math
 from concourse.bass import DstId, RemoteDMATransfer
-from concourse.mybir import AluOpType as O, ActivationFunctionType as F
+from concourse.mybir import AluOpType as O, ActivationFunctionType as F, AxisListType as AX
 
 RO = 4
 LN2 = 0.6931471805599453
 U = 2.0 ** 18
-F0, G0, NW = 16, 2576, 3344
-CH = ((0, 96), (96, 160))
-MERGE = (("s", 0, 32, "s"), ("s", 32, 64, "v"), ("v", 64, 96, "v"), ("s", 96, 128, "v"), ("v", 128, 160, "s"))
-LV0 = (MERGE, MERGE, (("s", 0, 48, ""), ("v", 48, 96, ""), ("s", 96, 128, ""), ("v", 128, 160, "")))
-PLAIN = (("s", 0, 48, ""), ("v", 48, 64, ""), ("v", 64, 80, ""), ("v", 80, 96, ""), ("s", 96, 160, ""))
-LV = (PLAIN,) * 3
-MOVES = {48: 0, 96: 48, 160: 96}
+BIG = 2.0 ** 20
+M0, M6, M14 = 1.5 * 2.0 ** 23, 1.5 * 2.0 ** 29, 1.5 * 2.0 ** 37
+G0, RT, NW = 2560, 3328, 3344
+TOP, FAR = 4416, 4360
+L0A = (("s", 0, 32, "s"), ("s", 32, 64, "s"), ("v", 64, 112, "a"), ("v", 112, 160, "a"))
+L0C = (("s", 0, 48, ""), ("v", 48, 80, ""), ("s", 80, 112, ""), ("v", 112, 160, ""))
+NA = 80
+LA = (("s", 0, 48, 0), ("s", 48, 80, 48)) + tuple(("v", c, c + 16, "a") for c in range(NA, 160, 16))
+LB = LA
+LC = (("s", 0, 48, ""), ("v", 48, 80, ""), ("s", 80, 144, ""), ("v", 144, 160, ""))
+LV0, LV = (L0A, L0A, L0C), (LA, LB, LC)
+MB = ("K5", "K5")
+MA = ((80, 160), (0, 80))
+MC = ((80, 112), (112, 160), (0, 80))
+MC0 = ((64, 112), (112, 160))
+CH0 = ((0, 64), (64, 112), (112, 160))
+CH = ((0, 80), (80, 128), (128, 160))
+CH4 = CH
+CP = ((0, 96), (96, 160))
 CD = ((0, 80), (80, 160))
-CS_, CV = ((0, 32), (32, 64)), ((64, 112), (112, 160))
+CS_ = ((0, 32), (32, 64))
+CV = ((64, 112), (112, 160))
 CC = ((0, 64), (64, 112), (112, 160))
-NS = 96
-CN = (("K4", 96, 192), ("K5", 192, 256), ("K6", 0, NS))
+NS = 128
+SS = ((("K1", "K2"), 0, 64), (("K3", "K7"), 64, 128))
+SV = ((128, 192), (192, 256))
+CN = (("K4", 128, 192, ((128, 192),)), ("K5", 192, 256, ((192, 256),)), ("K6", 0, 128, ((0, 64), (64, 128))))
+CANP = ((0, 128), (128, 256))
+VB = "K1"
+DQ = "s"
+WS = 2048
+ZS = 2
+ZG = 2
+GQ = "svv"
+CTQ = "vsssssvv"
+CAQ = "sssvs"
+LOADS = (("WK", "wk", 2048, 4096), ("S", "s0", 0, 4096), ("X", "x", 0, 2560), ("WK", "wk", 0, 2048))
+EARLY = 3
+FAMS = "CNT HC FS FF FP FQ FD FV FW".split()
+PIECE = 8
+PASSES = 2000
+ORDER = []
 SCRATCH, PACK = {}, {}
 WIDE = {"float32": 4, "bfloat16": 2, "int32": 4, "uint16": 2}
 FILL = dict.fromkeys(WIDE, 0)
@@ -33,54 +64,54 @@ def _b(names, cols, d="float32", w="sbuf"):
 
 
 _b("K0 K1 K2 K3 K4 K5 K6 K7", 512, "float32", "psum")
-_b("CNT HC FD FP FV FW", 2048, "bfloat16")
-_b("ONE B16 ID IM1 LT LE M16b I7 IM2K CR B32 BD BW B4 LTS UBS IDB IDN ONES SEL0 I768 I8K IBG IDM SH1 EV0 SH2 "
-   "A00 A01 A10 A11 H00 H01 H10 H11", 128, "bfloat16")
+_b("FAM", 144 * len(FAMS), "bfloat16")
+_b("ONE B16 ID IM1 LT LE M16b I7 IM2K BD BH BL BN BR BO LTN SEL0 I768", 128, "bfloat16")
+_b("A0 A1 H0 H1", 160, "bfloat16")
 _b("M16 IDF I160 IM25", 128)
 SCRATCH["C1"] = ("sbuf", [128, 16, 128], "bfloat16")
 SCRATCH["N1B"] = ("sbuf", [128, 16, 16], "bfloat16")
-_b("E", F0 + 4096 + 2560, "bfloat16")
+SCRATCH["EQ"] = ("sbuf", [128, 16, 256], "bfloat16")
+SCRATCH["EQg"] = ("sbuf", [128, 4, 64], "bfloat16")
+_b("E", 4096 + 2560 + 16, "bfloat16")
 _b("E1 E2 WP", NW, "bfloat16")
 _b("G1 G2 G3 DR XE", 2560, "bfloat16")
-_b("GT", 1536, "bfloat16")
+_b("GC", 16 * NS, "bfloat16")
 _b("X", 2576, "bfloat16")
 _b("S", 4368, "bfloat16")
 _b("WK CM", 4096, "bfloat16")
 _b("CT", 4096)
-_b("EQ", 2176, "bfloat16")
 _b("ST", 4 * 224, "bfloat16")
-_b("N0 DS EV2 Q2 CRB EV Q NEGM POSM XS", 256, "bfloat16")
-_b("R2 SG0 SG1 NG ZR EQS", 512, "bfloat16")
-_b("N1F MASK CS TR UU UX", 256)
+_b("DS EV Q DG XS CUM C8", 256, "bfloat16")
+_b("CRB PW", 272, "bfloat16")
+_b("R2 SG0 SG1 ZR EQS", 512, "bfloat16")
+_b("N1F MASK CS TR UU UX DMP ON", 256)
 _b("CAG", 272)
 _b("CA", 2576)
-_b("ON160 W1 T1", 160)
+_b("W1", 160)
 _b("RKM", 176)
 _b("CO", 64)
-_b("DG2", 32)
-_b("TH VC1 VC2 VF NL0 NL1 DUMP T14 T6 PM Z2 Z3", 16)
+_b("TH VC1 VC2 VF NL0 NL1 NLB T14 T6 MD AC", 16)
 _b("CSg TRg UUg", 64)
 _b("PI YI HI", 16, "int32")
-_b("AN LOI HII SHI PLI DI DM", 160, "int32")
+_b("AN LOI SHI PLI DI DM", 160, "int32")
 _b("OF", 208, "int32")
 _b("SNDI SA SB", 48, "int32")
-_b("HM BT DH DLO", 160, "bfloat16")
+_b("BT DH DLO P2H P2W P4H P4W", 160, "bfloat16")
 _b("RS", 176, "bfloat16")
-_b("C32v CB PW2 L96 RFN LB INV JJ MT RF RFg", 16, "bfloat16")
-_b("RR", 32, "bfloat16")
+_b("C32v CB INV JJ MT C96", 16, "bfloat16")
 _b("EN", 8, "bfloat16")
-_b("Qg EVg NONE XG", 64, "bfloat16")
+_b("Qg EVg XG", 64, "bfloat16")
 _b("GD", 768, "bfloat16")
-_b("XGE CMg", 1024, "bfloat16")
-_b("EQg", 160, "bfloat16")
+_b("GTg CMg JK CR", 1024, "bfloat16")
+_b("GT", 1536, "bfloat16")
 _b("PL P1L P2L P4L DL", 160, "uint16")
-_b("DNL VP VL POSE POSS POSG NL", 16, "uint16")
+_b("DNL VP VL POSE POSS NG", 16, "uint16")
 _b("CL", 32, "uint16")
-_b("SL CgL CRUg NGU", 64, "uint16")
+_b("SL CgL CRUg", 64, "uint16")
 _b("CAN", 256, "uint16")
 _b("OUT", 320)
 for _t in range(RO):
-    _b("GR%d" % _t, 64, "bfloat16")
+    _b("GR%d" % _t, 16, "uint16")
     _b("GX%d" % _t, 272, "bfloat16")
     _b("GN%d" % _t, 16, "uint16")
     if _t < RO - 1:
@@ -89,7 +120,19 @@ for _t in range(RO):
 SEMAPHORES = ["cv", "cs", "cp", "cg"] + ["d%d" % k for k in range(110)] + \
     ["%s%d" % (k, t) for k in ("ga", "gl", "GRa", "GRl", "GXa", "GXl", "GNa", "GNl") for t in range(RO)]
 
-CYC, PE, GAT, SCA, WAKE, LOCAL, RATE, REMOTE, SWEEPS = 0.00083, 0.00042, 1.4, 3.0, 0.22, 1.2, 200e3, 2.0, 2
+CYC = 0.001
+PE = 0.0005
+GAT = 1.17
+SCA = 2.3
+WAKE = 0.18
+LOCAL = 1.6
+RATE = 190e3
+REMOTE = 2.3
+FIRST = 3.0
+MEAN = 0.05
+NEAR = 0.5
+KICK = 3
+SLACK = 0.5
 
 
 def rank_program(g, core, T, topo):
@@ -99,7 +142,7 @@ def rank_program(g, core, T, topo):
     N = len(T.cores)
     V, S, P, G = g.vector, g.scalar, g.tensor, g
     QU = {"v": V, "s": S, "p": P, "g": G, "y": g.sync}
-    acc, bank, calls = {}, {}, []
+    acc, bank, calls, group = {}, {}, [], {}
 
     def r(name, lo=0, hi=None, step=1):
         ph, o, w = PACK.get(name, (name, 0, None))
@@ -108,11 +151,16 @@ def rank_program(g, core, T, topo):
         ap = T[ph][:, o + lo:o + hi:step] if step > 1 else T[ph][:, o + lo:o + hi]
         return (ap, name, lo, hi, step, lo % step, None, (hi - lo + step - 1) // step, WIDE[SCRATCH[ph][2]], 128)
 
+    def blk(name, a, b, lo, hi):
+        w = T[name].shape[2]
+        ap = T[name][:, a, lo:hi] if b == a + 1 else T[name][:, a:b, lo:hi]
+        return (ap, name, w * a + lo, w * (b - 1) + hi, 1, 0, None, (b - a) * (hi - lo), WIDE[SCRATCH[name][2]], 128)
+
     def rp(name, row, step, lo, hi, part=None):
         return (T[name][row::step, lo:hi], name, lo, hi, 1, 0, part, hi - lo, WIDE[SCRATCH[name][2]], 128 // step)
 
-    def half(name, h, hi):
-        return (T[name][64 * h:64 * h + 64, :], name, 0, hi, 1, 0, h, hi, 2, 64)
+    def part(name, a, b, lo, hi):
+        return (T[name][a:b, lo:hi], name, lo, hi, 1, 0, a, hi - lo, 2, b - a)
 
     def hbm(name, lo=None, hi=None):
         return (T[name][:] if lo is None else T[name][:, lo:hi], name, lo or 0, hi or 1, 1, 0, None, 1, 0, 0)
@@ -131,7 +179,7 @@ def rank_program(g, core, T, topo):
         return o
 
     def lap(a, b):
-        if a[1] <= b[0] or b[1] <= a[0] or (a[2] > 1 and a[2] == b[2] and a[3] != b[3]):
+        if a[1] <= b[0] or b[1] <= a[0] or (a[3] - b[3]) % math.gcd(a[2], b[2]):
             return False
         return a[4] is None or b[4] is None or a[4] == b[4]
 
@@ -146,7 +194,8 @@ def rank_program(g, core, T, topo):
                 for a in acc.get(R[1], []):
                     if (isw or a[1]) and lap(a[0], R[2:7]):
                         deps[a[2]] = 1
-        calls.append({"q": q, "call": call, "deps": deps, "cost": cost, "sem": sem, "hold": cost if hold is None else hold})
+        name = (q,) + tuple((x[1][:2] if x[1][:2] in ("GR", "GX", "GN", "LA") else x[1], 0 if x[1] == "TH" else x[2]) for x in writes + reads)
+        calls.append({"q": q, "call": call, "deps": deps, "cost": cost, "sem": sem, "hold": cost if hold is None else hold, "name": name})
         for R, isw in both:
             if R[1][0] == "K":
                 bank.setdefault(R[1], {})[q] = me
@@ -184,21 +233,34 @@ def rank_program(g, core, T, topo):
     def tr(o, a):
         op("v", lambda: V.transpose(o[0], a[0]), [a], [o], vc(o, a))
 
+    def red(o, a):
+        op("v", lambda: V.tensor_reduce(o[0], a[0], AX.X, O.add), [a], [o], vc(o, a, w=1))
+
     def scan(o, d0, d1, init, f0, f1):
         op("v", lambda: V.tensor_tensor_scan(o[0], d0[0], d1[0], init, f0, f1), [d0, d1], [o], vc(o, d0, d1))
 
-    def act(o, a, f=F.Copy, bias=None, scale=None, after=(), once=0.0):
+    def act(o, a, f=F.Copy, bias=None, scale=None, after=(), once=0.0, total=None):
         kw = {}
         if bias is not None:
             kw["bias"] = ap(bias)
         if scale is not None:
             kw["scale"] = ap(scale)
-        return op("s", lambda: S.activation(o[0], a[0], f, **kw), flat(a, bias, scale), [o], vc(o, a, w=1) + once, after=after)
+        if total is not None:
+            kw["accum_out"] = total[0]
+        return op("s", lambda: S.activation(o[0], a[0], f, **kw), flat(a, bias, scale), flat(o, total), vc(o, a, w=1) + 0.03 + once, after=after)
 
     def copy(q, o, a):
         return (act if q == "s" else cp)(o, a)
 
     def mm(o, pairs, start=True, stop=True, outs=None, each=None):
+        if len(pairs) > PIECE and not each:
+            first = len(calls)
+            for k in range(0, len(pairs), PIECE):
+                mm(o, pairs[k:k + PIECE], start and k == 0, stop and k + PIECE >= len(pairs), outs and outs[k:k + PIECE])
+            for k in range(first, len(calls)):
+                group[k] = (first, len(calls) - 1)
+            return
+
         def call():
             i = None
             for k, (l, x) in enumerate(pairs):
@@ -208,7 +270,8 @@ def rank_program(g, core, T, topo):
         op("p", call, [z for l, x in pairs for z in (l, x)], [o], sum(max(64, x[7]) * (x[8] * x[8] // 4) for l, x in pairs) * PE)
 
     def one(f, i):
-        return r(f, 128 * i, 128 * i + 128)
+        o = 144 * FAMS.index(f) + 15 - i
+        return r("FAM", o, o + 128)
 
     def fam(f, src, c0, c1, o=0):
         return [(one(f, i), r(src, o + 16 * c0 + i, o + 16 * c1, 16)) for i in range(16)]
@@ -230,7 +293,7 @@ def rank_program(g, core, T, topo):
         op("g", lambda: G.affine_select(o[0], a[0], pat, O.is_ge, 0.0, base, cm), [a], [o], c, hold=c + WAKE)
 
     def send(call, src, dst, left, landed, n, time):
-        s = op("g", call, [src], [], time, (left, n), hold=0.5)
+        s = op("g", call, [src], [], time, (left, n), hold=0.6 + max(0, time - 2 * REMOTE))
         op(None, None, [], [dst], time, (landed, n), after=[s])
 
     def visit(t, src, name, time):
@@ -241,151 +304,113 @@ def rank_program(g, core, T, topo):
         send(lambda: G.remote_dma(out_ap=out[0], in_ap=src[0], remote_sem=T.sem["%sa%d" % (name, t)], local_sem=T.sem["%sl%d" % (name, t)],
                                   pid=pid, routing_id=rid, dma_engine_mask=mask), src, out, "%sl%d" % (name, t), "%sa%d" % (name, t), 8, time)
 
-    def sel(dst, rows, val):
-        for k, row in enumerate(rows):
-            ts(col(dst) if k == 0 else col(63), col(0), float(row), val, O.is_equal, O.mult)
-            if k:
-                tt(col(dst), col(dst), col(63), O.add)
-
-    def scaled(o, a, s, q="v"):
-        for c in range(0, o[7], 512):
-            x, y = r(o[1], o[2] + c, min(o[3], o[2] + c + 512)), r(a[1], a[2] + c, min(a[3], a[2] + c + 512))
-            if q == "v":
-                ts(x, y, s, None, O.mult)
-            else:
-                act(x, y, F.Identity, scale=s)
-
-    dma("y", r("OF"), hbm("of0"))
-    dma("y", r("AN"), hbm("an0"))
+    last = [dma("y", r("OF"), hbm("of0")), dma("y", r("AN"), hbm("an0"))]
     dma("y", r("SNDI"), hbm("snd"))
-    last = ()
-    for n, x, w in (("WK", "wk", 4096), ("S", "s0", 4096), ("X", "x", 2560)):
-        for c in sorted(range(0, w, 512), key=lambda c: n == "WK" and c < 2048):
-            last = [dma("y", r(n, c, c + 512), hbm(x, c, c + 512), last)]
+    loads = [(n, x, c) for n, x, lo, hi in LOADS for c in range(lo, hi, 512)]
+    for n, x, c in loads[:EARLY]:
+        last = [dma("y", r(n, c, c + 512), hbm(x, c, c + 512), last)]
     iota(r("PI", 0, 2), [[0, 2]], 0, 1)
     iota(r("M16"), [[0, 8], [1, 16]])
     ms(r("ONE"), 1.0)
     gsel(r("B16"), r("ONE"), [[-16, 8], [0, 16]], 0, 1)
     gsel(r("B16"), r("B16"), [[16, 8], [0, 16]], 15, -1)
-    iota(half("R2", 0, 512), [[1, 32], [0, 16]])
-    iota(half("R2", 1, 512), [[0, 32], [1, 16]])
+    iota(part("R2", 0, 64, 0, 512), [[0, 2], [1, 256]])
+    ms(part("R2", 64, 96, 0, 256), 0.0)
+    ms(part("R2", 64, 96, 256, 512), 1.0)
+    ms(part("R2", 96, 128, 0, 512), 1.0)
     iota(r("N1F"), [[1, 256]], 1)
     n1b = (T.N1B[0:80], "N1B", 0, 256, 1, 0, None, 256, 2, 128)
     iota((T.N1B[:],) + n1b[1:], [[16, 16], [1, 16]], 1)
-    iota(r("N0"), [[1, 256]])
     iota(r("NL0"), [[16, 16]])
     for c in range(0, 2560, 640):
         fill(r("DR", c, c + 640), 0)
-    for k, m in enumerate((15, 31, 3, 1)):
+    for k, m in enumerate((15, 31)):
         ts(r("YI", k, k + 1), r("PI", 0, 1), m, None, O.bitwise_and)
-    cp(r("CO", 0, 3), r("YI", 0, 3))
+    cp(r("CO", 0, 2), r("YI", 0, 2))
     ms(r("ZR"), 0.0)
-    for c in range(0, NW, 512):
-        act(r("WP", c, min(NW, c + 512)), r("ZR", 0, min(NW, c + 512) - c))
+    for c in range(0, WS, 512):
+        act(r("WP", c, c + 512), r("ZR"))
+    ms(r("WP", WS, NW), 0.0)
+    for c in range(16 * MC0[0][0], 2560, 512):
+        act(r("E2", c, min(2560, c + 512)), r("ZR", 0, min(2560, c + 512) - c))
     ms(r("ST", 208, 448, 224), 0.0)
-    for k in (2, 3):
-        ms(r("ST", 224 * k + 160, 224 * k + 209), 0.0)
-    for c in range(0, 2048, 1024):
-        ms(r("CNT", c, c + 1024), 0.0)
-    for q in range(8):
-        ts(r("CNT", 16 * q, 2048, 129), r("B16", 16 * q, 16 * q + 16), U, None, O.mult)
+    ms(r("ST", 448 + 160, 448 + 209), float(RT))
+    ms(r("ST", 672 + 160, 672 + 209), 0.0)
+    for c in range(0, 144 * len(FAMS), 432):
+        act(r("FAM", c, c + 432), r("ZR", 0, 432))
     ts(r("M16b"), r("M16"), col(0), None, O.is_equal)
+    ts(r("MD"), r("M16", 0, 16), col(0), None, O.is_equal)
     tt(r("ID"), r("M16b"), r("B16"), O.mult)
-    ts(col(3), col(2), 0.0, None, O.is_equal)
-    sel(4, (1, 9), 1 / U)
-    sel(7, (4, 6), -1 / U)
-    tt(r("CB", 0, 1), col(7), col(4), O.add)
-    scaled(r("FP"), r("CNT"), r("CB", 0, 1))
-    sel(5, (4,), 4096.0)
-    act(r("IDM"), r("ID"), F.Identity, scale=col(3))
-    ts(col(24), col(3), 2.0, col(0), O.mult, O.add)
-    ts(col(25), col(4), U, col(3), O.mult, O.add)
-    ts(r("SH1"), r("M16"), col(24), col(25), O.is_equal, O.mult)
-    tt(r("SH1"), r("SH1"), r("B16"), O.mult)
-    ts(col(26), r("YI", 3, 4), -1.0, 1.0, O.mult, O.add)
-    act(r("EV0"), r("ID"), F.Identity, scale=col(26))
-    ms(r("SH2", 0, 1), 0.0)
-    act(r("SH2", 1, 128), r("EV0", 0, 127))
-    scaled(r("HC"), r("CNT"), 0.5)
-    ts(col(8), col(0), 1 / U, None, O.mult)
-    scaled(r("FV"), r("CNT"), col(8), "s")
-    ts(r("CB", 1, 2), col(8), 16 / U, None, O.add)
-    scaled(r("FW"), r("CNT"), r("CB", 1, 2))
-    for n, s in (("IM1", -1.0), ("I7", 7.0), ("IM2K", -2048.0), ("IDB", 0.125), ("IDN", -0.125), ("I768", 768.0),
-                 ("I8K", 8192.0), ("IBG", -2.0 ** 90), ("IDF", 1.0), ("I160", 160.0), ("IM25", -2559.0)):
+    for c, rws in ((2, (0, 13, 12)), (3, (4, 8)), (4, (8, 11, 2)), (6, (9, 12, 2)), (7, (8, 12)), (8, (0, 10, 9)), (22, (0, 16, 2 if GQ[2] == "v" else 1))):
+        red(col(c), r("MD", *rws))
+    ts(col(7), col(7), -1.0, 1.0, O.mult, O.add)
+    ts(r("CB", 0, 1), col(6), -1.0, 1.0, O.mult, O.add)
+    ts(r("CB", 1, 2), r("MD", 11, 12), float(RT), None, O.mult)
+    ts(col(9), col(0), 16.0, None, O.add)
+    for f, w in zip(FAMS, (U, U / 2, col(7), col(3), col(4), col(6), col(2), col(0), col(9))):
+        o = 144 * FAMS.index(f) + 15
+        ts(r("FAM", o, o + 128, 16), r("B16", 0, 128, 16), w, None, O.mult)
+    ts(col(5), r("MD", 4, 5), 4096.0, None, O.mult)
+    for n, s in (("IM1", -1.0), ("I7", 7.0), ("IM2K", -2048.0), ("I768", 768.0), ("IDF", 1.0), ("I160", 160.0), ("IM25", -2559.0)):
         act(r(n), r("ID"), F.Identity, scale=s)
-    for n, s in (("B32", -32 * U), ("B4", 2.0 ** 32)):
+    ts(col(10), r("MD", 1, 2), 1024.0, col(2), O.mult, O.subtract)
+    ts(col(11), r("MD", 1, 2), -1 / 8192, None, O.mult)
+    for n, s in (("BO", -BIG), ("BD", col(2)), ("BH", r("MD", 12, 13)), ("BL", col(8)), ("BN", col(10)), ("BR", col(11))):
         act(r(n), r("B16"), F.Identity, scale=s)
     ts(r("LE"), r("M16"), col(0), None, O.is_gt)
     tt(r("LT"), r("LE"), r("B16"), O.mult)
     tt(r("LE"), r("LT"), r("ID"), O.add)
-    act(r("LTS"), r("LT"), F.Identity, scale=2.0 ** -13)
-    tt(r("UBS"), r("B16"), r("LT"), O.subtract)
-    act(r("UBS"), r("UBS"), F.Identity, scale=2.0 ** -13)
-    act(r("ONES"), r("ONE"), F.Identity, scale=2.0 ** -13)
-    sel(9, (0,), 1.0)
-    act(r("SEL0"), r("ONE"), F.Identity, scale=col(9))
-    sel(10, (0, 12), 1.0)
-    act(r("BD"), r("B16"), F.Identity, scale=col(10))
+    act(r("LTN"), r("LT"), F.Identity, scale=-BIG)
+    act(r("SEL0"), r("ONE"), F.Identity, scale=r("MD", 0, 1))
     ts(col(12), col(1), 15.5, None, O.is_lt)
     ts(col(13), col(1), 15.5, None, O.is_gt)
-    for a, s in (("A", 1.0), ("H", 0.5)):
-        fill(r(a + "01", 0, 16), 0)
-        fill(r(a + "10", 112, 128), 0)
-        ts(r(a + "00"), r("ID"), col(12), s, O.mult, O.mult)
-        ts(r(a + "01", 16, 128), r("ID", 0, 112), col(12), s, O.mult, O.mult)
-        ts(r(a + "10", 0, 112), r("ID", 16, 128), col(13), s, O.mult, O.mult)
-        ts(r(a + "11"), r("ID"), col(13), s, O.mult, O.mult)
-    fill(r("ON160"), 1)
-    ms(col(32), 30 * LN2)
-    ms(col(33), -64 * LN2)
-    act(r("CB", 2, 3), col(0), F.Exp, scale=-LN2, bias=col(32), once=1.3)
-    cp(col(14), r("CB", 2, 3))
-    act(r("BW"), r("B16"), F.Identity, scale=col(14))
-    ms(half("CR", 0, 128), 0.25)
-    ms(half("CR", 1, 128), 1.0 / 64)
-    for b in range(4, 8):
-        ms(col(40 + b), 512.0 * b - 4095.5)
-    iota(r("CO", 48, 56), [[0, 2], [512, 4]])
-    ms(col(15), 2.0 ** -112)
-    ms(col(16), -2.0 ** -112)
-    fill(col(17), F0)
-    for c, e in ((18, 32), (19, 40), (20, 0)):
-        ts(col(c), col(0), -16384.0, 15 * 16384.0 + 4096.0 + e * U, O.mult, O.add)
-    ms(col(28), 1.5 * 2.0 ** 23)
-    ms(col(29), -1.5 * 2.0 ** 23 - 1)
-    ms(col(30), -7.5 / 16)
-    ts(col(21), col(14), -2.0, 2.0 ** 40, O.mult, O.add)
-    ms(col(22), -2.0 ** 40)
+    for a, s in (("A", 1.0), ("H", -0.5)):
+        for k in range(2):
+            fill(r("%s%d" % (a, k), 0, 16), 0)
+            fill(r("%s%d" % (a, k), 144, 160), 0)
+            ts(r("%s%d" % (a, k), 16, 144), r("ID"), col(12 + k), s, O.mult, O.mult)
+    fill(r("ON"), 1)
+    fill(r("C96"), 96)
+    fill(r("C8", 0, NS), 8 * U)
+    fill(r("C8", NS, 256), 0)
+    ms(col(32), -77.0)
+    act(col(15), col(32), F.Exp, once=1.3)
+    ts(col(16), col(15), -1.0, None, O.mult)
+    ms(part("CR", 0, 64, 0, 1024), 1.0 / 64)
+    ms(part("CR", 64, 96, 0, 1024), 8.0)
+    for b in range(8):
+        ms(part("CR", 96, 128, 128 * b, 128 * b + 128), 16.0 * b)
+    ms(col(40), -4095.5)
+    ms(col(41), -2048.0)
+    ts(col(21), col(0), -16384.0, 15 * 16384.0, O.mult, O.add)
+    ts(col(20), col(22), 8 * U, col(21), O.mult, O.add)
     for c in (0, 128):
         act(r("MASK", c, c + 128), r("M16"), F.Sign)
-        act(r("POSM", c, c + 128), r("M16b"), F.Identity, scale=16384.0)
-        act(r("NEGM", c, c + 128), r("M16b"), F.Identity, scale=col(21), bias=col(22))
+        ts(r("DG", c, c + 128), r("M16b"), BIG + TOP, -BIG, O.mult, O.add)
     ts(r("NL0"), r("NL0"), col(0), None, O.add)
     ts(r("NL1"), r("NL0"), 1.0, None, O.add)
-    ts(r("DUMP"), r("NL0"), 8192.0, None, O.add)
-    ts(r("DG2", 0, 16), r("NL0"), 256.0 - 1024.0, None, O.add)
-    ts(r("DG2", 16, 32), r("NL0"), 4096.0, None, O.add)
+    ts(r("NLB"), r("NL0"), -1.0, -0.5, O.mult, O.add)
+    fill(r("DMP"), 4 * BIG)
+    ts(r("DMP", 0, 256, 16), r("NL0"), -1.0, TOP - 4096.0, O.mult, O.add)
     fill(r("TH", 0, 1), 9 * U)
-    for x in [r("RS", 0, 1), r("RR", 0, 1), r("RKM", 160, 176), r("CA", 2560, 2576), r("X", 2560, 2576), r("Q"), r("Q2"), r("Qg")] + \
+    for x in [r("RS", 0, 1), r("RKM", 160, 176), r("X", 2560, 2576), r("Q"), r("Qg"), r("S", 4096, 4368)] + \
             [r("GX%d" % t, 256, 272) for t in range(RO)]:
         fill(x, 0)
-    fill(r("CAG", 256, 272), 1 - 2 ** 24)
-    fill(r("NONE"), 256)
-    for n in ("E", "E1", "E2"):
-        ts(r(n, 0, F0), r("ZR", 0, F0), col(5), None, O.add)
-    fill(r("Q", 4, 256, 16), 4096)
-    cp(r("ST", 0, 208), r("OF"))
+    ms(r("NG"), 0)
+    fill(r("CA", 2560, 2576), 32 * U + FAR)
+    fill(r("CAG", 256, 272), -32 * U)
+    for c, v in ((4, 4096), (10, RT), (9, 96)):
+        fill(r("Q", c, 256, 16), v)
+    ts(r("ST", 0, 208), r("OF"), M6, M6, O.add, O.subtract)
     tt(r("ST", 224, 432), r("OF"), r("ST", 0, 208), O.subtract)
+    ts(r("ST", 448, 608), r("AN"), M6, M6, O.add, O.subtract)
+    tt(r("ST", 672, 832), r("AN"), r("ST", 448, 608), O.subtract)
+    for row, seg in ((12, 0), (0, 1), (11, 2), (10, 2), (9, 3), (8, 3)):
+        last = [dma("y", rp("WP", row, 16, 0, NW, row), r("ST", 224 * seg, 224 * seg + 209), last)]
+    for n, x, c in loads[EARLY:]:
+        last = [dma("y", r(n, c, c + 512), hbm(x, c, c + 512), last)]
     ts(r("LOI"), r("AN"), 15, None, O.bitwise_and)
-    ts(r("HII"), r("AN"), 4080, None, O.bitwise_and)
     ts(r("SHI"), r("AN"), 4, None, O.arith_shift_right)
-    cp(r("ST", 672, 832), r("LOI"))
-    ts(r("T1"), r("HII"), 3328, 3344, O.is_lt, O.mult)
-    ts(r("HM"), r("HII"), -3328, None, O.add)
-    tt(r("ST", 448, 608), r("T1"), r("HM"), O.add)
-    for row, seg in ((12, 0), (0, 1), (9, 3), (1, 2)):
-        dma("y", rp("WP", row, 16, 0, NW, row), r("ST", 224 * seg, 224 * seg + 209))
     ts(r("W1"), r("LOI"), 209, None, O.mult)
     tt(r("PLI"), r("W1"), r("SHI"), O.add)
     cp(r("PL"), r("PLI"))
@@ -397,141 +422,160 @@ def rank_program(g, core, T, topo):
 
     def ctab(b):
         K, sg = ("K4", "K5")[b % 2], "SG%d" % (b % 2)
-        tv = [(r("I7"), r("WK", 512 * b, 512 * b + 512)), (r("CR"), r("R2"))]
+        tv, out = [(r("I7"), r("WK", 512 * b, 512 * b + 512)), (r("CR", 128 * b, 128 * b + 128), r("R2"))], r("CT", 512 * b, 512 * b + 512)
         mm(r(K), tv)
-        if b > 3:
-            act(r(sg), r(K), F.Sign, bias=col(40 + b))
+        if b < 4:
+            copy(CTQ[b], out, r(K))
+        elif CTQ[b] == "v":
+            ts(r(sg), r(K), 4095.5, -4096.0, O.is_gt, O.mult)
+            tt(out, r(K), r(sg), O.add)
+        else:
+            act(r(sg), r(K), F.Sign, bias=col(40))
             mm(r(K), tv + [(r("IM2K"), r(sg))])
-        act(r("CT", 512 * b, 512 * b + 512), r(K), F.Identity, bias=col(48 + b))
+            act(out, r(K), F.Identity, bias=col(41))
 
     BK = ("K0", "K7", "K6")
 
-    def rows(dst, a, src, b, step, o, c0, c1):
-        dma("y", rp(dst, a, step, F0 + 16 * c0, F0 + 16 * c1, a), rp(src, b, step, o + 16 * c0, o + 16 * c1))
+    def rows(dst, a, src, b, step, c0, c1):
+        dma("y", rp(dst, a, step, 16 * c0, 16 * c1, a), rp(src, b, step, 16 * c0, 16 * c1))
 
-    def lists(src, o, lst):
-        for B, c in zip(BK, CH):
-            K = r(B, 0, c[1] - c[0])
-            mm(K, fam("FP", src, *c, o))
-            cp(r(lst, *c), K)
-
-    def level(win, lst, out, who, nxt=None, own=None, keep=None, shift=None, row=0, step=0):
+    def level(t, win, lst, out, who, nxt=None, own=None, step=0, new=None, moved=()):
+        for c0, c1 in moved:
+            if t and step == 2 and c1 <= NA:
+                rows(nxt, 0, "E", 0, 4, c0, c1)
+                rows(nxt, 2, "G1", 0, 4, c0, c1)
+            else:
+                rows(nxt, 0, own, 0, step, c0, c1)
         for q, c0, c1, p in who:
-            copy(q, r(out, 16 * c0, 16 * c1), ind(r(win, 0, NW), r(lst, c0, c1)))
-        for k, (q, c0, c1, p) in enumerate(who if nxt else ()):
-            if p:
-                K = r(("K1", "K2", "K3")[k % (3 if who is MERGE else 2)], 0, 16 * (c1 - c0))
-                mm(K, [(r(keep), r(own, F0 + 16 * c0, F0 + 16 * c1))], stop=False)
-                mm(K, [(r(shift), r(out, 16 * c0, 16 * c1))], start=False)
-                copy(p, r(nxt, F0 + 16 * c0, F0 + 16 * c1), K)
-            elif c1 in MOVES:
-                rows(nxt, row, out, 0, step, 0, MOVES[c1], c1)
+            a = ind(r(win, 0, NW), r(lst, c0, c1))
+            if p == "a":
+                tt(r(nxt, 16 * c0, 16 * c1), a, r(nxt if moved else own, 16 * c0, 16 * c1), O.add)
+            else:
+                copy(q, r(out, 16 * c0, 16 * c1), a)
+            if isinstance(p, int):
+                rows(nxt, step // 2, out, 0, step, p, c1)
+        for k, (q, c0, c1, p) in enumerate(who):
+            if p in ("s", "v"):
+                K = r((MB if t else ("K1", "K2"))[k % 2], 0, 16 * (c1 - c0))
+                mm(K, [(r("ID"), r(own, 16 * c0, 16 * c1))], stop=False)
+                mm(K, [(r("ID"), r(out, 16 * c0, 16 * c1))], start=False)
+                copy(p, r(nxt, 16 * c0, 16 * c1), K)
+        for B, (c0, c1) in zip(BK, ((CH if step == 4 else CH4) if t else CH0) if new else ()):
+            K, added = r(B, 0, c1 - c0), [p for q, a, b, p in who if a <= c0 < b] == ["a"]
+            hi, lo = r(new + "H", c0, c1), r(new + "W", c0, c1)
+            if t:
+                mm(K, [(r("ID"), hi), (r("ID"), lo)], stop=False)
+                mm(K, fam("FF", nxt if added else out, c0, c1), start=False)
+                ts(r(new + "L", c0, c1), K, float(RT), None, O.min)
+            else:
+                mm(K, fam("FQ", nxt if added else out, c0, c1))
+                cp(r(new + "L", c0, c1), K)
+                cp(hi, K)
+                tt(lo, K, hi, O.subtract)
 
-    def tl(a, src, m2, step=1):
-        return [(r("%s%d%d" % (a, m2, h)), r(src[1], src[2] + step * h, src[3], 2 * step)) for h in range(2)]
+    def tl(a, src, m2):
+        return [(r("%s%d" % (a, m2), 16 * (1 + m2 - h), 16 * (1 + m2 - h) + 128), r(src[1], src[2] + 16 * h, src[3], 32)) for h in range(2)]
 
-    def choose(K, n, tn, un, rf, q, ev, th):
+    def both(K, o, k, parts):
+        return [p for m2 in range(2) for a, x in parts for p in tl(a, x, m2)], [r(K, o + m2, o + k, 2) for m2 in range(2) for p in range(2 * len(parts))]
+
+    def choose(K, n, tn, un, q, ev, th):
         k = n // 16
-        for B, n0, n1 in K:
+        for B, n0, n1 in [x[:3] for x in K]:
             tr(r(tn, n0, n1), r(B, 128 + n0, 128 + n1))
             scan(r(un, n0, n1), r("MASK", 0, n1 - n0), r(tn, n0, n1), 0.0, O.mult, O.max)
         M = r(un, 15, n, 16)
-        ts(r(rf, 0, k), M, th, 8192.0 if n == 256 else 16384.0, O.is_lt, O.mult)
-        ts(r("T6", 0, k), M, 1.5 * 2.0 ** 29, 1.5 * 2.0 ** 29, O.add, O.subtract)
-        ts(r("T14", 0, k), M, 1.5 * 2.0 ** 37, 1.5 * 2.0 ** 37, O.add, O.subtract)
+        ts(r("T6", 0, k), M, M6, M6, O.add, O.subtract)
+        ts(r("T14", 0, k), M, M14, M14, O.add, O.subtract)
+        ts(r(q, 1, n, 16), M, th, -8192.0, O.is_lt, O.mult)
         tt(r(q, 0, n, 16), M, r("T6", 0, k), O.subtract)
         tt(r(q, 12, n, 16), r("T6", 0, k), r("T14", 0, k), O.subtract)
         tr(r(ev), r(q))
 
-    def settle(n, q, rf, ev, cr, eq, xs, inv):
+    def settle(n, q, ev, eq, xs):
         k = n // 16
-        for m2 in range(2):
-            mm(r("K5", m2, k, 2), ([(r("I8K"), r("INV", m2, k, 2))] if inv else []) + tl("A", r(rf, 0, k), m2)
-               + tl("A", r(q, 0, n), m2, step=16) + tl("A", r(q, 12, n), m2, step=16))
-        if inv:
-            act(r("PW2"), r(q, 12, n, 16), F.Exp, scale=LN2 / 64, bias=col(33))
-            ts(r("L96"), r(q, 0, n, 16), 96.0, None, O.add)
-            tt(r("Q2", 0, n, 16), r("L96"), r("PW2"), O.mult)
-            tr(r("EV2"), r("Q2"))
-            mm(r("K2", 256, 512), [(r("BD"), r("EV2"))])
-            act(r(cr), r("K2", 256, 512))
-            for m2 in range(2):
-                mm(r("K1", m2, k, 2), [(r("IBG"), r("INV", m2, k, 2))] + tl("A", r("RFN"), m2) + tl("A", r("Q2"), m2, step=16))
-            act(r("LB"), r("K1", 0, k))
+        lo, rf, hi = r(q, 0, n), r(q, 1, n), r(q, 12, n)
+        if n == 256:
+            mm(r("K1", n, n + k), [(r("ID"), r("C96"))], stop=False)
+            for K, parts, b in (("K2", [("A", hi)], "BH"), ("K1", [("A", lo), ("A", rf)], "BL")):
+                pairs, outs = both(K, n, k, parts)
+                mm(r(K), pairs, K == "K2", outs=outs, each=2 if K == "K2" else 8)
+                mm(r(K, 0, n), [(r(b), r(ev))])
+            act(r("PW"), r("K2", 0, n + k), F.Exp, scale=LN2 / 64)
+            tt(r("CRB"), r("K1", 0, n + k), r("PW"), O.mult)
+            cr, own = "CRB", lambda m: r("CRB", n + m, n + m + 1)
         else:
+            pairs, outs = both("K3", 0, k, [("A", lo), ("A", rf), ("A", hi)])
+            mm(r("K3"), pairs, outs=outs, each=6)
             mm(r("K3", 256, 256 + n), [(r("BD"), r(ev))])
-            cp(r(cr, 0, n), r("K3", 256, 256 + n))
-        mm(r("K4", 0, n), [(r("ID"), r("NEGM", 0, n))], stop=False)
-        o = 0
+            cp(r("CRUg", 0, n), r("K3", 256, 256 + n))
+            cr, own = "CRUg", lambda m: r("K3", m, m + 1)
+        mm(r("K4", 0, n), [(r("ID"), r("DG", 0, n)), (r("BN"), r(ev))], stop=False)
         for m in range(k):
             w = n - 16 * m
-            ts(r(eq, o, o + w), r(cr, 16 * m, n), r("LB" if inv else "K5", m, m + 1), None, O.is_equal)
-            mm(r("K4", 16 * m, 16 * m + 16), [(r("BW"), r(eq, o, o + 16))], start=False, stop=False)
+            ts(blk(eq, m, m + 1, 0, w), r(cr, 16 * m, n), own(m), None, O.is_equal)
             if w > 16:
-                mm(r("K4", 16 * m + 16, n), [(r("B4"), r(eq, o + 16, o + w))], start=False, stop=False)
-            o += w
-        mm(r("K4", 0, n), [(r("ID"), r("POSM", 0, n))], start=False)
-        scan(r("UX", 0, n), r("MASK", 0, n), r("K4", 0, n), 0.0, O.mult, O.max)
-        if inv:
-            tt(r("Z2", 0, k), r("UX", 15, n, 16), r("K5", 0, k), O.max)
-            tt(r("Z3", 0, k), r("Z2", 0, k), r("DUMP", 0, k), O.min)
-            ts(r("POSS", 0, k), r("Z3", 0, k), -4096.0, None, O.add)
-        else:
-            tt(r("Z2", 0, k), r("K5", 0, k), r("DUMP", 0, k), O.min)
-            ts(r("Z3", 0, k), r("Z2", 0, k), -4096.0, None, O.add)
-            for m in range(k):
-                ts(r("POSS", m, m + 1), r("UX", 16 * m + 15, 16 * m + 16), r("DG2", 16 + m, 17 + m), r("Z3", m, m + 1), O.min, O.max)
+                mm(r("K4", 16 * m + 16, n), [(r("BO"), blk(eq, m, m + 1, 16, w))], start=False, stop=False)
+            if m % 8 == 7 or m == k - 1:
+                a = m - m % 8
+                mm(r("K4", 16 * a, 16 * m + 16), [(r("LTN"), blk(eq, a, m + 1, 0, 16))], start=False, stop=m == k - 1)
+        scan(r("UX", 0, n), r("DMP", 0, n), r("K4", 0, n), 4 * BIG, O.min, O.max)
+        ts(r("POSS", 0, k), r("UX", 15, n, 16), -1.0, float(TOP), O.mult, O.add)
         cp(ind(r("S"), r("POSS", 0, k)), xs)
 
-    def signs(n, banks, xs, gt, cm, K):
-        per = 512 // n
-        for j, B in enumerate(banks[:(15 + per) // per]):
-            ks = range(per * j, min(16, per * j + per))
-            mm(r(B), [p for k in ks for p in ((r("ID"), xs), (r("IM1"), r(gt, k, 16 * n, 16)))], each=2,
-               outs=[r(B, n * (k - ks[0]), n * (k - ks[0] + 1)) for k in ks for p in range(2)])
-            act(r(cm, n * ks[0], n * ks[-1] + n), r(B, 0, n * len(ks)), F.Sign, bias=col(16))
-            mm(K, [(one("HC", k), r(cm, n * k, n * k + n)) for k in ks], start=False, stop=ks[-1] == 15)
+    def diff(B, w, x, s, how):
+        xs, outs = [(r("ID"), x)] * 8, [r(B, k, w, 8) for k in range(8)]
+        if how == 0:
+            mm(r(B, 0, w), [(r("IM1"), s)], stop=False)
+            mm(r(B), xs, start=False, outs=outs)
+        else:
+            if how == 1:
+                mm(r(B, 0, w), [(r("ID"), r("ZR", 0, w))], stop=False)
+            mm(r(B), xs, start=how == 2, stop=False, outs=outs)
+            mm(r(B, 0, w), [(r("IM1"), s)], start=False)
 
     def guests(t):
-        gr, gx = "GR%d" % t, "GX%d" % t
+        gr, gx = r("GR%d" % t, 0, 4), "GX%d" % t
         act(r("CAG", 0, 256), ind(r("CT"), r("GN%d" % t)))
-        cp(r("NGU"), r(gr))
-        mm(r("K3", 64, 68), fam("CNT", gr, 0, 4))
-        ts(r("NL", 0, 4), r("K3", 64, 68), 1 / (16 * U), None, O.mult)
-        act(r("XGE"), ind(r(gx), r("NGU")))
-        cp(r("CgL"), ind(r("CAG"), r("NL", 0, 4)))
-        act(r("CSg"), ind(r("CAG"), r("NL", 0, 4)), F.Identity, bias=col(20))
-        act(r("XG"), ind(r(gx), r("NL", 0, 4)))
+        cp(r("CgL"), ind(r("CAG"), gr))
+        act(r("XG"), ind(r(gx), gr))
+        act(r("CSg"), ind(r("CAG"), gr), F.Identity, bias=col(20))
         mm(r("K3", 128, 192), [(r("IDF"), r("CSg"))], stop=False)
-        tt(r("CMg"), ind(r("S", 0, 4096), r("CgL")), r("XGE"), O.is_lt)
-        mm(r("K3", 128, 192), fam("CNT", "CMg", 0, 64), start=False)
-        choose([("K3", 0, 64)], 64, "TRg", "UUg", "RFg", "Qg", "EVg", r("TH", t, t + 1))
-        settle(64, "Qg", "RFg", "EVg", "CRUg", "EQg", r("XG"), False)
+        for h in range(2):
+            copy(GQ[h], r("GTg", 512 * h, 512 * h + 512), ind(r("S"), r("CgL", 32 * h, 32 * h + 32)))
+        for h, B in enumerate(("K1", "K2")):
+            c = (512 * h, 512 * h + 512)
+            diff(B, 512, r("XG"), r("GTg", h, 1024, 2), ZG)
+            if h and GQ[2] == "v":
+                ts(r("CMg", *c), r(B), 0.0, 2.0, O.is_gt, O.mult)
+            else:
+                act(r("CMg", *c), r(B), F.Sign, bias=col(16))
+        for h in (1, 0):
+            mm(r("K3", 128, 192), [(one("HC", 2 * k + h), r("CMg", 512 * h + k, 512 * h + 512, 8)) for k in range(8)], start=False, stop=h == 0)
+        choose([("K3", 0, 64)], 64, "TRg", "UUg", "Qg", "EVg", r("TH", t, t + 1))
+        settle(64, "Qg", "EVg", "EQg", r("XG"))
 
     for t in range(RO):
         more = t < RO - 1
         if t == 0:
             for i in range(16):
-                cp(r("E", F0 + i, NW, 16), r("WP", 209 * i, 209 * i + 208))
-            for n in ("E1", "E2"):
-                cp(r(n, G0, NW), r("E", G0, NW))
+                ts(r("E", i, RT, 16), r("WP", 209 * i, 209 * i + 208), r("CB", 0, 1), None, O.mult)
+            ts(r("E", RT, NW), r("ZR", 0, NW - RT), col(5), None, O.add)
+            ts(r("E1", G0, NW), r("E", G0, NW), r("CB", 1, 2), None, O.add)
+            cp(r("E2", G0, NW), r("E", G0, NW))
         who = LV if t else LV0
-        level("E" if t else "WP", "P1L" if t else "PL", "G1", who[0], "E1", "E", "IDM", "SH1", 2, 4)
-        if t:
-            rows("E2", 2, "G1", 0, 4, 0, 0, 160)
-        lists("G1", 0, "P2L")
-        level("E1", "P2L", "G2", who[1], "E2", "E1", "EV0", "SH2", 1, 2)
-        lists("G2", 0, "P4L")
+        level(t, "E" if t else "WP", "P1L" if t else "PL", "G1", who[0], "E1", "E", 4, "P2", MA if t else ())
+        level(t, "E1", "P2L", "G2", who[1], "E2", "E1", 2, "P4", MC if t else MC0)
         for B, c in zip(BK, CD):
-            mm(r(B, 128, 128 + c[1] - c[0]), fam("CNT", "E2", *c, F0), stop=False)
-        level("E2", "P4L", "G3", who[2])
+            mm(r(B, 128, 128 + c[1] - c[0]), fam("FS", "E2", *c), stop=False)
+        level(t, "E2", "P4L", "G3", who[2])
         for B, c in zip(BK, CD):
             K = r(B, 128, 128 + c[1] - c[0])
-            mm(K, fam("CNT", "G3", *c), start=False)
-            ts(r("DI", *c), K, 1 / U, None, O.mult)
+            mm(K, fam("FS", "G3", *c), start=False)
+            cp(r("DI", *c), K)
             ts(r("DM", *c), r("DI", *c), 4095, None, O.bitwise_and)
             cp(r("DL", *c), r("DM", *c))
-        cp(r("DH"), r("DM"))
+        ts(r("DH"), r("DM"), M6, M6, O.add, O.subtract)
         tt(r("DLO"), r("DM"), r("DH"), O.subtract)
         if t == 0:
             for b in (4, 5, 6, 7, 0, 1, 2, 3):
@@ -547,11 +591,12 @@ def rank_program(g, core, T, topo):
                 e = topo.engines(core, dst)
                 tls.append(RemoteDMATransfer(src=T.GD[:, 256 * d - 256:256 * d], dst=T[la][:, 256 * d - 256:256 * d], dst_ids=[DstId(rid=rid, pnc=pid)],
                                              dma_engine_mask=(1 << e[d - 1]) | (1 << e[d + 3]), remote_sem=T.sem["ga%d" % t]))
-            send(lambda tls=tls, t=t: G.remote_dma_fused(tls, local_sem=T.sem["gl%d" % t]), r("GD"), r(la), "gl%d" % t, "ga%d" % t, 6, 2 * REMOTE)
+            send(lambda tls=tls, t=t: G.remote_dma_fused(tls, local_sem=T.sem["gl%d" % t]), r("GD"), r(la), "gl%d" % t, "ga%d" % t, 6,
+                 2 * REMOTE + (0 if t else FIRST))
             for n in ("E", "E1", "E2"):
-                dma("y", rp(n, 0, 4, G0, NW), rp(la, 0, 4, 0, 768))
-        W = r("S", 0, 4096)
-        for j, (K, (c0, c1)) in enumerate(zip(("K1", "K2"), CS_)):
+                dma("y", rp(n, 0, 4, G0, RT), rp(la, 0, 4, 0, 768))
+        W = r("S")
+        for j, (K, (c0, c1)) in enumerate(zip(("K1", "K2", "K5"), CS_)):
             gt, K = r("GT", 512 * j, 512 * j + 16 * (c1 - c0)), r(K, 0, 16 * (c1 - c0))
             act(gt, ind(W, r("DL", c0, c1)))
             mm(K, [(r("ID"), r("X", 16 * c0, 16 * c1))], stop=False)
@@ -564,8 +609,8 @@ def rank_program(g, core, T, topo):
             mm(K, fam("CNT" if c[0] else "HC", "CM", *c))
             ts(r("BT", *c), K, (4.5 if c[0] else -3.5) * U, None, O.is_lt)
         for c in range(0, 160, 32):
-            copy("v" if t == 0 and c % 64 else "s", r("CA", 16 * c, 16 * c + 512), ind(r("CT"), r("DL", c, c + 32)))
-        scan(r("RS", 1, 161), r("ON160"), r("BT"), 0.0, O.mult, O.add)
+            copy("s" if t else CAQ[c // 32], r("CA", 16 * c, 16 * c + 512), ind(r("CT"), r("DL", c, c + 32)))
+        scan(r("RS", 1, 161), r("ON", 0, 160), r("BT"), 0.0, O.mult, O.add)
         ends = r("K3", 0, 8)[1:]
         mm((T.K3[0:80, 0:8],) + ends, [(r("RS", 2, 161, 2), r("B16", 0, 128, 16))])
         mm(r("K4", 0, 160), [(r("B16"), r("RS", 0, 160)), (r("LE"), r("BT"))])
@@ -588,79 +633,71 @@ def rank_program(g, core, T, topo):
             tt(r("EQS", 256 * h, 256 * h + 256), ind(r("RKM"), r("CL", 16 * h, 16 * h + 16)), r("N1F"), O.is_equal)
             mm(r("K3", 48, 64), ([] if h else [(r("ID"), r("C32v"))]) + fam(("FV", "FW")[h], "EQS", 16 * h, 16 * h + 16), h == 0, h == 1)
         cp(r("VL"), r("K3", 48, 64))
-        act(r("VF"), r("K3", 48, 64), F.Identity, bias=col(17))
+        act(r("VF"), r("K3", 48, 64))
         cp(r("XS"), ind(r("X"), r("VL")))
-        cp(r("CAN", 0, NS), ind(r("CA"), r("VL", 0, NS // 16)))
-        cp(r("CAN", NS, 256), ind(r("CA"), r("VL", NS // 16, 16)))
-        act(r("VC1"), r("VF"), F.Identity, scale=1 / 16, bias=col(30))
-        act(r("VC1"), r("VC1"), F.Identity, bias=col(28))
-        act(r("VC2"), r("VC1"), F.Identity, bias=col(29))
-        mm(r("K7", 0, 16), [(r("I160"), r("VF")), (r("IM25"), r("VC2"))])
-        ts(r("VP"), r("K7", 0, 16), -2560.0, None, O.add)
-        act(r("DS"), ind(r("DR"), r("VP")))
-        mm(r("K7", 16, 32), fam("CNT", "DS", 0, 16))
-        ts(r("DNL"), r("K7", 16, 32), 1 / U, None, O.mult)
-        mm(r("K0", 0, 16), [(r("IDF"), r("VF")), (r("I768"), r("INV"))], stop=False)
+        for a, b in CANP:
+            ts(r("CAN", a, b), ind(r("CA"), r("VL", a // 16, b // 16)), float(FAR), None, O.min)
+        mm(r("K0", 0, 16), [(r("IDF"), r("VF")), (r("I768"), r("INV")), (r("ID"), r("JJ"))], stop=False)
         visit(t, r("XS"), "GX", 2 * REMOTE)
-        visit(t, r("DNL"), "GN", REMOTE)
         for k in range(16):
             cp(r("XE", k, 16 * (256 - NS), 16), r("XS", NS, 256))
-        keys = [act(r("CS", n0, n1), ind(r("CA"), r("VL", n0 // 16, n1 // 16)), F.Identity, bias=col(c)) for n0, n1, c in ((NS, 256, 18), (0, NS, 19))]
-        act(r("GT", 0, 16 * NS), ind(W, r("CAN", 0, NS)), after=keys)
-        for B, n0, n1 in CN[:-1]:
+        keys = [act(r("CS"), ind(r("CA"), r("VL")), F.Identity, bias=col(21))]
+        for Bs, n0, n1 in SS:
+            w = 8 * (n1 - n0)
+            act(r("GC", 16 * n0, 16 * n1), ind(W, r("CAN", n0, n1)), after=keys)
+            for h, B in enumerate(Bs):
+                diff(B, w, r("XS", n0, n1), r("GC", 16 * n0 + h, 16 * n1, 2), ZS)
+                act(r("CM", 16 * n0 + w * h, 16 * n0 + w * h + w), r(B, 0, w), F.Sign, bias=col(16))
+        for n0, n1 in SV:
             tt(r("CM", 16 * n0, 16 * n1), ind(W, r("CAN", n0, n1)), r("XE", 16 * (n0 - NS), 16 * (n1 - NS)), O.is_lt)
-        for B, n0, n1 in CN:
+        for B, n0, n1, parts in CN:
             K = r(B, 128 + n0, 128 + n1)
-            mm(K, [(r("IDF"), r("CS", n0, n1)), (r("B32"), r("EQS", n0, n1)), (r("B32"), r("EQS", 256 + n0, 256 + n1))], stop=False)
-            if n0:
-                mm(K, fam("CNT", "CM", n0, n1), start=False)
-            else:
-                signs(NS, ("K1", "K2", "K3", "K1"), r("XS", 0, NS), "GT", "CM", K)
-        choose(CN, 256, "TR", "UU", "RF", "Q", "EV", r("TH", t, t + 1))
-        mm(r("K0", 0, 16), tl("H", r("RF"), 0) + tl("H", r("RF"), 1) + [(r("ID"), r("JJ"))], start=False,
-           outs=[r("K0", 0, 16, 2)] * 2 + [r("K0", 1, 16, 2)] * 2 + [r("K0", 0, 16)])
+            mm(K, [(r("IDF"), r("CS", n0, n1))] + [(r("ID"), r("C8", n0, n1))] * (n0 < NS), stop=False)
+            for a, b in parts:
+                w, end = 8 * (b - a), (a, b) == parts[-1]
+                if a >= NS:
+                    mm(r(B, 128 + a, 128 + b), fam("CNT", "CM", a, b), start=False, stop=end)
+                for h in range(2 * (a < NS)):
+                    o = 16 * a + w * h
+                    mm(r(B, 128 + a, 128 + b), [(one("HC", 2 * k + h), r("CM", o + k, o + w, 8)) for k in range(8)], start=False, stop=end and h == 1)
+        ts(r("VC1"), r("VF"), 1 / 16, -7.5 / 16, O.mult, O.add)
+        ts(r("VC2"), r("VC1"), M0, M0, O.add, O.subtract)
+        mm(r(VB, 0, 16), [(r("I160"), r("VF")), (r("IM25"), r("VC2"))])
+        cp(r("VP"), r(VB, 0, 16))
+        copy(DQ, r("DS"), ind(r("DR"), r("VP")))
+        mm(r(VB, 16, 32), fam("FS", "DS", 0, 16))
+        cp(r("DNL"), r(VB, 16, 32))
+        visit(t, r("DNL"), "GN", REMOTE)
+        choose(CN, 256, "TR", "UU", "Q", "EV", r("TH", t, t + 1))
+        pairs, outs = both("K0", 0, 16, [("H", r("Q", 1, 256))])
+        mm(r("K0"), pairs, start=False, outs=outs)
         cp(r("POSE"), r("K0", 0, 16))
         cp(ind(r("E"), r("POSE")), r("EV"))
+        for B, c in zip(BK, CP if more else ()):
+            mm(r(B, 0, c[1] - c[0]), fam("FP", "E", *c))
+            cp(r("P1L", *c), r(B, 0, c[1] - c[0]))
+        mm(r("K3", 0, 256), [(r("BR"), r("EV"))])
+        scan(r("CUM"), r("ON"), r("K3", 0, 256), 0.0, O.mult, O.add)
+        for m in range(4):
+            act(r("JK", 256 * m, 256 * m + 256), r("CUM"), F.Sign, bias=r("NLB", m, m + 1), total=r("AC", m, m + 1))
+        ts(r("NG", 0, 4), r("AC", 0, 4), -0.5, 128.0, O.mult, O.add)
+        visit(t, r("NG"), "GR", REMOTE)
+        settle(256, "Q", "EV", "EQ", r("XS"))
         if more:
-            for n in ("E1", "E2"):
-                rows(n, 0, "E", 0, 4, F0, 0, 160)
-            lists("E", F0, "P1L")
-        for m2 in range(2):
-            mm(r("K3", m2, 16, 2), tl("A", r("RF"), m2))
-        scan(r("RR", 1, 17), r("ON160", 0, 16), r("K3", 0, 16), 0.0, O.mult, O.add)
-        a, b = r("RR", 1, 17), r("RR", 0, 16)
-        mm(r("K3", 16, 32), [(r("LTS"), a), (r("UBS"), b), (r("IDN"), a), (r("IDB"), b)])
-        tt(r("PM"), r("K3", 16, 32), r("DG2", 0, 16), O.min)
-        ts(r("POSG"), r("PM"), 1024.0, None, O.add)
-        act(r("NG", 0, 64), r("NONE"))
-        cp(ind(r("NG"), r("POSG")), r("N0"))
-        visit(t, r("NG", 0, 64), "GR", REMOTE)
-        ts(r("RFN"), r("UU", 15, 256, 16), r("TH", t, t + 1), -2.0 ** 90, O.is_lt, O.mult)
-        settle(256, "Q", "RF", "EV", "CRB", "EQ", r("XS"), True)
-        if more:
-            mm(r("K5", 40, 41), [(r("ONES"), r("RR", 16, 17)), (r("SEL0"), r("MT", 0, 1))])
-            cp(r("HI", 0, 1), r("K5", 40, 41))
+            mm(r("K3", 400, 401), [(r("SEL0"), r("CUM", 255, 256)), (r("SEL0"), r("MT", 0, 1))])
+            cp(r("HI", 0, 1), r("K3", 400, 401))
             ts(r("HI", 1, 2), r("HI", 0, 1), 1, None, O.bitwise_and)
             ts(r("TH", t + 1, t + 2), r("HI", 1, 2), U, 9 * U, O.mult, O.add)
-        if t == 0:
-            ts(col(6), col(5), -1 / 4096, col(10), O.mult, O.add)
-            ts(col(6), col(6), 1 / U, None, O.mult)
-            scaled(r("FD"), r("CNT"), col(6), "s")
-        if not more:
+        else:
             for c in range(8):
-                mm(r("K1", 0, 320), [(one(f, 2 * c + k), r("E", F0 + 320 * c, F0 + 320 * c + 320)) for k, f in enumerate(("FD", "FP"))], c == 0, c == 7)
-            ts(col(23), col(26), -3344.0, 3344.0, O.mult, O.add)
-            ts(col(27), col(26), 16.0, -16.0, O.mult, O.add)
-            act(r("CA", 640, 960), r("K1", 0, 320))
-            for c in range(0, 320, 80):
-                ts(r("CA", c, c + 80), r("CA", 640 + c, 720 + c), 0.5, col(23), O.is_lt, O.mult)
-                ts(r("CA", 320 + c, 400 + c), r("CA", 640 + c, 720 + c), 0.0, col(27), O.max, O.add)
-                tt(r("OUT", c, c + 80), r("CA", c, c + 80), r("CA", 320 + c, 400 + c), O.add)
+                mm(r("K7", 0, 320), [(one(f, 2 * c + k), r("E", 320 * c, 320 * c + 320)) for k, f in enumerate(("FD", "FP"))], c == 0, c == 7)
+            act(r("OUT"), r("K7", 0, 320))
             dma("y", hbm("yof"), rp("OUT", 0, 2, 0, 320))
             dma("y", hbm("yan"), rp("OUT", 1, 2, 0, 320))
         guests(t)
     dma("y", hbm("ys"), r("S", 0, 4096))
 
+    every = range(len(calls))
     lead = [LOCAL if c["sem"] == "local" else 0.0 for c in calls]
     res = ["dma" if c["sem"] == "local" else c["q"] for c in calls]
     hold = [c["cost"] - LOCAL if c["sem"] == "local" else c["hold"] for c in calls]
@@ -671,34 +708,112 @@ def rank_program(g, core, T, topo):
             fwd[i].append((d, lag))
             bwd[d].append((i, lag + hold[i] - hold[d]))
 
-    def place(turn, before, first):
-        taken, at = {}, [0.0] * len(calls)
-        for i in turn:
-            x, L = max([at[d] + lag for d, lag in before[i]] + [first[i]]), taken.setdefault(res[i], [])
-            k, step = 0, 1024
-            while step:
-                if k + step <= len(L) and L[k + step - 1][1] <= x:
-                    k += step
-                else:
-                    step //= 2
-            while res[i] and k < len(L) and x + hold[i] > L[k][0]:
-                x = max(x, L[k][1])
-                k += 1
-            L.insert(k, (x, x + hold[i]))
+    def place(key, before, first):
+        ahead = before is fwd
+        key = [key[group[i][0 if ahead else 1]] if i in group else key[i] for i in every]
+        for i in (reversed(every) if ahead else every):
+            x = key[i] + 1e-7
+            for d, lag in before[i]:
+                if key[d] < x:
+                    key[d] = x
+        taken, at = {q: ([], []) for q in res}, [0.0] * len(calls)
+        for i in sorted(every, key=lambda i: -key[i]):
+            x = first[i]
+            for d, lag in before[i]:
+                if at[d] + lag > x:
+                    x = at[d] + lag
+            if res[i]:
+                A, B = taken[res[i]]
+                k, h = len(B), hold[i]
+                while k and B[k - 1] > x:
+                    k -= 1
+                while k < len(B) and x + h > A[k]:
+                    x = B[k] if B[k] > x else x
+                    k += 1
+                A.insert(k, x)
+                B.insert(k, x + h)
             at[i] = x
         return at
-    way = [0.0] * len(calls)
-    for i in range(len(calls) - 1, -1, -1):
-        way[i] = max([way[j] + lag - hold[j] + hold[i] for j, lag in bwd[i]] + [hold[i]])
-    every = range(len(calls))
-    at = place(sorted(every, key=lambda i: (-way[i], i)), fwd, lead)
-    for sweep in range(SWEEPS):
-        back = place(sorted(every, key=lambda i: (-at[i] - hold[i], -i)), bwd, [0.0] * len(calls))
-        at = place(sorted(every, key=lambda i: (-back[i] - hold[i], i)), fwd, lead)
-    order = sorted(every, key=lambda i: at[i] - lead[i])
+
+    def sweep(at):
+        back = place([at[i] + hold[i] for i in every], bwd, [0.0] * len(calls))
+        return place([back[i] + hold[i] for i in every], fwd, lead)
+
+    def span(at):
+        return max(at[i] - lead[i] + calls[i]["cost"] for i in every)
+
+    def score(at):
+        return span(at) + MEAN * sum(at) / len(at)
+
+    twin = {}
+
+    def ahead(key, at, p, i):
+        for j in twin[calls[i]["name"]]:
+            near = min(twin[calls[p]["name"]], key=lambda k: abs(at[j] - at[k] - at[i] + at[p]))
+            if abs(at[j] - at[near] - at[i] + at[p]) < 3 and key[j] < key[near]:
+                key[group.get(j, (j,))[0]] = key[group.get(near, (near,))[0]] + 1e-5
+
+    if not ORDER:
+        way = [0.0] * len(calls)
+        for i in reversed(every):
+            way[i] = max([way[j] + lag - hold[j] + hold[i] for j, lag in bwd[i]] + [hold[i]])
+        at = kept = sweep(place(way, fwd, lead))
+        tried, left, best = set(), PASSES, score(at)
+        for i, c in enumerate(calls):
+            twin.setdefault(c["name"], []).append(i)
+        while left > 0:
+            turn, tail, nxt, prev = sorted(every, key=lambda i: at[i]), [0.0] * len(calls), {}, {}
+            for i in reversed(turn):
+                n = nxt.get(res[i]) if res[i] else None
+                tail[i] = max([calls[i]["cost"] - lead[i]] + [tail[j] + lag - hold[j] + hold[i] for j, lag in bwd[i]]
+                              + ([hold[i] + tail[n]] if n is not None else []))
+                if n is not None:
+                    prev[n] = i
+                nxt[res[i]] = i
+            end, swaps = span(at), []
+            for i in turn:
+                ready = max([at[d] + lag for d, lag in fwd[i]] + [lead[i]])
+                if res[i] and at[i] - ready > 0.03 and end - at[i] - tail[i] < NEAR:
+                    p = prev[i]
+                    swaps.append((end - at[i] - tail[i] - min(hold[p], at[i] - ready), p, i))
+                    while p in prev and at[p] > ready:
+                        p = prev[p]
+                    swaps.append((end - at[i] - tail[i] - (at[i] - ready), p, i))
+            new = [x for x in sorted(swaps) if (calls[x[1]]["name"], calls[x[2]]["name"]) not in tried]
+            if not new:
+                key, tried, left = [-v for v in at], set(), left - 1
+                for k in range(KICK if swaps else 0):
+                    x, p, i = swaps[(7919 * left + 104729 * k) % len(swaps)]
+                    ahead(key, at, p, i)
+                at = sweep(place(key, fwd, lead))
+                best = score(at)
+            for x, p, i in new[:6]:
+                pair = (calls[p]["name"], calls[i]["name"])
+                if pair in tried:
+                    continue
+                tried.add(pair)
+                left -= 1
+                key = [-v for v in at]
+                ahead(key, at, p, i)
+                a2 = place(key, fwd, lead)
+                s2 = score(a2)
+                if best - 1e-4 < s2 < best + SLACK:
+                    a2 = sweep(a2)
+                    s2 = score(a2)
+                if s2 < best - 1e-4:
+                    if s2 < best - 0.05:
+                        tried = set()
+                    at, best = a2, s2
+                    break
+            if best < score(kept):
+                kept = at
+            elif best > score(kept) + 1.0:
+                at, best = kept, score(kept)
+        ORDER.append(sorted(every, key=lambda i: kept[i] - lead[i]))
+        ORDER.append(span(kept))
 
     cnt, known, nd = {"cv": 0, "cs": 0, "cp": 0, "cg": 0}, {q: {} for q in QU}, 0
-    for i in order:
+    for i in ORDER[0]:
         c = calls[i]
         q = c["q"]
         if q is None:

import math
from concourse.bass import DstId, RemoteDMATransfer
from concourse.mybir import AluOpType as O, ActivationFunctionType as F, AxisListType as AX

RO = 4
LN2 = 0.6931471805599453
U = 2.0 ** 18
BIG = 2.0 ** 20
M0, M6, M14 = 1.5 * 2.0 ** 23, 1.5 * 2.0 ** 29, 1.5 * 2.0 ** 37
G0, RT, NW = 2560, 3328, 3344
TOP, FAR = 4416, 4360
L0A = (("s", 0, 32, "s"), ("s", 32, 64, "s"), ("v", 64, 112, "a"), ("v", 112, 160, "a"))
L0C = (("s", 0, 48, ""), ("v", 48, 80, ""), ("s", 80, 112, ""), ("v", 112, 160, ""))
NA = 80
LA = (("s", 0, 48, 0), ("s", 48, 80, 48)) + tuple(("v", c, c + 16, "a") for c in range(NA, 160, 16))
LB = LA
LC = (("s", 0, 48, ""), ("v", 48, 80, ""), ("s", 80, 144, ""), ("v", 144, 160, ""))
LV0, LV = (L0A, L0A, L0C), (LA, LB, LC)
MB = ("K5", "K5")
MA = ((80, 160), (0, 80))
MC = ((80, 112), (112, 160), (0, 80))
MC0 = ((64, 112), (112, 160))
CH0 = ((0, 64), (64, 112), (112, 160))
CH = ((0, 80), (80, 128), (128, 160))
CH4 = CH
CP = ((0, 96), (96, 160))
CD = ((0, 80), (80, 160))
CS_ = ((0, 32), (32, 64))
CV = ((64, 112), (112, 160))
CC = ((0, 64), (64, 112), (112, 160))
NS = 128
SS = ((("K1", "K2"), 0, 64), (("K3", "K7"), 64, 128))
SV = ((128, 192), (192, 256))
CN = (("K4", 128, 192, ((128, 192),)), ("K5", 192, 256, ((192, 256),)), ("K6", 0, 128, ((0, 64), (64, 128))))
CANP = ((0, 128), (128, 256))
VB = "K1"
DQ = "s"
WS = 2048
ZS = 2
ZG = 2
GQ = "svv"
CTQ = "vsssssvv"
CAQ = "sssvs"
LOADS = (("WK", "wk", 2048, 4096), ("S", "s0", 0, 4096), ("X", "x", 0, 2560), ("WK", "wk", 0, 2048))
EARLY = 3
FAMS = "CNT HC FS FF FP FQ FD FV FW".split()
PIECE = 8
PASSES = 2000
ORDER = []
SCRATCH, PACK = {}, {}
WIDE = {"float32": 4, "bfloat16": 2, "int32": 4, "uint16": 2}
FILL = dict.fromkeys(WIDE, 0)
OWN = "AN WK X S OF SNDI WP ST E E1 E2 G1 G2 DR GD NG XS DNL OUT ONE B16 R2 CR DH DLO EN".split()


def _b(names, cols, d="float32", w="sbuf"):
    for n in names.split():
        if w == "psum" or n in OWN or n[:2] in ("LA", "GR", "GX", "GN"):
            SCRATCH[n] = (w, [128, cols], d)
        else:
            PACK[n] = ("pk_" + d, FILL[d], cols)
            FILL[d] += (cols + 15) // 16 * 16
            SCRATCH["pk_" + d] = ("sbuf", [128, FILL[d]], d)


_b("K0 K1 K2 K3 K4 K5 K6 K7", 512, "float32", "psum")
_b("FAM", 144 * len(FAMS), "bfloat16")
_b("ONE B16 ID IM1 LT LE M16b I7 IM2K BD BH BL BN BR BO LTN SEL0 I768", 128, "bfloat16")
_b("A0 A1 H0 H1", 160, "bfloat16")
_b("M16 IDF I160 IM25", 128)
SCRATCH["C1"] = ("sbuf", [128, 16, 128], "bfloat16")
SCRATCH["N1B"] = ("sbuf", [128, 16, 16], "bfloat16")
SCRATCH["EQ"] = ("sbuf", [128, 16, 256], "bfloat16")
SCRATCH["EQg"] = ("sbuf", [128, 4, 64], "bfloat16")
_b("E", 4096 + 2560 + 16, "bfloat16")
_b("E1 E2 WP", NW, "bfloat16")
_b("G1 G2 G3 DR XE", 2560, "bfloat16")
_b("GC", 16 * NS, "bfloat16")
_b("X", 2576, "bfloat16")
_b("S", 4368, "bfloat16")
_b("WK CM", 4096, "bfloat16")
_b("CT", 4096)
_b("ST", 4 * 224, "bfloat16")
_b("DS EV Q DG XS CUM C8", 256, "bfloat16")
_b("CRB PW", 272, "bfloat16")
_b("R2 SG0 SG1 ZR EQS", 512, "bfloat16")
_b("N1F MASK CS TR UU UX DMP ON", 256)
_b("CAG", 272)
_b("CA", 2576)
_b("W1", 160)
_b("RKM", 176)
_b("CO", 64)
_b("TH VC1 VC2 VF NL0 NL1 NLB T14 T6 MD AC", 16)
_b("CSg TRg UUg", 64)
_b("PI YI HI", 16, "int32")
_b("AN LOI SHI PLI DI DM", 160, "int32")
_b("OF", 208, "int32")
_b("SNDI SA SB", 48, "int32")
_b("BT DH DLO P2H P2W P4H P4W", 160, "bfloat16")
_b("RS", 176, "bfloat16")
_b("C32v CB INV JJ MT C96", 16, "bfloat16")
_b("EN", 8, "bfloat16")
_b("Qg EVg XG", 64, "bfloat16")
_b("GD", 768, "bfloat16")
_b("GTg CMg JK CR", 1024, "bfloat16")
_b("GT", 1536, "bfloat16")
_b("PL P1L P2L P4L DL", 160, "uint16")
_b("DNL VP VL POSE POSS NG", 16, "uint16")
_b("CL", 32, "uint16")
_b("SL CgL CRUg", 64, "uint16")
_b("CAN", 256, "uint16")
_b("OUT", 320)
for _t in range(RO):
    _b("GR%d" % _t, 16, "uint16")
    _b("GX%d" % _t, 272, "bfloat16")
    _b("GN%d" % _t, 16, "uint16")
    if _t < RO - 1:
        _b("LA%d" % _t, 768, "bfloat16")

SEMAPHORES = ["cv", "cs", "cp", "cg"] + ["d%d" % k for k in range(110)] + \
    ["%s%d" % (k, t) for k in ("ga", "gl", "GRa", "GRl", "GXa", "GXl", "GNa", "GNl") for t in range(RO)]

CYC = 0.001
PE = 0.0005
GAT = 1.17
SCA = 2.3
WAKE = 0.18
LOCAL = 1.6
RATE = 190e3
REMOTE = 2.3
FIRST = 3.0
MEAN = 0.05
NEAR = 0.5
KICK = 3
SLACK = 0.5


def rank_program(g, core, T, topo):
    rank = T.rank_of(core)
    if rank is None:
        return
    N = len(T.cores)
    V, S, P, G = g.vector, g.scalar, g.tensor, g
    QU = {"v": V, "s": S, "p": P, "g": G, "y": g.sync}
    acc, bank, calls, group = {}, {}, [], {}

    def r(name, lo=0, hi=None, step=1):
        ph, o, w = PACK.get(name, (name, 0, None))
        if hi is None:
            hi = w or T[name].shape[1]
        ap = T[ph][:, o + lo:o + hi:step] if step > 1 else T[ph][:, o + lo:o + hi]
        return (ap, name, lo, hi, step, lo % step, None, (hi - lo + step - 1) // step, WIDE[SCRATCH[ph][2]], 128)

    def blk(name, a, b, lo, hi):
        w = T[name].shape[2]
        ap = T[name][:, a, lo:hi] if b == a + 1 else T[name][:, a:b, lo:hi]
        return (ap, name, w * a + lo, w * (b - 1) + hi, 1, 0, None, (b - a) * (hi - lo), WIDE[SCRATCH[name][2]], 128)

    def rp(name, row, step, lo, hi, part=None):
        return (T[name][row::step, lo:hi], name, lo, hi, 1, 0, part, hi - lo, WIDE[SCRATCH[name][2]], 128 // step)

    def part(name, a, b, lo, hi):
        return (T[name][a:b, lo:hi], name, lo, hi, 1, 0, a, hi - lo, 2, b - a)

    def hbm(name, lo=None, hi=None):
        return (T[name][:] if lo is None else T[name][:, lo:hi], name, lo or 0, hi or 1, 1, 0, None, 1, 0, 0)

    def ind(win, off):
        return (win[0].indirect(off[0]), [win, off], 16 * off[7])

    def col(c):
        return r("CO", c, c + 1)

    def flat(*xs):
        o = []
        for x in xs:
            if not (x is None or isinstance(x, (int, float))):
                o += list(x[1]) if isinstance(x[1], list) else [x]
        return o

    def lap(a, b):
        if a[1] <= b[0] or b[1] <= a[0] or (a[3] - b[3]) % math.gcd(a[2], b[2]):
            return False
        return a[4] is None or b[4] is None or a[4] == b[4]

    def op(q, call, reads, writes, cost, sem=None, after=(), hold=None):
        me, deps = len(calls), dict.fromkeys(after, 0)
        both = [(x, 0) for x in reads] + [(x, 1) for x in writes]
        for R, isw in both:
            if R[1][0] == "K":
                for qq, e in bank.get(R[1], {}).items():
                    deps[e] = max(deps.get(e, 0), int(qq != q))
            else:
                for a in acc.get(R[1], []):
                    if (isw or a[1]) and lap(a[0], R[2:7]):
                        deps[a[2]] = 1
        name = (q,) + tuple((x[1][:2] if x[1][:2] in ("GR", "GX", "GN", "LA") else x[1], 0 if x[1] == "TH" else x[2]) for x in writes + reads)
        calls.append({"q": q, "call": call, "deps": deps, "cost": cost, "sem": sem, "hold": cost if hold is None else hold, "name": name})
        for R, isw in both:
            if R[1][0] == "K":
                bank.setdefault(R[1], {})[q] = me
                continue
            reg, L = R[2:7], acc.get(R[1], [])
            if isw and reg[2] == 1 and reg[4] is None and R[9] == 128:
                L = [a for a in L if not (reg[0] <= a[0][0] and a[0][1] <= reg[1])]
            acc[R[1]] = L + [(reg, isw, me)]
        return me

    def ap(x):
        return x if x is None or isinstance(x, (int, float)) else x[0]

    def vc(o, a, *more, w=None):
        if isinstance(o[1], list):
            return 0.05 + o[2] * SCA * CYC
        if isinstance(a[1], list):
            return 0.06 + a[2] * GAT * CYC
        return max(64, a[7] * (w or (0.5 if all(x[8] == 2 for x in (o, a) + more) else 1))) * CYC

    def tt(o, a, b, f):
        w = 1 if "K" in (a[1][0], b[1][0]) else 2
        return op("v", lambda: V.tensor_tensor(o[0], a[0], b[0], f), flat(a, b), flat(o), vc(o, a, w=w))

    def ts(o, a, s1, s2, f, f2=None):
        more = () if f2 is None else (f2,)
        return op("v", lambda: V.tensor_scalar(o[0], a[0], ap(s1), ap(s2), f, *more), flat(a, s1, s2), flat(o), vc(o, a, *flat(s1, s2)))

    def cp(o, a):
        return op("v", lambda: V.tensor_copy(o[0], a[0]), flat(a), flat(o), vc(o, a))

    def ms(o, v):
        op("v", lambda: V.memset(o[0], v), [], [o], vc(o, o))

    def tr(o, a):
        op("v", lambda: V.transpose(o[0], a[0]), [a], [o], vc(o, a))

    def red(o, a):
        op("v", lambda: V.tensor_reduce(o[0], a[0], AX.X, O.add), [a], [o], vc(o, a, w=1))

    def scan(o, d0, d1, init, f0, f1):
        op("v", lambda: V.tensor_tensor_scan(o[0], d0[0], d1[0], init, f0, f1), [d0, d1], [o], vc(o, d0, d1))

    def act(o, a, f=F.Copy, bias=None, scale=None, after=(), once=0.0, total=None):
        kw = {}
        if bias is not None:
            kw["bias"] = ap(bias)
        if scale is not None:
            kw["scale"] = ap(scale)
        if total is not None:
            kw["accum_out"] = total[0]
        return op("s", lambda: S.activation(o[0], a[0], f, **kw), flat(a, bias, scale), flat(o, total), vc(o, a, w=1) + 0.03 + once, after=after)

    def copy(q, o, a):
        return (act if q == "s" else cp)(o, a)

    def mm(o, pairs, start=True, stop=True, outs=None, each=None):
        if len(pairs) > PIECE and not each:
            first = len(calls)
            for k in range(0, len(pairs), PIECE):
                mm(o, pairs[k:k + PIECE], start and k == 0, stop and k + PIECE >= len(pairs), outs and outs[k:k + PIECE])
            for k in range(first, len(calls)):
                group[k] = (first, len(calls) - 1)
            return

        def call():
            i = None
            for k, (l, x) in enumerate(pairs):
                i = P.matmul((outs[k] if outs else o)[0], l[0], x[0], start and k % (each or 999) == 0,
                             stop and (k + 1) % (each or len(pairs)) == 0)
            return i
        op("p", call, [z for l, x in pairs for z in (l, x)], [o], sum(max(64, x[7]) * (x[8] * x[8] // 4) for l, x in pairs) * PE)

    def one(f, i):
        o = 144 * FAMS.index(f) + 15 - i
        return r("FAM", o, o + 128)

    def fam(f, src, c0, c1, o=0):
        return [(one(f, i), r(src, o + 16 * c0 + i, o + 16 * c1, 16)) for i in range(16)]

    def dma(q, o, a, after=()):
        x = o if o[9] else a
        return op(q, lambda: QU[q].dma_start(o[0], a[0]), [a], [o], LOCAL + x[7] * x[8] * x[9] / RATE, "local", after, 0.05)

    def iota(o, pat, base=0, cm=0):
        kw = {} if o[1] == "PI" else {"allow_small_or_imprecise_dtypes": True}
        c = 0.13 + 2 * CYC * o[7]
        op("g", lambda: G.iota(o[0], pat, base, cm, **kw), [], [o], c, hold=c + WAKE)

    def fill(o, v):
        iota(o, [[0, o[7]]], int(v))

    def gsel(o, a, pat, base, cm):
        c = 0.17 + 2 * CYC * o[7]
        op("g", lambda: G.affine_select(o[0], a[0], pat, O.is_ge, 0.0, base, cm), [a], [o], c, hold=c + WAKE)

    def send(call, src, dst, left, landed, n, time):
        s = op("g", call, [src], [], time, (left, n), hold=0.6 + max(0, time - 2 * REMOTE))
        op(None, None, [], [dst], time, (landed, n), after=[s])

    def visit(t, src, name, time):
        dst = T.cores[(rank + 1 + t % 3) % N]
        rid, pid, _ = topo.addr(dst)
        mask = sum(1 << e for e in topo.engines(core, dst)[:8])
        out = r("%s%d" % (name, t), 0, src[7])
        send(lambda: G.remote_dma(out_ap=out[0], in_ap=src[0], remote_sem=T.sem["%sa%d" % (name, t)], local_sem=T.sem["%sl%d" % (name, t)],
                                  pid=pid, routing_id=rid, dma_engine_mask=mask), src, out, "%sl%d" % (name, t), "%sa%d" % (name, t), 8, time)

    last = [dma("y", r("OF"), hbm("of0")), dma("y", r("AN"), hbm("an0"))]
    dma("y", r("SNDI"), hbm("snd"))
    loads = [(n, x, c) for n, x, lo, hi in LOADS for c in range(lo, hi, 512)]
    for n, x, c in loads[:EARLY]:
        last = [dma("y", r(n, c, c + 512), hbm(x, c, c + 512), last)]
    iota(r("PI", 0, 2), [[0, 2]], 0, 1)
    iota(r("M16"), [[0, 8], [1, 16]])
    ms(r("ONE"), 1.0)
    gsel(r("B16"), r("ONE"), [[-16, 8], [0, 16]], 0, 1)
    gsel(r("B16"), r("B16"), [[16, 8], [0, 16]], 15, -1)
    iota(part("R2", 0, 64, 0, 512), [[0, 2], [1, 256]])
    ms(part("R2", 64, 96, 0, 256), 0.0)
    ms(part("R2", 64, 96, 256, 512), 1.0)
    ms(part("R2", 96, 128, 0, 512), 1.0)
    iota(r("N1F"), [[1, 256]], 1)
    n1b = (T.N1B[0:80], "N1B", 0, 256, 1, 0, None, 256, 2, 128)
    iota((T.N1B[:],) + n1b[1:], [[16, 16], [1, 16]], 1)
    iota(r("NL0"), [[16, 16]])
    for c in range(0, 2560, 640):
        fill(r("DR", c, c + 640), 0)
    for k, m in enumerate((15, 31)):
        ts(r("YI", k, k + 1), r("PI", 0, 1), m, None, O.bitwise_and)
    cp(r("CO", 0, 2), r("YI", 0, 2))
    ms(r("ZR"), 0.0)
    for c in range(0, WS, 512):
        act(r("WP", c, c + 512), r("ZR"))
    ms(r("WP", WS, NW), 0.0)
    for c in range(16 * MC0[0][0], 2560, 512):
        act(r("E2", c, min(2560, c + 512)), r("ZR", 0, min(2560, c + 512) - c))
    ms(r("ST", 208, 448, 224), 0.0)
    ms(r("ST", 448 + 160, 448 + 209), float(RT))
    ms(r("ST", 672 + 160, 672 + 209), 0.0)
    for c in range(0, 144 * len(FAMS), 432):
        act(r("FAM", c, c + 432), r("ZR", 0, 432))
    ts(r("M16b"), r("M16"), col(0), None, O.is_equal)
    ts(r("MD"), r("M16", 0, 16), col(0), None, O.is_equal)
    tt(r("ID"), r("M16b"), r("B16"), O.mult)
    for c, rws in ((2, (0, 13, 12)), (3, (4, 8)), (4, (8, 11, 2)), (6, (9, 12, 2)), (7, (8, 12)), (8, (0, 10, 9)), (22, (0, 16, 2 if GQ[2] == "v" else 1))):
        red(col(c), r("MD", *rws))
    ts(col(7), col(7), -1.0, 1.0, O.mult, O.add)
    ts(r("CB", 0, 1), col(6), -1.0, 1.0, O.mult, O.add)
    ts(r("CB", 1, 2), r("MD", 11, 12), float(RT), None, O.mult)
    ts(col(9), col(0), 16.0, None, O.add)
    for f, w in zip(FAMS, (U, U / 2, col(7), col(3), col(4), col(6), col(2), col(0), col(9))):
        o = 144 * FAMS.index(f) + 15
        ts(r("FAM", o, o + 128, 16), r("B16", 0, 128, 16), w, None, O.mult)
    ts(col(5), r("MD", 4, 5), 4096.0, None, O.mult)
    for n, s in (("IM1", -1.0), ("I7", 7.0), ("IM2K", -2048.0), ("I768", 768.0), ("IDF", 1.0), ("I160", 160.0), ("IM25", -2559.0)):
        act(r(n), r("ID"), F.Identity, scale=s)
    ts(col(10), r("MD", 1, 2), 1024.0, col(2), O.mult, O.subtract)
    ts(col(11), r("MD", 1, 2), -1 / 8192, None, O.mult)
    for n, s in (("BO", -BIG), ("BD", col(2)), ("BH", r("MD", 12, 13)), ("BL", col(8)), ("BN", col(10)), ("BR", col(11))):
        act(r(n), r("B16"), F.Identity, scale=s)
    ts(r("LE"), r("M16"), col(0), None, O.is_gt)
    tt(r("LT"), r("LE"), r("B16"), O.mult)
    tt(r("LE"), r("LT"), r("ID"), O.add)
    act(r("LTN"), r("LT"), F.Identity, scale=-BIG)
    act(r("SEL0"), r("ONE"), F.Identity, scale=r("MD", 0, 1))
    ts(col(12), col(1), 15.5, None, O.is_lt)
    ts(col(13), col(1), 15.5, None, O.is_gt)
    for a, s in (("A", 1.0), ("H", -0.5)):
        for k in range(2):
            fill(r("%s%d" % (a, k), 0, 16), 0)
            fill(r("%s%d" % (a, k), 144, 160), 0)
            ts(r("%s%d" % (a, k), 16, 144), r("ID"), col(12 + k), s, O.mult, O.mult)
    fill(r("ON"), 1)
    fill(r("C96"), 96)
    fill(r("C8", 0, NS), 8 * U)
    fill(r("C8", NS, 256), 0)
    ms(col(32), -77.0)
    act(col(15), col(32), F.Exp, once=1.3)
    ts(col(16), col(15), -1.0, None, O.mult)
    ms(part("CR", 0, 64, 0, 1024), 1.0 / 64)
    ms(part("CR", 64, 96, 0, 1024), 8.0)
    for b in range(8):
        ms(part("CR", 96, 128, 128 * b, 128 * b + 128), 16.0 * b)
    ms(col(40), -4095.5)
    ms(col(41), -2048.0)
    ts(col(21), col(0), -16384.0, 15 * 16384.0, O.mult, O.add)
    ts(col(20), col(22), 8 * U, col(21), O.mult, O.add)
    for c in (0, 128):
        act(r("MASK", c, c + 128), r("M16"), F.Sign)
        ts(r("DG", c, c + 128), r("M16b"), BIG + TOP, -BIG, O.mult, O.add)
    ts(r("NL0"), r("NL0"), col(0), None, O.add)
    ts(r("NL1"), r("NL0"), 1.0, None, O.add)
    ts(r("NLB"), r("NL0"), -1.0, -0.5, O.mult, O.add)
    fill(r("DMP"), 4 * BIG)
    ts(r("DMP", 0, 256, 16), r("NL0"), -1.0, TOP - 4096.0, O.mult, O.add)
    fill(r("TH", 0, 1), 9 * U)
    for x in [r("RS", 0, 1), r("RKM", 160, 176), r("X", 2560, 2576), r("Q"), r("Qg"), r("S", 4096, 4368)] + \
            [r("GX%d" % t, 256, 272) for t in range(RO)]:
        fill(x, 0)
    ms(r("NG"), 0)
    fill(r("CA", 2560, 2576), 32 * U + FAR)
    fill(r("CAG", 256, 272), -32 * U)
    for c, v in ((4, 4096), (10, RT), (9, 96)):
        fill(r("Q", c, 256, 16), v)
    ts(r("ST", 0, 208), r("OF"), M6, M6, O.add, O.subtract)
    tt(r("ST", 224, 432), r("OF"), r("ST", 0, 208), O.subtract)
    ts(r("ST", 448, 608), r("AN"), M6, M6, O.add, O.subtract)
    tt(r("ST", 672, 832), r("AN"), r("ST", 448, 608), O.subtract)
    for row, seg in ((12, 0), (0, 1), (11, 2), (10, 2), (9, 3), (8, 3)):
        last = [dma("y", rp("WP", row, 16, 0, NW, row), r("ST", 224 * seg, 224 * seg + 209), last)]
    for n, x, c in loads[EARLY:]:
        last = [dma("y", r(n, c, c + 512), hbm(x, c, c + 512), last)]
    ts(r("LOI"), r("AN"), 15, None, O.bitwise_and)
    ts(r("SHI"), r("AN"), 4, None, O.arith_shift_right)
    ts(r("W1"), r("LOI"), 209, None, O.mult)
    tt(r("PLI"), r("W1"), r("SHI"), O.add)
    cp(r("PL"), r("PLI"))
    ts(r("SA"), r("SNDI"), 15, None, O.bitwise_and)
    ts(r("SB"), r("SNDI"), 4, None, O.arith_shift_right)
    ts(r("SA"), r("SA"), 160, None, O.mult)
    tt(r("SA"), r("SA"), r("SB"), O.add)
    cp(r("SL", 0, 48), r("SA"))

    def ctab(b):
        K, sg = ("K4", "K5")[b % 2], "SG%d" % (b % 2)
        tv, out = [(r("I7"), r("WK", 512 * b, 512 * b + 512)), (r("CR", 128 * b, 128 * b + 128), r("R2"))], r("CT", 512 * b, 512 * b + 512)
        mm(r(K), tv)
        if b < 4:
            copy(CTQ[b], out, r(K))
        elif CTQ[b] == "v":
            ts(r(sg), r(K), 4095.5, -4096.0, O.is_gt, O.mult)
            tt(out, r(K), r(sg), O.add)
        else:
            act(r(sg), r(K), F.Sign, bias=col(40))
            mm(r(K), tv + [(r("IM2K"), r(sg))])
            act(out, r(K), F.Identity, bias=col(41))

    BK = ("K0", "K7", "K6")

    def rows(dst, a, src, b, step, c0, c1):
        dma("y", rp(dst, a, step, 16 * c0, 16 * c1, a), rp(src, b, step, 16 * c0, 16 * c1))

    def level(t, win, lst, out, who, nxt=None, own=None, step=0, new=None, moved=()):
        for c0, c1 in moved:
            if t and step == 2 and c1 <= NA:
                rows(nxt, 0, "E", 0, 4, c0, c1)
                rows(nxt, 2, "G1", 0, 4, c0, c1)
            else:
                rows(nxt, 0, own, 0, step, c0, c1)
        for q, c0, c1, p in who:
            a = ind(r(win, 0, NW), r(lst, c0, c1))
            if p == "a":
                tt(r(nxt, 16 * c0, 16 * c1), a, r(nxt if moved else own, 16 * c0, 16 * c1), O.add)
            else:
                copy(q, r(out, 16 * c0, 16 * c1), a)
            if isinstance(p, int):
                rows(nxt, step // 2, out, 0, step, p, c1)
        for k, (q, c0, c1, p) in enumerate(who):
            if p in ("s", "v"):
                K = r((MB if t else ("K1", "K2"))[k % 2], 0, 16 * (c1 - c0))
                mm(K, [(r("ID"), r(own, 16 * c0, 16 * c1))], stop=False)
                mm(K, [(r("ID"), r(out, 16 * c0, 16 * c1))], start=False)
                copy(p, r(nxt, 16 * c0, 16 * c1), K)
        for B, (c0, c1) in zip(BK, ((CH if step == 4 else CH4) if t else CH0) if new else ()):
            K, added = r(B, 0, c1 - c0), [p for q, a, b, p in who if a <= c0 < b] == ["a"]
            hi, lo = r(new + "H", c0, c1), r(new + "W", c0, c1)
            if t:
                mm(K, [(r("ID"), hi), (r("ID"), lo)], stop=False)
                mm(K, fam("FF", nxt if added else out, c0, c1), start=False)
                ts(r(new + "L", c0, c1), K, float(RT), None, O.min)
            else:
                mm(K, fam("FQ", nxt if added else out, c0, c1))
                cp(r(new + "L", c0, c1), K)
                cp(hi, K)
                tt(lo, K, hi, O.subtract)

    def tl(a, src, m2):
        return [(r("%s%d" % (a, m2), 16 * (1 + m2 - h), 16 * (1 + m2 - h) + 128), r(src[1], src[2] + 16 * h, src[3], 32)) for h in range(2)]

    def both(K, o, k, parts):
        return [p for m2 in range(2) for a, x in parts for p in tl(a, x, m2)], [r(K, o + m2, o + k, 2) for m2 in range(2) for p in range(2 * len(parts))]

    def choose(K, n, tn, un, q, ev, th):
        k = n // 16
        for B, n0, n1 in [x[:3] for x in K]:
            tr(r(tn, n0, n1), r(B, 128 + n0, 128 + n1))
            scan(r(un, n0, n1), r("MASK", 0, n1 - n0), r(tn, n0, n1), 0.0, O.mult, O.max)
        M = r(un, 15, n, 16)
        ts(r("T6", 0, k), M, M6, M6, O.add, O.subtract)
        ts(r("T14", 0, k), M, M14, M14, O.add, O.subtract)
        ts(r(q, 1, n, 16), M, th, -8192.0, O.is_lt, O.mult)
        tt(r(q, 0, n, 16), M, r("T6", 0, k), O.subtract)
        tt(r(q, 12, n, 16), r("T6", 0, k), r("T14", 0, k), O.subtract)
        tr(r(ev), r(q))

    def settle(n, q, ev, eq, xs):
        k = n // 16
        lo, rf, hi = r(q, 0, n), r(q, 1, n), r(q, 12, n)
        if n == 256:
            mm(r("K1", n, n + k), [(r("ID"), r("C96"))], stop=False)
            for K, parts, b in (("K2", [("A", hi)], "BH"), ("K1", [("A", lo), ("A", rf)], "BL")):
                pairs, outs = both(K, n, k, parts)
                mm(r(K), pairs, K == "K2", outs=outs, each=2 if K == "K2" else 8)
                mm(r(K, 0, n), [(r(b), r(ev))])
            act(r("PW"), r("K2", 0, n + k), F.Exp, scale=LN2 / 64)
            tt(r("CRB"), r("K1", 0, n + k), r("PW"), O.mult)
            cr, own = "CRB", lambda m: r("CRB", n + m, n + m + 1)
        else:
            pairs, outs = both("K3", 0, k, [("A", lo), ("A", rf), ("A", hi)])
            mm(r("K3"), pairs, outs=outs, each=6)
            mm(r("K3", 256, 256 + n), [(r("BD"), r(ev))])
            cp(r("CRUg", 0, n), r("K3", 256, 256 + n))
            cr, own = "CRUg", lambda m: r("K3", m, m + 1)
        mm(r("K4", 0, n), [(r("ID"), r("DG", 0, n)), (r("BN"), r(ev))], stop=False)
        for m in range(k):
            w = n - 16 * m
            ts(blk(eq, m, m + 1, 0, w), r(cr, 16 * m, n), own(m), None, O.is_equal)
            if w > 16:
                mm(r("K4", 16 * m + 16, n), [(r("BO"), blk(eq, m, m + 1, 16, w))], start=False, stop=False)
            if m % 8 == 7 or m == k - 1:
                a = m - m % 8
                mm(r("K4", 16 * a, 16 * m + 16), [(r("LTN"), blk(eq, a, m + 1, 0, 16))], start=False, stop=m == k - 1)
        scan(r("UX", 0, n), r("DMP", 0, n), r("K4", 0, n), 4 * BIG, O.min, O.max)
        ts(r("POSS", 0, k), r("UX", 15, n, 16), -1.0, float(TOP), O.mult, O.add)
        cp(ind(r("S"), r("POSS", 0, k)), xs)

    def diff(B, w, x, s, how):
        xs, outs = [(r("ID"), x)] * 8, [r(B, k, w, 8) for k in range(8)]
        if how == 0:
            mm(r(B, 0, w), [(r("IM1"), s)], stop=False)
            mm(r(B), xs, start=False, outs=outs)
        else:
            if how == 1:
                mm(r(B, 0, w), [(r("ID"), r("ZR", 0, w))], stop=False)
            mm(r(B), xs, start=how == 2, stop=False, outs=outs)
            mm(r(B, 0, w), [(r("IM1"), s)], start=False)

    def guests(t):
        gr, gx = r("GR%d" % t, 0, 4), "GX%d" % t
        act(r("CAG", 0, 256), ind(r("CT"), r("GN%d" % t)))
        cp(r("CgL"), ind(r("CAG"), gr))
        act(r("XG"), ind(r(gx), gr))
        act(r("CSg"), ind(r("CAG"), gr), F.Identity, bias=col(20))
        mm(r("K3", 128, 192), [(r("IDF"), r("CSg"))], stop=False)
        for h in range(2):
            copy(GQ[h], r("GTg", 512 * h, 512 * h + 512), ind(r("S"), r("CgL", 32 * h, 32 * h + 32)))
        for h, B in enumerate(("K1", "K2")):
            c = (512 * h, 512 * h + 512)
            diff(B, 512, r("XG"), r("GTg", h, 1024, 2), ZG)
            if h and GQ[2] == "v":
                ts(r("CMg", *c), r(B), 0.0, 2.0, O.is_gt, O.mult)
            else:
                act(r("CMg", *c), r(B), F.Sign, bias=col(16))
        for h in (1, 0):
            mm(r("K3", 128, 192), [(one("HC", 2 * k + h), r("CMg", 512 * h + k, 512 * h + 512, 8)) for k in range(8)], start=False, stop=h == 0)
        choose([("K3", 0, 64)], 64, "TRg", "UUg", "Qg", "EVg", r("TH", t, t + 1))
        settle(64, "Qg", "EVg", "EQg", r("XG"))

    for t in range(RO):
        more = t < RO - 1
        if t == 0:
            for i in range(16):
                ts(r("E", i, RT, 16), r("WP", 209 * i, 209 * i + 208), r("CB", 0, 1), None, O.mult)
            ts(r("E", RT, NW), r("ZR", 0, NW - RT), col(5), None, O.add)
            ts(r("E1", G0, NW), r("E", G0, NW), r("CB", 1, 2), None, O.add)
            cp(r("E2", G0, NW), r("E", G0, NW))
        who = LV if t else LV0
        level(t, "E" if t else "WP", "P1L" if t else "PL", "G1", who[0], "E1", "E", 4, "P2", MA if t else ())
        level(t, "E1", "P2L", "G2", who[1], "E2", "E1", 2, "P4", MC if t else MC0)
        for B, c in zip(BK, CD):
            mm(r(B, 128, 128 + c[1] - c[0]), fam("FS", "E2", *c), stop=False)
        level(t, "E2", "P4L", "G3", who[2])
        for B, c in zip(BK, CD):
            K = r(B, 128, 128 + c[1] - c[0])
            mm(K, fam("FS", "G3", *c), start=False)
            cp(r("DI", *c), K)
            ts(r("DM", *c), r("DI", *c), 4095, None, O.bitwise_and)
            cp(r("DL", *c), r("DM", *c))
        ts(r("DH"), r("DM"), M6, M6, O.add, O.subtract)
        tt(r("DLO"), r("DM"), r("DH"), O.subtract)
        if t == 0:
            for b in (4, 5, 6, 7, 0, 1, 2, 3):
                ctab(b)
        dma("y", rp("DR", 12, 16, 0, 2560, 12), r("DH"))
        dma("y", rp("DR", 0, 16, 0, 2560, 0), r("DLO"))
        if more:
            act(r("GD"), ind(r("DR"), r("SL", 0, 48)))
            la, tls = "LA%d" % t, []
            for d in range(1, N):
                dst = T.cores[(rank + d) % N]
                rid, pid, _ = topo.addr(dst)
                e = topo.engines(core, dst)
                tls.append(RemoteDMATransfer(src=T.GD[:, 256 * d - 256:256 * d], dst=T[la][:, 256 * d - 256:256 * d], dst_ids=[DstId(rid=rid, pnc=pid)],
                                             dma_engine_mask=(1 << e[d - 1]) | (1 << e[d + 3]), remote_sem=T.sem["ga%d" % t]))
            send(lambda tls=tls, t=t: G.remote_dma_fused(tls, local_sem=T.sem["gl%d" % t]), r("GD"), r(la), "gl%d" % t, "ga%d" % t, 6,
                 2 * REMOTE + (0 if t else FIRST))
            for n in ("E", "E1", "E2"):
                dma("y", rp(n, 0, 4, G0, RT), rp(la, 0, 4, 0, 768))
        W = r("S")
        for j, (K, (c0, c1)) in enumerate(zip(("K1", "K2", "K5"), CS_)):
            gt, K = r("GT", 512 * j, 512 * j + 16 * (c1 - c0)), r(K, 0, 16 * (c1 - c0))
            act(gt, ind(W, r("DL", c0, c1)))
            mm(K, [(r("ID"), r("X", 16 * c0, 16 * c1))], stop=False)
            mm(K, [(r("IM1"), gt)], start=False)
            act(r("CM", 16 * c0, 16 * c1), K, F.Sign, bias=col(15))
        for c0, c1 in CV:
            tt(r("CM", 16 * c0, 16 * c1), ind(W, r("DL", c0, c1)), r("X", 16 * c0, 16 * c1), O.is_le)
        for B, c in zip(BK, CC):
            K = r(B, 256, 256 + c[1] - c[0])
            mm(K, fam("CNT" if c[0] else "HC", "CM", *c))
            ts(r("BT", *c), K, (4.5 if c[0] else -3.5) * U, None, O.is_lt)
        for c in range(0, 160, 32):
            copy("s" if t else CAQ[c // 32], r("CA", 16 * c, 16 * c + 512), ind(r("CT"), r("DL", c, c + 32)))
        scan(r("RS", 1, 161), r("ON", 0, 160), r("BT"), 0.0, O.mult, O.add)
        ends = r("K3", 0, 8)[1:]
        mm((T.K3[0:80, 0:8],) + ends, [(r("RS", 2, 161, 2), r("B16", 0, 128, 16))])
        mm(r("K4", 0, 160), [(r("B16"), r("RS", 0, 160)), (r("LE"), r("BT"))])
        mm(r("K0", 400, 401), [(r("B16"), r("RS", 160, 161))])
        ts((T.EN[0:80, :],) + r("EN")[1:], (T.K3[0:80, 0:8],) + ends, 256.0, None, O.min)
        for k in range(8):
            ts((T.C1[0:80, :, 16 * k:16 * k + 16], "C1", 0, 2048, 1, 0, k, 256, 2, 128), n1b, (T.EN[0:80, k:k + 1],) + r("EN")[1:], None, O.is_gt)
        tt(r("RKM", 0, 160), r("K4", 0, 160), r("BT"), O.mult)
        TOT = r("K0", 400, 401)
        ts(r("INV"), r("NL0"), TOT, None, O.is_ge)
        ts(r("JJ"), r("NL1"), TOT, 0.0, O.subtract, O.max)
        if more:
            ts(r("MT", 0, 1), TOT, 256.0, None, O.min)
        mm(r("K5", 32, 48), [((T.C1[0:80, m, :], "C1", 0, 2048, 1, 0, None, 128, 2, 128), (T.ONE[0:80, 0:1],) + r("ONE", 0, 1)[1:]) for m in range(16)],
           outs=[r("K5", 32 + m, 33 + m) for m in range(16)], each=1)
        for h in range(2):
            ts(r("CL", 16 * h, 16 * h + 16), r("K5", 32, 48), 2.0, float(h), O.mult, O.add)
        ts(r("C32v"), r("K5", 32, 48), 32.0, None, O.mult)
        for h in range(2):
            tt(r("EQS", 256 * h, 256 * h + 256), ind(r("RKM"), r("CL", 16 * h, 16 * h + 16)), r("N1F"), O.is_equal)
            mm(r("K3", 48, 64), ([] if h else [(r("ID"), r("C32v"))]) + fam(("FV", "FW")[h], "EQS", 16 * h, 16 * h + 16), h == 0, h == 1)
        cp(r("VL"), r("K3", 48, 64))
        act(r("VF"), r("K3", 48, 64))
        cp(r("XS"), ind(r("X"), r("VL")))
        for a, b in CANP:
            ts(r("CAN", a, b), ind(r("CA"), r("VL", a // 16, b // 16)), float(FAR), None, O.min)
        mm(r("K0", 0, 16), [(r("IDF"), r("VF")), (r("I768"), r("INV")), (r("ID"), r("JJ"))], stop=False)
        visit(t, r("XS"), "GX", 2 * REMOTE)
        for k in range(16):
            cp(r("XE", k, 16 * (256 - NS), 16), r("XS", NS, 256))
        keys = [act(r("CS"), ind(r("CA"), r("VL")), F.Identity, bias=col(21))]
        for Bs, n0, n1 in SS:
            w = 8 * (n1 - n0)
            act(r("GC", 16 * n0, 16 * n1), ind(W, r("CAN", n0, n1)), after=keys)
            for h, B in enumerate(Bs):
                diff(B, w, r("XS", n0, n1), r("GC", 16 * n0 + h, 16 * n1, 2), ZS)
                act(r("CM", 16 * n0 + w * h, 16 * n0 + w * h + w), r(B, 0, w), F.Sign, bias=col(16))
        for n0, n1 in SV:
            tt(r("CM", 16 * n0, 16 * n1), ind(W, r("CAN", n0, n1)), r("XE", 16 * (n0 - NS), 16 * (n1 - NS)), O.is_lt)
        for B, n0, n1, parts in CN:
            K = r(B, 128 + n0, 128 + n1)
            mm(K, [(r("IDF"), r("CS", n0, n1))] + [(r("ID"), r("C8", n0, n1))] * (n0 < NS), stop=False)
            for a, b in parts:
                w, end = 8 * (b - a), (a, b) == parts[-1]
                if a >= NS:
                    mm(r(B, 128 + a, 128 + b), fam("CNT", "CM", a, b), start=False, stop=end)
                for h in range(2 * (a < NS)):
                    o = 16 * a + w * h
                    mm(r(B, 128 + a, 128 + b), [(one("HC", 2 * k + h), r("CM", o + k, o + w, 8)) for k in range(8)], start=False, stop=end and h == 1)
        ts(r("VC1"), r("VF"), 1 / 16, -7.5 / 16, O.mult, O.add)
        ts(r("VC2"), r("VC1"), M0, M0, O.add, O.subtract)
        mm(r(VB, 0, 16), [(r("I160"), r("VF")), (r("IM25"), r("VC2"))])
        cp(r("VP"), r(VB, 0, 16))
        copy(DQ, r("DS"), ind(r("DR"), r("VP")))
        mm(r(VB, 16, 32), fam("FS", "DS", 0, 16))
        cp(r("DNL"), r(VB, 16, 32))
        visit(t, r("DNL"), "GN", REMOTE)
        choose(CN, 256, "TR", "UU", "Q", "EV", r("TH", t, t + 1))
        pairs, outs = both("K0", 0, 16, [("H", r("Q", 1, 256))])
        mm(r("K0"), pairs, start=False, outs=outs)
        cp(r("POSE"), r("K0", 0, 16))
        cp(ind(r("E"), r("POSE")), r("EV"))
        for B, c in zip(BK, CP if more else ()):
            mm(r(B, 0, c[1] - c[0]), fam("FP", "E", *c))
            cp(r("P1L", *c), r(B, 0, c[1] - c[0]))
        mm(r("K3", 0, 256), [(r("BR"), r("EV"))])
        scan(r("CUM"), r("ON"), r("K3", 0, 256), 0.0, O.mult, O.add)
        for m in range(4):
            act(r("JK", 256 * m, 256 * m + 256), r("CUM"), F.Sign, bias=r("NLB", m, m + 1), total=r("AC", m, m + 1))
        ts(r("NG", 0, 4), r("AC", 0, 4), -0.5, 128.0, O.mult, O.add)
        visit(t, r("NG"), "GR", REMOTE)
        settle(256, "Q", "EV", "EQ", r("XS"))
        if more:
            mm(r("K3", 400, 401), [(r("SEL0"), r("CUM", 255, 256)), (r("SEL0"), r("MT", 0, 1))])
            cp(r("HI", 0, 1), r("K3", 400, 401))
            ts(r("HI", 1, 2), r("HI", 0, 1), 1, None, O.bitwise_and)
            ts(r("TH", t + 1, t + 2), r("HI", 1, 2), U, 9 * U, O.mult, O.add)
        else:
            for c in range(8):
                mm(r("K7", 0, 320), [(one(f, 2 * c + k), r("E", 320 * c, 320 * c + 320)) for k, f in enumerate(("FD", "FP"))], c == 0, c == 7)
            act(r("OUT"), r("K7", 0, 320))
            dma("y", hbm("yof"), rp("OUT", 0, 2, 0, 320))
            dma("y", hbm("yan"), rp("OUT", 1, 2, 0, 320))
        guests(t)
    dma("y", hbm("ys"), r("S", 0, 4096))

    every = range(len(calls))
    lead = [LOCAL if c["sem"] == "local" else 0.0 for c in calls]
    res = ["dma" if c["sem"] == "local" else c["q"] for c in calls]
    hold = [c["cost"] - LOCAL if c["sem"] == "local" else c["hold"] for c in calls]
    fwd, bwd = [[] for c in calls], [[] for c in calls]
    for i, c in enumerate(calls):
        for d, w in c["deps"].items():
            lag = (calls[d]["cost"] + WAKE if w else 1e-5 if res[d] != res[i] else hold[d]) - lead[d] + lead[i]
            fwd[i].append((d, lag))
            bwd[d].append((i, lag + hold[i] - hold[d]))

    def place(key, before, first):
        ahead = before is fwd
        key = [key[group[i][0 if ahead else 1]] if i in group else key[i] for i in every]
        for i in (reversed(every) if ahead else every):
            x = key[i] + 1e-7
            for d, lag in before[i]:
                if key[d] < x:
                    key[d] = x
        taken, at = {q: ([], []) for q in res}, [0.0] * len(calls)
        for i in sorted(every, key=lambda i: -key[i]):
            x = first[i]
            for d, lag in before[i]:
                if at[d] + lag > x:
                    x = at[d] + lag
            if res[i]:
                A, B = taken[res[i]]
                k, h = len(B), hold[i]
                while k and B[k - 1] > x:
                    k -= 1
                while k < len(B) and x + h > A[k]:
                    x = B[k] if B[k] > x else x
                    k += 1
                A.insert(k, x)
                B.insert(k, x + h)
            at[i] = x
        return at

    def sweep(at):
        back = place([at[i] + hold[i] for i in every], bwd, [0.0] * len(calls))
        return place([back[i] + hold[i] for i in every], fwd, lead)

    def span(at):
        return max(at[i] - lead[i] + calls[i]["cost"] for i in every)

    def score(at):
        return span(at) + MEAN * sum(at) / len(at)

    twin = {}

    def ahead(key, at, p, i):
        for j in twin[calls[i]["name"]]:
            near = min(twin[calls[p]["name"]], key=lambda k: abs(at[j] - at[k] - at[i] + at[p]))
            if abs(at[j] - at[near] - at[i] + at[p]) < 3 and key[j] < key[near]:
                key[group.get(j, (j,))[0]] = key[group.get(near, (near,))[0]] + 1e-5

    if not ORDER:
        way = [0.0] * len(calls)
        for i in reversed(every):
            way[i] = max([way[j] + lag - hold[j] + hold[i] for j, lag in bwd[i]] + [hold[i]])
        at = kept = sweep(place(way, fwd, lead))
        tried, left, best = set(), PASSES, score(at)
        for i, c in enumerate(calls):
            twin.setdefault(c["name"], []).append(i)
        while left > 0:
            turn, tail, nxt, prev = sorted(every, key=lambda i: at[i]), [0.0] * len(calls), {}, {}
            for i in reversed(turn):
                n = nxt.get(res[i]) if res[i] else None
                tail[i] = max([calls[i]["cost"] - lead[i]] + [tail[j] + lag - hold[j] + hold[i] for j, lag in bwd[i]]
                              + ([hold[i] + tail[n]] if n is not None else []))
                if n is not None:
                    prev[n] = i
                nxt[res[i]] = i
            end, swaps = span(at), []
            for i in turn:
                ready = max([at[d] + lag for d, lag in fwd[i]] + [lead[i]])
                if res[i] and at[i] - ready > 0.03 and end - at[i] - tail[i] < NEAR:
                    p = prev[i]
                    swaps.append((end - at[i] - tail[i] - min(hold[p], at[i] - ready), p, i))
                    while p in prev and at[p] > ready:
                        p = prev[p]
                    swaps.append((end - at[i] - tail[i] - (at[i] - ready), p, i))
            new = [x for x in sorted(swaps) if (calls[x[1]]["name"], calls[x[2]]["name"]) not in tried]
            if not new:
                key, tried, left = [-v for v in at], set(), left - 1
                for k in range(KICK if swaps else 0):
                    x, p, i = swaps[(7919 * left + 104729 * k) % len(swaps)]
                    ahead(key, at, p, i)
                at = sweep(place(key, fwd, lead))
                best = score(at)
            for x, p, i in new[:6]:
                pair = (calls[p]["name"], calls[i]["name"])
                if pair in tried:
                    continue
                tried.add(pair)
                left -= 1
                key = [-v for v in at]
                ahead(key, at, p, i)
                a2 = place(key, fwd, lead)
                s2 = score(a2)
                if best - 1e-4 < s2 < best + SLACK:
                    a2 = sweep(a2)
                    s2 = score(a2)
                if s2 < best - 1e-4:
                    if s2 < best - 0.05:
                        tried = set()
                    at, best = a2, s2
                    break
            if best < score(kept):
                kept = at
            elif best > score(kept) + 1.0:
                at, best = kept, score(kept)
        ORDER.append(sorted(every, key=lambda i: kept[i] - lead[i]))
        ORDER.append(span(kept))

    cnt, known, nd = {"cv": 0, "cs": 0, "cp": 0, "cg": 0}, {q: {} for q in QU}, 0
    for i in ORDER[0]:
        c = calls[i]
        q = c["q"]
        if q is None:
            c["ev"] = c["sem"] + ({},)
            cnt[c["sem"][0]] = c["sem"][1]
            continue
        evs = [calls[d]["ev"] for d, w in c["deps"].items() if w]
        if q == "g" and c["sem"] is None and cnt["cg"]:
            evs.append(("cg", cnt["cg"], {}))
        for e in sorted(evs, key=lambda e: (-sum(e[2].values()), -e[1])):
            if known[q].get(e[0], 0) < e[1]:
                QU[q].wait_ge(T.sem[e[0]], e[1])
                for k, v in list(e[2].items()) + [(e[0], e[1])]:
                    known[q][k] = max(v, known[q].get(k, 0))
        inst = c["call"]()
        if c["sem"] is None:
            s, n = "c" + q, cnt["c" + q] + 1
            inst.then_inc(T.sem[s], 1)
        elif c["sem"] == "local":
            s, n = "d%d" % nd, 16
            nd += 1
            inst.then_inc(T.sem[s], 16)
        else:
            s, n = c["sem"]
        cnt[s] = n
        c["ev"] = (s, n, dict(known[q]))
    for s in cnt:
        if max(known[q].get(s, 0) for q in QU) < cnt[s]:
            G.wait_ge(T.sem[s], cnt[s])
